import numpy as np
import ml_dtypes


def mxq(x, axis, fmt="e4m3"):
    dtype, down = {"e4m3": (ml_dtypes.float8_e4m3fn, 7), "e5m2": (ml_dtypes.float8_e5m2, 14)}[fmt]
    v = np.moveaxis(np.asarray(x, np.float32).astype(ml_dtypes.bfloat16).astype(np.float64), axis, -1)
    blocks = v.reshape(v.shape[:-1] + (-1, 32))
    amax = np.abs(blocks).max(-1, keepdims=True)
    byte = np.maximum(np.where(amax > 0, np.frexp(amax)[1] - 1 + 127, 0) - down, 1)
    scale = np.exp2(byte - 127.0)
    codes = (blocks / scale).astype(np.float32).astype(dtype).astype(np.float64)
    return np.moveaxis((codes * scale).reshape(v.shape), -1, axis)


WIDE = False


def mx_kscale(k):
    if not WIDE:
        return np.ones(k)
    levels = np.array([10, -10, 5, -5, 0])
    if k % 512:
        return np.exp2(np.random.permutation(np.resize(levels, k // 32))).repeat(32)
    a = np.empty((k // 512, 16))
    for p in range(k // 512):
        a[p, :8] = np.random.permutation(np.resize(levels, 8))
        for g in range(8):
            far = levels[np.abs(levels - a[p, g]) >= 10]
            a[p, g + 8] = far[np.random.randint(len(far))]
    return np.exp2(a.ravel()).repeat(32)


def f64(x):
    return np.asarray(x).astype(np.float64)


def striped(idx):
    return np.tile(idx.reshape(-1, 16).T, (8, 1)).astype(np.uint16)


def unstriped(offs):
    return offs[:16].T.reshape(-1).astype(np.int64)


E2M1 = np.array([0.0, 0.5, 1.0, 1.5, 2.0, 3.0, 4.0, 6.0, -0.0, -0.5, -1.0, -1.5, -2.0, -3.0, -4.0, -6.0])


def pack_weight(w, fmt):
    k, n = w.shape
    w = f64(np.asarray(w, np.float32).astype(ml_dtypes.bfloat16)).reshape(k // 32, 32, n)
    amax = np.abs(w).max(1)
    if fmt == "e4m3":
        byte = np.frexp(amax)[1] - 1 + 127 - 7
    else:
        mant, ex = np.frexp(amax / 6.0)
        byte = np.where(mant > 0.5, ex, ex - 1) + 127
    byte = np.clip(np.where(amax > 0, byte, 1), 1, 254)
    scaled = (w * np.exp2(127.0 - byte)[:, None, :]).reshape(k, n).astype(np.float32)
    by_word = np.ascontiguousarray(scaled.reshape(k // 512, 128, 4, n).transpose(0, 1, 3, 2))
    if fmt == "e4m3":
        words = by_word.astype(ml_dtypes.float8_e4m3fn).view(np.uint8)
    else:
        c = by_word.astype(ml_dtypes.float4_e2m1fn).view(np.uint8) & 0xF
        words = (c[..., 0::2] | (c[..., 1::2] << 4)).reshape(k // 512, 128, 2 * n)
    return np.ascontiguousarray(words), np.ascontiguousarray(byte.astype(np.uint8).reshape(k // 512, 16, n))


def unpack_weight(words, scales, fmt):
    g, _, n = scales.shape
    words = np.ascontiguousarray(words).reshape(g, 128, n, -1)
    if fmt == "e4m3":
        vals = words.view(ml_dtypes.float8_e4m3fn).astype(np.float64)
    else:
        nib = np.empty((g, 128, n, 4), np.uint8)
        nib[..., 0::2] = words & 0xF
        nib[..., 1::2] = words >> 4
        vals = E2M1[nib]
    vals = vals * np.repeat(np.exp2(scales.astype(np.float64) - 127.0), 8, axis=1)[..., None]
    return vals.transpose(0, 1, 3, 2).reshape(g * 512, n)


def gelu(v):
    return 0.5 * v * (1.0 + np.tanh(np.sqrt(2.0 / np.pi) * (v + 0.044715 * v**3)))


K, T, S, R, N = 1024, 2048, 1024, 512, 256

def setup_inputs():
    n = np.random.standard_normal
    s = mx_kscale(K)[:, None]
    u = mx_kscale(R)[:, None]
    tab_words, tab_scales = pack_weight(n((K, T)) * s, "e4m3")
    wb_words, wb_scales = pack_weight(n((K, R)) / np.sqrt(K) / s, "e2m1")
    wl_words, wl_scales = pack_weight(0.7 * n((K, N)) / np.sqrt(K) / s, "e4m3")
    return {
        "tab_words": tab_words, "tab_scales": tab_scales,
        "offs": striped(np.random.permutation(T)[:S]),
        "wa": (n((K, R)) / np.sqrt(K) / s * u.T).astype(np.float32),
        "ba": (0.5 * n(R) * u[:, 0]).astype(np.float32),
        "wb_words": wb_words, "wb_scales": wb_scales,
        "bb": (0.5 * n(R)).astype(np.float32),
        "wl_words": wl_words, "wl_scales": wl_scales,
        "wo": (n((R, N)) / np.sqrt(R) / u).astype(np.float32),
        "bo": (0.5 * n(N)).astype(np.float32),
    }

def reference(tab_words, tab_scales, offs, wa, ba, wb_words, wb_scales, bb, wl_words, wl_scales, wo, bo):
    v = unpack_weight(tab_words, tab_scales, "e4m3")[:, unstriped(offs)]
    wbq = unpack_weight(wb_words, wb_scales, "e2m1")
    wlq = unpack_weight(wl_words, wl_scales, "e4m3")
    waq = mxq(f64(wa), 0, "e4m3")
    a = (waq.T @ v) + f64(ba)[:, None]
    b = (wbq.T @ v) + f64(bb)[:, None]
    h = mxq(a * b, 0, "e4m3")
    woq = mxq(f64(wo), 0, "e4m3")
    y = woq.T @ h + wlq.T @ v
    return y + f64(bo)[:, None]

@@ -1,0 +1,264 @@
+from contextlib import ExitStack
+
+import concourse.mybir as mybir
+from concourse.masks import make_identity
+
+K, T, S, R, N = 1024, 2048, 1024, 512, 256
+FLOPS = 2 * S * (2 * K * R + R * N + K * N)
+
+F32 = mybir.dt.float32
+BF16 = mybir.dt.bfloat16
+I32 = mybir.dt.int32
+U32 = mybir.dt.uint32
+U16 = mybir.dt.uint16
+U8 = mybir.dt.uint8
+FP8X4 = mybir.dt.float8_e4m3fn_x4
+FP4X4 = mybir.dt.float4_e2m1fn_x4
+IDENTITY = mybir.ActivationFunctionType.Identity
+MULT = mybir.AluOpType.mult
+ADD = mybir.AluOpType.add
+
+P = 128
+PASSES = K // 512
+HALF = 512
+CHUNKS = [(0, 128), (128, 256), (256, 512), (512, 768), (768, 896), (896, 1024)]
+GROUPS = [(0, 1, 2), (3, 4), (5,)]
+
+
+def tile_list_ad_feature_cross_kernel(
+    tc, tab_words, tab_scales, offs, wa, ba, wb_words, wb_scales, bb, wl_words, wl_scales, wo, bo, out
+):
+    nc = tc.nc
+    with ExitStack() as ctx:
+        keep = ctx.enter_context(tc.tile_pool(name="keep", bufs=1))
+        psum = ctx.enter_context(tc.psum_pool(name="psum", bufs=1))
+
+        def sb(name, shape, dtype, tag=None):
+            return keep.tile(shape, dtype, name=name, tag=tag or name, align_bytes=64)
+
+        def bank(index, name):
+            return psum.tile([P, HALF], F32, name=name, tag="bank%d" % index)
+
+        offsets = keep.tile([P, S // 16], U16, name="offsets")
+        tab_s = sb("tab_s", [P, T], U8)
+        tab_w = [sb("tab_w%d" % a, [P, T], U32) for a in range(PASSES)]
+        wb_raw = sb("wb_raw", [P, PASSES, 2 * R], U8)
+        wb_s_raw = sb("wb_s_raw", [P, PASSES, R], U8)
+        wb_w = sb("wb_w", [P, PASSES, 2 * R], U8)
+        wb_s = sb("wb_s", [P, PASSES, R], U8)
+        wa_raw = [sb("wa_raw0", [P, 4, R], F32)]
+        wa_bf = [sb("wa_bf%d" % a, [P, 4, 4 * P], BF16) for a in range(PASSES)]
+        wa_w = [sb("wa_w%d" % a, [P, R], U32) for a in range(PASSES)]
+        wa_s = [sb("wa_s%d" % a, [P, R], U8) for a in range(PASSES)]
+        wo_bf = sb("wo_bf", [P, N, 4], BF16)
+        wo_w = sb("wo_w", [P, N], U32)
+        wo_s = sb("wo_s", [P, N], U8)
+        v_w = [sb("v_w%d" % a, [P, S], U32) for a in range(PASSES)]
+        v_s = sb("v_s", [P, S], U8)
+        v_planes = sb("v_planes", [P, PASSES, S], U8)
+        bias_rows = sb("bias_rows", [P, P], F32)
+        ident = sb("ident", [P, P], F32)
+        bias = sb("bias", [P, 10], F32)
+        b_sb = sb("b_sb", [P, 4, S], F32)
+
+        nc.gpsimd.memset(wb_s_raw[:].rearrange("p a c -> p (a c)").bitcast(I32), 0)
+        for q in range(4):
+            nc.vector.memset(tab_s[32 * q : 32 * q + 24, :].bitcast(I32), 0)
+        nc.vector.memset(v_planes[96:128].rearrange("p a c -> p (a c)").bitcast(I32), 0)
+        nc.vector.memset(bias_rows[0:96, :], 0.0)
+        nc.vector.memset(bias_rows[96:118, :], 0.0)
+
+        nc.sync.dma_start(offsets[:], offs)
+        for q in range(4):
+            nc.sync.dma_start(
+                tab_s[32 * q + 24 : 32 * q + 32, :].bitcast(I32), tab_scales[:, 4 * q : 4 * q + 4, :].bitcast(I32)
+            )
+
+        def load_table_words(a):
+            nc.sync.dma_start(tab_w[a][:].bitcast(I32), tab_words[a].rearrange("p t i -> p (t i)").bitcast(I32))
+
+        load_table_words(0)
+        for q in range(4):
+            nc.sync.dma_start(
+                wb_s_raw[32 * q : 32 * q + 4].bitcast(I32),
+                wb_scales[:, 4 * q : 4 * q + 4, :].rearrange("a r c -> r a c").bitcast(I32),
+            )
+        nc.sync.dma_start(wb_raw[:].bitcast(I32), wb_words.rearrange("a p c -> p a c").bitcast(I32))
+        load_table_words(1)
+        nc.sync.dma_start(
+            bias_rows[122:126, :].rearrange("t (q u) -> t q u", u=8), bb.rearrange("(q t u) -> t q u", t=4, u=8)
+        )
+        nc.sync.dma_start(
+            bias_rows[118:122, :].rearrange("t (q u) -> t q u", u=8), ba.rearrange("(q t u) -> t q u", t=4, u=8)
+        )
+        nc.sync.dma_start(bias_rows[126:128, :], bo.rearrange("(h p) -> h p", p=P))
+        nc.sync.dma_start(wa_raw[0][:], wa[0:512, :].rearrange("(p j) c -> p j c", j=4))
+
+        make_identity(nc, ident[:])
+
+        nc.vector.tensor_copy(v_s[:], tab_s[:].indirect(offsets[:]))
+        for a in range(PASSES):
+            shift = 24 + 4 * a
+            nc.scalar.dma_start(v_planes[0 : P - shift, a, :].bitcast(I32), v_s[shift:P, :].bitcast(I32))
+        wa_raw.append(sb("wa_raw1", [P, 4, R], F32, tag="tab_s"))
+        nc.sync.dma_start(wa_raw[1][:], wa[512:1024, :].rearrange("(p j) c -> p j c", j=4))
+        nc.vector.tensor_copy(v_w[0][:], tab_w[0][:].indirect(offsets[:]))
+        wl_w = sb("wl_w", [P, PASSES, N], U32, tag="tab_w0")
+        nc.sync.dma_start(wl_w[:].bitcast(I32), wl_words.rearrange("a p c i -> p a (c i)").bitcast(I32))
+
+        bias_ps = bank(7, "bias_ps")
+        nc.tensor.transpose(bias_ps[:, 0:P], bias_rows[:], ident[:])
+        nc.scalar.activation(bias[:], bias_ps[:, 118:128], IDENTITY)
+
+        nc.vector.tensor_copy(
+            wb_w[:].bitcast(I32).rearrange("p a (t q w) -> p a t q w", t=4, w=4),
+            wb_raw[:].bitcast(I32).rearrange("p a (q t w) -> p a t q w", t=4, w=4),
+        )
+        nc.vector.tensor_copy(
+            wb_s[:].bitcast(I32).rearrange("p a (t q w) -> p a t q w", t=4, w=2),
+            wb_s_raw[:].bitcast(I32).rearrange("p a (q t w) -> p a t q w", t=4, w=2),
+        )
+        wo_raw = sb("wo_raw", [P, 4, N], F32, tag="wb_raw")
+        wo_by_t = wo.rearrange("(q t u) n -> t q u n", t=4, u=8)
+        for t in range(4):
+            nc.sync.dma_start(wo_raw[:, t, :], wo_by_t[t])
+        wl_s = sb("wl_s", [P, PASSES, N], U8, tag="wb_s_raw")
+        nc.gpsimd.memset(wl_s[:].rearrange("p a c -> p (a c)").bitcast(I32), 0)
+        for q in range(4):
+            nc.sync.dma_start(
+                wl_s[32 * q : 32 * q + 4].bitcast(I32),
+                wl_scales[:, 4 * q : 4 * q + 4, :].rearrange("a r c -> r a c").bitcast(I32),
+            )
+        for h in range(2):
+            nc.vector.tensor_copy(
+                v_w[1][:, HALF * h : HALF * (h + 1)], tab_w[1][:].indirect(offsets[:, 32 * h : 32 * (h + 1)])
+            )
+
+        def v_plane(a, cols):
+            return v_planes[:, a, cols]
+
+        b_ps = [[bank(4 * h + t, "b_ps%d%d" % (h, t)) for t in range(4)] for h in range(2)]
+        for a in range(PASSES):
+            for h in range(2):
+                cols = slice(HALF * h, HALF * (h + 1))
+                for t in range(4):
+                    nc.tensor.matmul_mx(
+                        out=b_ps[h][t][:],
+                        lhsT=wb_w[:, a, 256 * t : 256 * (t + 1)].bitcast(FP4X4),
+                        lhsT_scale=wb_s[:, a, P * t : P * (t + 1)],
+                        rhs=v_w[a][:, cols].bitcast(FP8X4),
+                        rhs_scale=v_plane(a, cols),
+                        start=(a == 0),
+                        stop=(a == PASSES - 1),
+                    )
+        for h in range(2):
+            for t in range(4):
+                nc.scalar.activation(
+                    b_sb[:, t, HALF * h : HALF * (h + 1)], b_ps[h][t][:], IDENTITY, bias=bias[:, 4 + t : 5 + t]
+                )
+
+        def round_wa(a, t):
+            nc.vector.tensor_copy(
+                wa_bf[a][:, t, :].rearrange("p (q g i j) -> p q g j i", g=2, i=4, j=4),
+                wa_raw[a][:].rearrange("p j (q t g i) -> p t q g j i", t=4, g=2, i=4)[:, t],
+            )
+
+        def quantise_wa(a, t):
+            cols = slice(P * t, P * (t + 1))
+            nc.vector.quantize_mx(out=wa_w[a][:, cols].bitcast(FP8X4), scales=wa_s[a][:, cols], in_=wa_bf[a][:, t, :])
+
+        steps = [(a, t) for a in range(PASSES) for t in range(4)]
+        for i, step in enumerate(steps):
+            round_wa(*step)
+            if i > 0:
+                quantise_wa(*steps[i - 1])
+        nc.vector.tensor_copy(
+            wo_bf[:].rearrange("p (c i) t -> p c t i", i=4), wo_raw[:].rearrange("p t (c i) -> p c t i", i=4)
+        )
+        quantise_wa(*steps[-1])
+        nc.vector.quantize_mx(out=wo_w[:].bitcast(FP8X4), scales=wo_s[:], in_=wo_bf[:].rearrange("p n t -> p (n t)"))
+
+        a_ps = [[bank(4 * h + t, "a_ps%d%d" % (h, t)) for t in range(4)] for h in range(2)]
+
+        def a_pass(a, h, t):
+            cols = slice(HALF * h, HALF * (h + 1))
+            nc.tensor.matmul_mx(
+                out=a_ps[h][t][:],
+                lhsT=wa_w[a][:, P * t : P * (t + 1)].bitcast(FP8X4),
+                lhsT_scale=wa_s[a][:, P * t : P * (t + 1)],
+                rhs=v_w[a][:, cols].bitcast(FP8X4),
+                rhs_scale=v_plane(a, cols),
+                start=(a == 0),
+                stop=(a == PASSES - 1),
+            )
+
+        for h in range(2):
+            for a in range(PASSES):
+                for t in range(4):
+                    a_pass(a, h, t)
+
+        a_sb = [sb("a_sb%d" % c, [P, 4, hi - lo], F32) for c, (lo, hi) in enumerate(CHUNKS)]
+        h_bf = [sb("h_bf%d" % c, [P, hi - lo, 4], BF16) for c, (lo, hi) in enumerate(CHUNKS)]
+        h_w = [sb("h_w%d" % c, [P, hi - lo], U32) for c, (lo, hi) in enumerate(CHUNKS)]
+        h_s = [sb("h_s%d" % c, [P, hi - lo], U8) for c, (lo, hi) in enumerate(CHUNKS)]
+        for c, (lo, hi) in enumerate(CHUNKS):
+            h = lo // HALF
+            for t in range(4):
+                nc.scalar.activation(
+                    a_sb[c][:, t, :], a_ps[h][t][:, lo - HALF * h : hi - HALF * h], IDENTITY, bias=bias[:, t : t + 1]
+                )
+
+        def cross(c):
+            lo, hi = CHUNKS[c]
+            nc.vector.tensor_tensor(
+                h_bf[c][:].rearrange("p (c i) t -> p c t i", i=4),
+                a_sb[c][:].rearrange("p t (c i) -> p c t i", i=4),
+                b_sb[:, :, lo:hi].rearrange("p t (c i) -> p c t i", i=4),
+                MULT,
+            )
+
+        def quantise_h(c):
+            nc.vector.quantize_mx(
+                out=h_w[c][:].bitcast(FP8X4), scales=h_s[c][:], in_=h_bf[c][:].rearrange("p s t -> p (s t)")
+            )
+
+        for c in range(len(CHUNKS)):
+            cross(c)
+            if c > 0:
+                quantise_h(c - 1)
+        quantise_h(len(CHUNKS) - 1)
+
+        out_by_half = out.rearrange("(h p) s -> p h s", p=P)
+        for g, chunks in enumerate(GROUPS):
+            first, last = CHUNKS[chunks[0]][0], CHUNKS[chunks[-1]][1]
+            y_ps = [bank(2 * g + n, "y_ps%d%d" % (g, n)) for n in range(2)]
+            for c in chunks:
+                lo, hi = CHUNKS[c]
+                for n in range(2):
+                    for a in range(PASSES):
+                        nc.tensor.matmul_mx(
+                            out=y_ps[n][:, lo - first : hi - first],
+                            lhsT=wl_w[:, a, P * n : P * (n + 1)].bitcast(FP8X4),
+                            lhsT_scale=wl_s[:, a, P * n : P * (n + 1)],
+                            rhs=v_w[a][:, lo:hi].bitcast(FP8X4),
+                            rhs_scale=v_plane(a, slice(lo, hi)),
+                            start=(a == 0),
+                            stop=False,
+                        )
+                for n in range(2):
+                    nc.tensor.matmul_mx(
+                        out=y_ps[n][:, lo - first : hi - first],
+                        lhsT=wo_w[:, P * n : P * (n + 1)].bitcast(FP8X4),
+                        lhsT_scale=wo_s[:, P * n : P * (n + 1)],
+                        rhs=h_w[c][:].bitcast(FP8X4),
+                        rhs_scale=h_s[c][:],
+                        start=False,
+                        stop=True,
+                    )
+            y_sb = sb("y_sb%d" % g, [P, 2, last - first], F32)
+            nc.scalar.activation(y_sb[:, 0, :], y_ps[0][:, 0 : last - first], IDENTITY, bias=bias[:, 8:9])
+            if g == len(GROUPS) - 1:
+                nc.vector.tensor_scalar(y_sb[:, 1, :], y_ps[1][:, 0 : last - first], bias[:, 9:10], None, ADD)
+            else:
+                nc.scalar.activation(y_sb[:, 1, :], y_ps[1][:, 0 : last - first], IDENTITY, bias=bias[:, 9:10])
+            nc.sync.dma_start(out_by_half[:, :, first:last], y_sb[:])

@@ -31,6 +31,7 @@ def tile_list_ad_feature_cross_kernel(
     nc = tc.nc
     with ExitStack() as ctx:
         keep = ctx.enter_context(tc.tile_pool(name="keep", bufs=1))
+        reuse = ctx.enter_context(tc.tile_pool(name="reuse", bufs=1))
         psum = ctx.enter_context(tc.psum_pool(name="psum", bufs=1))
 
         def sb(name, shape, dtype, tag=None):
@@ -40,13 +41,12 @@ def tile_list_ad_feature_cross_kernel(
             return psum.tile([P, HALF], F32, name=name, tag="bank%d" % index)
 
         offsets = keep.tile([P, S // 16], U16, name="offsets")
-        tab_s = sb("tab_s", [P, T], U8)
+        tab_s = reuse.tile([P, T], U8, name="tab_s", align_bytes=64, offset=11264)
         tab_w = [sb("tab_w%d" % a, [P, T], U32) for a in range(PASSES)]
         wb_raw = sb("wb_raw", [P, PASSES, 2 * R], U8)
         wb_s_raw = sb("wb_s_raw", [P, PASSES, R], U8)
         wb_w = sb("wb_w", [P, PASSES, 2 * R], U8)
-        wb_s = sb("wb_s", [P, PASSES, R], U8)
-        wa_raw = [sb("wa_raw0", [P, 4, R], F32)]
+        wa_first = sb("wa_first", [P, 4, R // 2], F32)
         wa_bf = [sb("wa_bf%d" % a, [P, 4, 4 * P], BF16) for a in range(PASSES)]
         wa_w = [sb("wa_w%d" % a, [P, R], U32) for a in range(PASSES)]
         wa_s = [sb("wa_s%d" % a, [P, R], U8) for a in range(PASSES)]
@@ -61,12 +61,11 @@ def tile_list_ad_feature_cross_kernel(
         bias = sb("bias", [P, 10], F32)
         b_sb = sb("b_sb", [P, 4, S], F32)
 
-        nc.gpsimd.memset(wb_s_raw[:].rearrange("p a c -> p (a c)").bitcast(I32), 0)
         for q in range(4):
             nc.vector.memset(tab_s[32 * q : 32 * q + 24, :].bitcast(I32), 0)
-        nc.vector.memset(v_planes[96:128].rearrange("p a c -> p (a c)").bitcast(I32), 0)
         nc.vector.memset(bias_rows[0:96, :], 0.0)
         nc.vector.memset(bias_rows[96:118, :], 0.0)
+        nc.gpsimd.memset(v_planes[96:128].rearrange("p a c -> p (a c)").bitcast(I32), 0)
 
         nc.sync.dma_start(offsets[:], offs)
         for q in range(4):
@@ -77,34 +76,51 @@ def tile_list_ad_feature_cross_kernel(
         def load_table_words(a):
             nc.sync.dma_start(tab_w[a][:].bitcast(I32), tab_words[a].rearrange("p t i -> p (t i)").bitcast(I32))
 
-        load_table_words(0)
-        for q in range(4):
-            nc.sync.dma_start(
+        def load_wa(dst, a, half):
+            rows = wa[512 * a : 512 * (a + 1), 256 * half : 256 * (half + 1)]
+            nc.sync.dma_start(dst, rows.rearrange("(p j) c -> p j c", j=4))
+
+        def load_wb_scales(engine, q):
+            engine.dma_start(
                 wb_s_raw[32 * q : 32 * q + 4].bitcast(I32),
                 wb_scales[:, 4 * q : 4 * q + 4, :].rearrange("a r c -> r a c").bitcast(I32),
             )
+
+        load_table_words(0)
         nc.sync.dma_start(wb_raw[:].bitcast(I32), wb_words.rearrange("a p c -> p a c").bitcast(I32))
-        load_table_words(1)
+        for q in range(3):
+            load_wb_scales(nc.sync, q)
         nc.sync.dma_start(
             bias_rows[122:126, :].rearrange("t (q u) -> t q u", u=8), bb.rearrange("(q t u) -> t q u", t=4, u=8)
         )
         nc.sync.dma_start(
             bias_rows[118:122, :].rearrange("t (q u) -> t q u", u=8), ba.rearrange("(q t u) -> t q u", t=4, u=8)
         )
+        load_table_words(1)
         nc.sync.dma_start(bias_rows[126:128, :], bo.rearrange("(h p) -> h p", p=P))
-        nc.sync.dma_start(wa_raw[0][:], wa[0:512, :].rearrange("(p j) c -> p j c", j=4))
+        load_wa(wa_first[:], 0, 0)
 
+        load_wb_scales(nc.gpsimd, 3)
         make_identity(nc, ident[:])
 
         nc.vector.tensor_copy(v_s[:], tab_s[:].indirect(offsets[:]))
         for a in range(PASSES):
             shift = 24 + 4 * a
-            nc.scalar.dma_start(v_planes[0 : P - shift, a, :].bitcast(I32), v_s[shift:P, :].bitcast(I32))
-        wa_raw.append(sb("wa_raw1", [P, 4, R], F32, tag="tab_s"))
-        nc.sync.dma_start(wa_raw[1][:], wa[512:1024, :].rearrange("(p j) c -> p j c", j=4))
-        nc.vector.tensor_copy(v_w[0][:], tab_w[0][:].indirect(offsets[:]))
-        wl_w = sb("wl_w", [P, PASSES, N], U32, tag="tab_w0")
-        nc.sync.dma_start(wl_w[:].bitcast(I32), wl_words.rearrange("a p c i -> p a (c i)").bitcast(I32))
+            (nc.sync if a == 0 else nc.scalar).dma_start(v_planes[0 : P - shift, a, :].bitcast(I32), v_s[shift:P, :].bitcast(I32))
+        wa_rest = reuse.tile([P, 3, 4, R // 2], F32, name="wa_rest", align_bytes=64, offset=0)
+        wb_s = reuse.tile([P, PASSES, R], U8, name="wb_s", align_bytes=64, offset=12288)
+        nc.gpsimd.memset(wb_s[:].rearrange("p a c -> p (a c)").bitcast(I32), 0)
+        wa_raw = [[wa_first[:], wa_rest[:, 0]], [wa_rest[:, 1], wa_rest[:, 2]]]
+        load_wa(wa_raw[0][1], 0, 1)
+        load_wa(wa_raw[1][0], 1, 0)
+        load_wa(wa_raw[1][1], 1, 1)
+
+        def gather_words(a, h):
+            nc.vector.tensor_copy(
+                v_w[a][:, HALF * h : HALF * (h + 1)], tab_w[a][:].indirect(offsets[:, 32 * h : 32 * (h + 1)])
+            )
+
+        gather_words(0, 0)
 
         bias_ps = bank(7, "bias_ps")
         nc.tensor.transpose(bias_ps[:, 0:P], bias_rows[:], ident[:])
@@ -114,11 +130,14 @@ def tile_list_ad_feature_cross_kernel(
             wb_w[:].bitcast(I32).rearrange("p a (t q w) -> p a t q w", t=4, w=4),
             wb_raw[:].bitcast(I32).rearrange("p a (q t w) -> p a t q w", t=4, w=4),
         )
-        nc.vector.tensor_copy(
-            wb_s[:].bitcast(I32).rearrange("p a (t q w) -> p a t q w", t=4, w=2),
-            wb_s_raw[:].bitcast(I32).rearrange("p a (q t w) -> p a t q w", t=4, w=2),
-        )
-        wo_raw = sb("wo_raw", [P, 4, N], F32, tag="wb_raw")
+        for q in range(4):
+            rows = slice(32 * q, 32 * q + 4)
+            nc.vector.tensor_copy(
+                wb_s[rows].bitcast(I32).rearrange("p a (t q w) -> p a t q w", t=4, w=2),
+                wb_s_raw[rows].bitcast(I32).rearrange("p a (q t w) -> p a t q w", t=4, w=2),
+            )
+        gather_words(0, 1)
+        wo_raw = sb("wo_raw", [P, 4, N], F32, tag="tab_w0")
         wo_by_t = wo.rearrange("(q t u) n -> t q u n", t=4, u=8)
         for t in range(4):
             nc.sync.dma_start(wo_raw[:, t, :], wo_by_t[t])
@@ -129,19 +148,29 @@ def tile_list_ad_feature_cross_kernel(
                 wl_s[32 * q : 32 * q + 4].bitcast(I32),
                 wl_scales[:, 4 * q : 4 * q + 4, :].rearrange("a r c -> r a c").bitcast(I32),
             )
-        for h in range(2):
-            nc.vector.tensor_copy(
-                v_w[1][:, HALF * h : HALF * (h + 1)], tab_w[1][:].indirect(offsets[:, 32 * h : 32 * (h + 1)])
-            )
+        gather_words(1, 0)
+        gather_words(1, 1)
+        wl_w = sb("wl_w", [P, PASSES, N], U32, tag="tab_w1")
+        nc.sync.dma_start(wl_w[:].bitcast(I32), wl_words.rearrange("a p c i -> p a (c i)").bitcast(I32))
 
         def v_plane(a, cols):
             return v_planes[:, a, cols]
 
         b_ps = [[bank(4 * h + t, "b_ps%d%d" % (h, t)) for t in range(4)] for h in range(2)]
-        for a in range(PASSES):
-            for h in range(2):
-                cols = slice(HALF * h, HALF * (h + 1))
-                for t in range(4):
+        for t in range(4):
+            nc.tensor.matmul_mx(
+                out=b_ps[0][t][:],
+                lhsT=wb_raw[:, 0, 0:256].bitcast(FP4X4),
+                lhsT_scale=v_s[:, 0:P],
+                rhs=v_w[0][:, 0:HALF].bitcast(FP8X4),
+                rhs_scale=v_s[:, 0:HALF],
+                start=True,
+                stop=True,
+            )
+        for h in range(2):
+            cols = slice(HALF * h, HALF * (h + 1))
+            for t in range(4):
+                for a in range(PASSES):
                     nc.tensor.matmul_mx(
                         out=b_ps[h][t][:],
                         lhsT=wb_w[:, a, 256 * t : 256 * (t + 1)].bitcast(FP4X4),
@@ -157,25 +186,27 @@ def tile_list_ad_feature_cross_kernel(
                     b_sb[:, t, HALF * h : HALF * (h + 1)], b_ps[h][t][:], IDENTITY, bias=bias[:, 4 + t : 5 + t]
                 )
 
-        def round_wa(a, t):
+        def round_wa(a, half, pair):
+            slots = slice(2 * pair, 2 * pair + 2)
             nc.vector.tensor_copy(
-                wa_bf[a][:, t, :].rearrange("p (q g i j) -> p q g j i", g=2, i=4, j=4),
-                wa_raw[a][:].rearrange("p j (q t g i) -> p t q g j i", t=4, g=2, i=4)[:, t],
+                wa_bf[a][:, slots, 256 * half : 256 * (half + 1)].rearrange("p t (q u j) -> p t q j u", u=8, j=4),
+                wa_raw[a][half].rearrange("p j (q t u) -> p t q j u", t=4, u=8)[:, slots],
             )
 
-        def quantise_wa(a, t):
-            cols = slice(P * t, P * (t + 1))
-            nc.vector.quantize_mx(out=wa_w[a][:, cols].bitcast(FP8X4), scales=wa_s[a][:, cols], in_=wa_bf[a][:, t, :])
-
-        steps = [(a, t) for a in range(PASSES) for t in range(4)]
-        for i, step in enumerate(steps):
-            round_wa(*step)
-            if i > 0:
-                quantise_wa(*steps[i - 1])
+        for a in range(PASSES):
+            for half in range(2):
+                for pair in range(2):
+                    round_wa(a, half, pair)
+                for t in range(4):
+                    cols = slice(P * t + 64 * half, P * t + 64 * (half + 1))
+                    nc.vector.quantize_mx(
+                        out=wa_w[a][:, cols].bitcast(FP8X4),
+                        scales=wa_s[a][:, cols],
+                        in_=wa_bf[a][:, t, 256 * half : 256 * (half + 1)],
+                    )
         nc.vector.tensor_copy(
             wo_bf[:].rearrange("p (c i) t -> p c t i", i=4), wo_raw[:].rearrange("p t (c i) -> p c t i", i=4)
         )
-        quantise_wa(*steps[-1])
         nc.vector.quantize_mx(out=wo_w[:].bitcast(FP8X4), scales=wo_s[:], in_=wo_bf[:].rearrange("p n t -> p (n t)"))
 
         a_ps = [[bank(4 * h + t, "a_ps%d%d" % (h, t)) for t in range(4)] for h in range(2)]
@@ -193,8 +224,8 @@ def tile_list_ad_feature_cross_kernel(
             )
 
         for h in range(2):
-            for a in range(PASSES):
-                for t in range(4):
+            for t in range(4):
+                for a in range(PASSES):
                     a_pass(a, h, t)
 
         a_sb = [sb("a_sb%d" % c, [P, 4, hi - lo], F32) for c, (lo, hi) in enumerate(CHUNKS)]

@@ -41,13 +41,11 @@ def tile_list_ad_feature_cross_kernel(
             return psum.tile([P, HALF], F32, name=name, tag="bank%d" % index)
 
         offsets = keep.tile([P, S // 16], U16, name="offsets")
-        tab_s = reuse.tile([P, T], U8, name="tab_s", align_bytes=64, offset=11264)
-        tab_w = [sb("tab_w%d" % a, [P, T], U32) for a in range(PASSES)]
+        tab_s = reuse.tile([P, T], U8, name="tab_s", align_bytes=64, offset=3072)
+        tab_w = [sb("tab_w0", [P, T], U32), reuse.tile([P, T], U32, name="tab_w1", align_bytes=64, offset=5120)]
         wb_raw = sb("wb_raw", [P, PASSES, 2 * R], U8)
         wb_s_raw = sb("wb_s_raw", [P, PASSES, R], U8)
         wb_w = sb("wb_w", [P, PASSES, 2 * R], U8)
-        wa_first = sb("wa_first", [P, 4, R // 2], F32)
-        wa_bf = [sb("wa_bf%d" % a, [P, 4, 4 * P], BF16) for a in range(PASSES)]
         wa_w = [sb("wa_w%d" % a, [P, R], U32) for a in range(PASSES)]
         wa_s = [sb("wa_s%d" % a, [P, R], U8) for a in range(PASSES)]
         wo_bf = sb("wo_bf", [P, N, 4], BF16)
@@ -58,14 +56,12 @@ def tile_list_ad_feature_cross_kernel(
         v_planes = sb("v_planes", [P, PASSES, S], U8)
         bias_rows = sb("bias_rows", [P, P], F32)
         ident = sb("ident", [P, P], F32)
-        bias = sb("bias", [P, 10], F32)
+        bias = sb("bias", [P, 8], F32)
+        bo_sb = sb("bo_sb", [P, 2], F32)
         b_sb = sb("b_sb", [P, 4, S], F32)
 
         for q in range(4):
             nc.vector.memset(tab_s[32 * q : 32 * q + 24, :].bitcast(I32), 0)
-        nc.vector.memset(bias_rows[0:96, :], 0.0)
-        nc.vector.memset(bias_rows[96:118, :], 0.0)
-        nc.gpsimd.memset(v_planes[96:128].rearrange("p a c -> p (a c)").bitcast(I32), 0)
 
         nc.sync.dma_start(offsets[:], offs)
         for q in range(4):
@@ -86,45 +82,41 @@ def tile_list_ad_feature_cross_kernel(
                 wb_scales[:, 4 * q : 4 * q + 4, :].rearrange("a r c -> r a c").bitcast(I32),
             )
 
-        load_table_words(0)
         nc.sync.dma_start(wb_raw[:].bitcast(I32), wb_words.rearrange("a p c -> p a c").bitcast(I32))
-        for q in range(3):
+        load_table_words(0)
+        for q in range(4):
             load_wb_scales(nc.sync, q)
-        nc.sync.dma_start(
-            bias_rows[122:126, :].rearrange("t (q u) -> t q u", u=8), bb.rearrange("(q t u) -> t q u", t=4, u=8)
-        )
-        nc.sync.dma_start(
-            bias_rows[118:122, :].rearrange("t (q u) -> t q u", u=8), ba.rearrange("(q t u) -> t q u", t=4, u=8)
-        )
         load_table_words(1)
-        nc.sync.dma_start(bias_rows[126:128, :], bo.rearrange("(h p) -> h p", p=P))
-        load_wa(wa_first[:], 0, 0)
+        nc.sync.dma_start(
+            bias_rows[124:128, :].rearrange("t (q u) -> t q u", u=8), bb.rearrange("(q t u) -> t q u", t=4, u=8)
+        )
 
-        load_wb_scales(nc.gpsimd, 3)
+        nc.gpsimd.memset(v_planes[96:128].rearrange("p a c -> p (a c)").bitcast(I32), 0)
+        nc.gpsimd.dma_start(
+            bias_rows[120:124, :].rearrange("t (q u) -> t q u", u=8), ba.rearrange("(q t u) -> t q u", t=4, u=8)
+        )
         make_identity(nc, ident[:])
+        nc.gpsimd.memset(bias_rows[0:96, :], 0.0)
+        nc.gpsimd.memset(bias_rows[96:120, :], 0.0)
+        with nc.allow_non_contiguous_dma(reason="one bias value a partition and output half"):
+            nc.gpsimd.dma_start(bo_sb[:], bo.rearrange("(h p) -> p h", p=P))
 
-        nc.vector.tensor_copy(v_s[:], tab_s[:].indirect(offsets[:]))
-        for a in range(PASSES):
-            shift = 24 + 4 * a
-            (nc.sync if a == 0 else nc.scalar).dma_start(v_planes[0 : P - shift, a, :].bitcast(I32), v_s[shift:P, :].bitcast(I32))
-        wa_rest = reuse.tile([P, 3, 4, R // 2], F32, name="wa_rest", align_bytes=64, offset=0)
-        wb_s = reuse.tile([P, PASSES, R], U8, name="wb_s", align_bytes=64, offset=12288)
-        nc.gpsimd.memset(wb_s[:].rearrange("p a c -> p (a c)").bitcast(I32), 0)
-        wa_raw = [[wa_first[:], wa_rest[:, 0]], [wa_rest[:, 1], wa_rest[:, 2]]]
-        load_wa(wa_raw[0][1], 0, 1)
-        load_wa(wa_raw[1][0], 1, 0)
-        load_wa(wa_raw[1][1], 1, 1)
+        for h in range(2):
+            cols = slice(HALF * h, HALF * (h + 1))
+            nc.vector.tensor_copy(v_s[:, cols], tab_s[:].indirect(offsets[:, 32 * h : 32 * (h + 1)]))
+            for a in range(PASSES):
+                shift = 24 + 4 * a
+                nc.scalar.dma_start(v_planes[0:100, a, cols].bitcast(I32), v_s[shift : shift + 100, cols].bitcast(I32))
+        wa_first = reuse.tile([P, 4, R // 2], F32, name="wa_first", align_bytes=64, offset=0)
+        load_wa(wa_first[:], 0, 0)
+        wb_s = reuse.tile([P, PASSES, R], U8, name="wb_s", align_bytes=64, offset=4096)
+        nc.vector.memset(wb_s[:].rearrange("p a c -> p (a c)").bitcast(I32), 0)
 
         def gather_words(a, h):
             nc.vector.tensor_copy(
                 v_w[a][:, HALF * h : HALF * (h + 1)], tab_w[a][:].indirect(offsets[:, 32 * h : 32 * (h + 1)])
             )
 
-        gather_words(0, 0)
-
-        bias_ps = bank(7, "bias_ps")
-        nc.tensor.transpose(bias_ps[:, 0:P], bias_rows[:], ident[:])
-        nc.scalar.activation(bias[:], bias_ps[:, 118:128], IDENTITY)
 
         nc.vector.tensor_copy(
             wb_w[:].bitcast(I32).rearrange("p a (t q w) -> p a t q w", t=4, w=4),
@@ -136,55 +128,78 @@ def tile_list_ad_feature_cross_kernel(
                 wb_s[rows].bitcast(I32).rearrange("p a (t q w) -> p a t q w", t=4, w=2),
                 wb_s_raw[rows].bitcast(I32).rearrange("p a (q t w) -> p a t q w", t=4, w=2),
             )
+        warm_ps = bank(7, "warm_ps")
+        for t in range(4):
+            nc.tensor.matmul_mx(
+                out=warm_ps[:],
+                lhsT=wb_w[:, 0, 0:256].bitcast(FP4X4),
+                lhsT_scale=wb_s[:, 0, 0:P],
+                rhs=tab_w[0][:, 0:HALF].bitcast(FP8X4),
+                rhs_scale=v_s[:, 0:HALF],
+                start=True,
+                stop=True,
+            )
+        bias_ps = bank(7, "bias_ps")
+        nc.tensor.transpose(bias_ps[:, 0:P], bias_rows[:], ident[:])
+        nc.scalar.activation(bias[:], bias_ps[:, 120:128], IDENTITY)
+
+        gather_words(0, 0)
+        wa_rest = sb("wa_rest", [P, 3, 4, R // 2], F32, tag="wb_s_raw")
+        wa_raw = [[wa_first[:], wa_rest[:, 0]], [wa_rest[:, 1], wa_rest[:, 2]]]
+        load_wa(wa_raw[0][1], 0, 1)
+        load_wa(wa_raw[1][0], 1, 0)
+        load_wa(wa_raw[1][1], 1, 1)
         gather_words(0, 1)
         wo_raw = sb("wo_raw", [P, 4, N], F32, tag="tab_w0")
         wo_by_t = wo.rearrange("(q t u) n -> t q u n", t=4, u=8)
         for t in range(4):
             nc.sync.dma_start(wo_raw[:, t, :], wo_by_t[t])
-        wl_s = sb("wl_s", [P, PASSES, N], U8, tag="wb_s_raw")
+        gather_words(1, 0)
+        gather_words(1, 1)
+        wa_bf = [
+            reuse.tile([P, 4, 4 * P], BF16, name="wa_bf0", align_bytes=64, offset=5120),
+            sb("wa_bf1", [P, 4, 4 * P], BF16),
+        ]
+        wl_w = reuse.tile([P, PASSES, N], U32, name="wl_w", align_bytes=64, offset=9216)
+        nc.sync.dma_start(wl_w[:].bitcast(I32), wl_words.rearrange("a p c i -> p a (c i)").bitcast(I32))
+        wl_s = reuse.tile([P, PASSES, N], U8, name="wl_s", align_bytes=64, offset=11264)
         nc.gpsimd.memset(wl_s[:].rearrange("p a c -> p (a c)").bitcast(I32), 0)
         for q in range(4):
             nc.sync.dma_start(
                 wl_s[32 * q : 32 * q + 4].bitcast(I32),
                 wl_scales[:, 4 * q : 4 * q + 4, :].rearrange("a r c -> r a c").bitcast(I32),
             )
-        gather_words(1, 0)
-        gather_words(1, 1)
-        wl_w = sb("wl_w", [P, PASSES, N], U32, tag="tab_w1")
-        nc.sync.dma_start(wl_w[:].bitcast(I32), wl_words.rearrange("a p c i -> p a (c i)").bitcast(I32))
 
         def v_plane(a, cols):
             return v_planes[:, a, cols]
 
         b_ps = [[bank(4 * h + t, "b_ps%d%d" % (h, t)) for t in range(4)] for h in range(2)]
-        for t in range(4):
-            nc.tensor.matmul_mx(
-                out=b_ps[0][t][:],
-                lhsT=wb_raw[:, 0, 0:256].bitcast(FP4X4),
-                lhsT_scale=v_s[:, 0:P],
-                rhs=v_w[0][:, 0:HALF].bitcast(FP8X4),
-                rhs_scale=v_s[:, 0:HALF],
-                start=True,
-                stop=True,
-            )
-        for h in range(2):
+
+        def pass_order(h):
+            return (0, 1) if h == 0 else (1, 0)
+
+        def b_half(h):
             cols = slice(HALF * h, HALF * (h + 1))
             for t in range(4):
-                for a in range(PASSES):
+                for i, a in enumerate(pass_order(h)):
                     nc.tensor.matmul_mx(
                         out=b_ps[h][t][:],
                         lhsT=wb_w[:, a, 256 * t : 256 * (t + 1)].bitcast(FP4X4),
                         lhsT_scale=wb_s[:, a, P * t : P * (t + 1)],
                         rhs=v_w[a][:, cols].bitcast(FP8X4),
                         rhs_scale=v_plane(a, cols),
-                        start=(a == 0),
-                        stop=(a == PASSES - 1),
+                        start=(i == 0),
+                        stop=(i == PASSES - 1),
                     )
-        for h in range(2):
+
+        def b_out(h):
             for t in range(4):
                 nc.scalar.activation(
                     b_sb[:, t, HALF * h : HALF * (h + 1)], b_ps[h][t][:], IDENTITY, bias=bias[:, 4 + t : 5 + t]
                 )
+
+        b_half(0)
+        b_out(0)
 
         def round_wa(a, half, pair):
             slots = slice(2 * pair, 2 * pair + 2)
@@ -209,35 +224,39 @@ def tile_list_ad_feature_cross_kernel(
         )
         nc.vector.quantize_mx(out=wo_w[:].bitcast(FP8X4), scales=wo_s[:], in_=wo_bf[:].rearrange("p n t -> p (n t)"))
 
-        a_ps = [[bank(4 * h + t, "a_ps%d%d" % (h, t)) for t in range(4)] for h in range(2)]
-
-        def a_pass(a, h, t):
-            cols = slice(HALF * h, HALF * (h + 1))
-            nc.tensor.matmul_mx(
-                out=a_ps[h][t][:],
-                lhsT=wa_w[a][:, P * t : P * (t + 1)].bitcast(FP8X4),
-                lhsT_scale=wa_s[a][:, P * t : P * (t + 1)],
-                rhs=v_w[a][:, cols].bitcast(FP8X4),
-                rhs_scale=v_plane(a, cols),
-                start=(a == 0),
-                stop=(a == PASSES - 1),
-            )
-
-        for h in range(2):
-            for t in range(4):
-                for a in range(PASSES):
-                    a_pass(a, h, t)
-
         a_sb = [sb("a_sb%d" % c, [P, 4, hi - lo], F32) for c, (lo, hi) in enumerate(CHUNKS)]
         h_bf = [sb("h_bf%d" % c, [P, hi - lo, 4], BF16) for c, (lo, hi) in enumerate(CHUNKS)]
         h_w = [sb("h_w%d" % c, [P, hi - lo], U32) for c, (lo, hi) in enumerate(CHUNKS)]
         h_s = [sb("h_s%d" % c, [P, hi - lo], U8) for c, (lo, hi) in enumerate(CHUNKS)]
-        for c, (lo, hi) in enumerate(CHUNKS):
-            h = lo // HALF
+
+        def a_half(h):
+            cols = slice(HALF * h, HALF * (h + 1))
+            a_ps = [bank(4 * h + t, "a_ps%d%d" % (h, t)) for t in range(4)]
             for t in range(4):
-                nc.scalar.activation(
-                    a_sb[c][:, t, :], a_ps[h][t][:, lo - HALF * h : hi - HALF * h], IDENTITY, bias=bias[:, t : t + 1]
-                )
+                for i, a in enumerate(pass_order(h)):
+                    nc.tensor.matmul_mx(
+                        out=a_ps[t][:],
+                        lhsT=wa_w[a][:, P * t : P * (t + 1)].bitcast(FP8X4),
+                        lhsT_scale=wa_s[a][:, P * t : P * (t + 1)],
+                        rhs=v_w[a][:, cols].bitcast(FP8X4),
+                        rhs_scale=v_plane(a, cols),
+                        start=(i == 0),
+                        stop=(i == PASSES - 1),
+                    )
+            for c, (lo, hi) in enumerate(CHUNKS):
+                if lo // HALF == h:
+                    for t in range(4):
+                        nc.scalar.activation(
+                            a_sb[c][:, t, :],
+                            a_ps[t][:, lo - HALF * h : hi - HALF * h],
+                            IDENTITY,
+                            bias=bias[:, t : t + 1],
+                        )
+
+        a_half(0)
+        b_half(1)
+        b_out(1)
+        a_half(1)
 
         def cross(c):
             lo, hi = CHUNKS[c]
@@ -287,9 +306,9 @@ def tile_list_ad_feature_cross_kernel(
                         stop=True,
                     )
             y_sb = sb("y_sb%d" % g, [P, 2, last - first], F32)
-            nc.scalar.activation(y_sb[:, 0, :], y_ps[0][:, 0 : last - first], IDENTITY, bias=bias[:, 8:9])
+            nc.scalar.activation(y_sb[:, 0, :], y_ps[0][:, 0 : last - first], IDENTITY, bias=bo_sb[:, 0:1])
             if g == len(GROUPS) - 1:
-                nc.vector.tensor_scalar(y_sb[:, 1, :], y_ps[1][:, 0 : last - first], bias[:, 9:10], None, ADD)
+                nc.vector.tensor_scalar(y_sb[:, 1, :], y_ps[1][:, 0 : last - first], bo_sb[:, 1:2], None, ADD)
             else:
-                nc.scalar.activation(y_sb[:, 1, :], y_ps[1][:, 0 : last - first], IDENTITY, bias=bias[:, 9:10])
+                nc.scalar.activation(y_sb[:, 1, :], y_ps[1][:, 0 : last - first], IDENTITY, bias=bo_sb[:, 1:2])
             nc.sync.dma_start(out_by_half[:, :, first:last], y_sb[:])

@@ -34,195 +34,156 @@ def tile_list_ad_feature_cross_kernel(
         reuse = ctx.enter_context(tc.tile_pool(name="reuse", bufs=1))
         psum = ctx.enter_context(tc.psum_pool(name="psum", bufs=1))
 
-        def sb(name, shape, dtype, tag=None):
-            return keep.tile(shape, dtype, name=name, tag=tag or name, align_bytes=64)
+        def sb(name, shape, dtype):
+            return keep.tile(shape, dtype, name=name, align_bytes=64)
 
         def bank(index, name):
             return psum.tile([P, HALF], F32, name=name, tag="bank%d" % index)
 
         offsets = keep.tile([P, S // 16], U16, name="offsets")
-        tab_s = reuse.tile([P, T], U8, name="tab_s", align_bytes=64, offset=3072)
-        tab_w = [sb("tab_w0", [P, T], U32), reuse.tile([P, T], U32, name="tab_w1", align_bytes=64, offset=5120)]
+        tab_s = sb("tab_s", [P, T], U8)
+        tab_w = [sb("tab_w%d" % a, [P, T], U32) for a in range(PASSES)]
         wb_raw = sb("wb_raw", [P, PASSES, 2 * R], U8)
-        wb_s_raw = sb("wb_s_raw", [P, PASSES, R], U8)
+        wb_s_raw = reuse.tile([P, PASSES, R], U8, name="wb_s_raw", align_bytes=64, offset=1536)
         wb_w = sb("wb_w", [P, PASSES, 2 * R], U8)
+        wb_s = sb("wb_s", [P, PASSES, R], U8)
+        wl_w = sb("wl_w", [P, PASSES, N], U32)
+        wl_s = sb("wl_s", [P, PASSES, N], U8)
+        wa_raw0 = sb("wa_raw0", [P, 4, R], F32)
+        wa_bf = [sb("wa_bf%d" % a, [P, 4, 4 * P], BF16) for a in range(PASSES)]
         wa_w = [sb("wa_w%d" % a, [P, R], U32) for a in range(PASSES)]
         wa_s = [sb("wa_s%d" % a, [P, R], U8) for a in range(PASSES)]
+        wo_raw = sb("wo_raw", [P, 4, N], F32)
         wo_bf = sb("wo_bf", [P, N, 4], BF16)
         wo_w = sb("wo_w", [P, N], U32)
         wo_s = sb("wo_s", [P, N], U8)
-        v_w = [sb("v_w%d" % a, [P, S], U32) for a in range(PASSES)]
         v_s = sb("v_s", [P, S], U8)
-        v_planes = sb("v_planes", [P, PASSES, S], U8)
+        v_s1 = sb("v_s1", [P, S], U8)
         bias_rows = sb("bias_rows", [P, P], F32)
         ident = sb("ident", [P, P], F32)
         bias = sb("bias", [P, 8], F32)
         bo_sb = sb("bo_sb", [P, 2], F32)
         b_sb = sb("b_sb", [P, 4, S], F32)
 
-        for q in range(4):
-            nc.vector.memset(tab_s[32 * q : 32 * q + 24, :].bitcast(I32), 0)
+        nc.gpsimd.memset(tab_s[:, 0 : T // 2].bitcast(I32), 0)
+        nc.vector.memset(tab_s[:, T // 2 : T].bitcast(I32), 0)
+        nc.gpsimd.memset(wb_s_raw[:].rearrange("p a c -> p (a c)").bitcast(I32), 0)
+        nc.vector.memset(v_s1[96:128, :].bitcast(I32), 0)
+        nc.vector.memset(wl_s[:].rearrange("p a c -> p (a c)").bitcast(I32), 0)
+        nc.vector.memset(bias_rows[0:96, :], 0.0)
+        nc.vector.memset(bias_rows[96:120, :], 0.0)
 
-        nc.sync.dma_start(offsets[:], offs)
-        for q in range(4):
-            nc.sync.dma_start(
-                tab_s[32 * q + 24 : 32 * q + 32, :].bitcast(I32), tab_scales[:, 4 * q : 4 * q + 4, :].bitcast(I32)
-            )
+        def load_scale_rows(dst, src):
+            for q in range(4):
+                nc.sync.dma_start(
+                    dst[32 * q : 32 * q + 4].bitcast(I32),
+                    src[:, 4 * q : 4 * q + 4, :].rearrange("a r c -> r a c").bitcast(I32),
+                )
 
         def load_table_words(a):
             nc.sync.dma_start(tab_w[a][:].bitcast(I32), tab_words[a].rearrange("p t i -> p (t i)").bitcast(I32))
 
-        def load_wa(dst, a, half):
-            rows = wa[512 * a : 512 * (a + 1), 256 * half : 256 * (half + 1)]
-            nc.sync.dma_start(dst, rows.rearrange("(p j) c -> p j c", j=4))
+        def load_wa(dst, a):
+            nc.sync.dma_start(dst[:], wa[512 * a : 512 * (a + 1), :].rearrange("(p j) c -> p j c", j=4))
 
-        def load_wb_scales(engine, q):
-            engine.dma_start(
-                wb_s_raw[32 * q : 32 * q + 4].bitcast(I32),
-                wb_scales[:, 4 * q : 4 * q + 4, :].rearrange("a r c -> r a c").bitcast(I32),
-            )
-
+        nc.sync.dma_start(offsets[:], offs)
         nc.sync.dma_start(wb_raw[:].bitcast(I32), wb_words.rearrange("a p c -> p a c").bitcast(I32))
-        load_table_words(0)
         for q in range(4):
-            load_wb_scales(nc.sync, q)
+            nc.sync.dma_start(
+                tab_s[32 * q : 32 * q + 8, :].bitcast(I32), tab_scales[:, 4 * q : 4 * q + 4, :].bitcast(I32)
+            )
+        load_table_words(0)
+        load_scale_rows(wb_s_raw, wb_scales)
         load_table_words(1)
         nc.sync.dma_start(
             bias_rows[124:128, :].rearrange("t (q u) -> t q u", u=8), bb.rearrange("(q t u) -> t q u", t=4, u=8)
         )
+        load_wa(wa_raw0, 0)
 
-        nc.gpsimd.memset(v_planes[96:128].rearrange("p a c -> p (a c)").bitcast(I32), 0)
         nc.gpsimd.dma_start(
             bias_rows[120:124, :].rearrange("t (q u) -> t q u", u=8), ba.rearrange("(q t u) -> t q u", t=4, u=8)
         )
         make_identity(nc, ident[:])
-        nc.gpsimd.memset(bias_rows[0:96, :], 0.0)
-        nc.gpsimd.memset(bias_rows[96:120, :], 0.0)
         with nc.allow_non_contiguous_dma(reason="one bias value a partition and output half"):
             nc.gpsimd.dma_start(bo_sb[:], bo.rearrange("(h p) -> p h", p=P))
 
-        for h in range(2):
-            cols = slice(HALF * h, HALF * (h + 1))
-            nc.vector.tensor_copy(v_s[:, cols], tab_s[:].indirect(offsets[:, 32 * h : 32 * (h + 1)]))
-            for a in range(PASSES):
-                shift = 24 + 4 * a
-                nc.scalar.dma_start(v_planes[0:100, a, cols].bitcast(I32), v_s[shift : shift + 100, cols].bitcast(I32))
-        wa_first = reuse.tile([P, 4, R // 2], F32, name="wa_first", align_bytes=64, offset=0)
-        load_wa(wa_first[:], 0, 0)
-        wb_s = reuse.tile([P, PASSES, R], U8, name="wb_s", align_bytes=64, offset=4096)
-        nc.vector.memset(wb_s[:].rearrange("p a c -> p (a c)").bitcast(I32), 0)
+        nc.vector.tensor_copy(v_s[:], tab_s[:].indirect(offsets[:]))
+        nc.scalar.dma_start(v_s1[0:112, :].bitcast(I32), v_s[4:116, :].bitcast(I32))
 
-        def gather_words(a, h):
-            nc.vector.tensor_copy(
-                v_w[a][:, HALF * h : HALF * (h + 1)], tab_w[a][:].indirect(offsets[:, 32 * h : 32 * (h + 1)])
-            )
-
+        def gather_words(a, h, dst):
+            nc.vector.tensor_copy(dst[:], tab_w[a][:].indirect(offsets[:, 32 * h : 32 * (h + 1)]))
+            return dst
 
         nc.vector.tensor_copy(
             wb_w[:].bitcast(I32).rearrange("p a (t q w) -> p a t q w", t=4, w=4),
             wb_raw[:].bitcast(I32).rearrange("p a (q t w) -> p a t q w", t=4, w=4),
         )
-        for q in range(4):
-            rows = slice(32 * q, 32 * q + 4)
-            nc.vector.tensor_copy(
-                wb_s[rows].bitcast(I32).rearrange("p a (t q w) -> p a t q w", t=4, w=2),
-                wb_s_raw[rows].bitcast(I32).rearrange("p a (q t w) -> p a t q w", t=4, w=2),
-            )
-        warm_ps = bank(7, "warm_ps")
+        v_w00 = gather_words(0, 0, sb("v_w00", [P, HALF], U32))
+        nc.vector.tensor_copy(
+            wb_s[:].bitcast(I32).rearrange("p a (t q w) -> p a t q w", t=4, w=2),
+            wb_s_raw[:].bitcast(I32).rearrange("p a (q t w) -> p a t q w", t=4, w=2),
+        )
+        v_w01 = gather_words(0, 1, reuse.tile([P, HALF], U32, name="v_w01", align_bytes=64, offset=0))
+        v_w = [[v_w00, v_w01], [gather_words(1, h, sb("v_w1%d" % h, [P, HALF], U32)) for h in range(2)]]
+
+        wa_raw = [wa_raw0, reuse.tile([P, 4, R], F32, name="wa_raw1", align_bytes=64, offset=2048)]
+        load_wa(wa_raw[1], 1)
+        wo_by_t = wo.rearrange("(q t u) n -> t q u n", t=4, u=8)
         for t in range(4):
-            nc.tensor.matmul_mx(
-                out=warm_ps[:],
-                lhsT=wb_w[:, 0, 0:256].bitcast(FP4X4),
-                lhsT_scale=wb_s[:, 0, 0:P],
-                rhs=tab_w[0][:, 0:HALF].bitcast(FP8X4),
-                rhs_scale=v_s[:, 0:HALF],
-                start=True,
-                stop=True,
-            )
+            nc.sync.dma_start(wo_raw[:, t, :], wo_by_t[t])
+        nc.sync.dma_start(wl_w[:].bitcast(I32), wl_words.rearrange("a p c i -> p a (c i)").bitcast(I32))
+        load_scale_rows(wl_s, wl_scales)
+
         bias_ps = bank(7, "bias_ps")
         nc.tensor.transpose(bias_ps[:, 0:P], bias_rows[:], ident[:])
         nc.scalar.activation(bias[:], bias_ps[:, 120:128], IDENTITY)
 
-        gather_words(0, 0)
-        wa_rest = sb("wa_rest", [P, 3, 4, R // 2], F32, tag="wb_s_raw")
-        wa_raw = [[wa_first[:], wa_rest[:, 0]], [wa_rest[:, 1], wa_rest[:, 2]]]
-        load_wa(wa_raw[0][1], 0, 1)
-        load_wa(wa_raw[1][0], 1, 0)
-        load_wa(wa_raw[1][1], 1, 1)
-        gather_words(0, 1)
-        wo_raw = sb("wo_raw", [P, 4, N], F32, tag="tab_w0")
-        wo_by_t = wo.rearrange("(q t u) n -> t q u n", t=4, u=8)
-        for t in range(4):
-            nc.sync.dma_start(wo_raw[:, t, :], wo_by_t[t])
-        gather_words(1, 0)
-        gather_words(1, 1)
-        wa_bf = [
-            reuse.tile([P, 4, 4 * P], BF16, name="wa_bf0", align_bytes=64, offset=5120),
-            sb("wa_bf1", [P, 4, 4 * P], BF16),
-        ]
-        wl_w = reuse.tile([P, PASSES, N], U32, name="wl_w", align_bytes=64, offset=9216)
-        nc.sync.dma_start(wl_w[:].bitcast(I32), wl_words.rearrange("a p c i -> p a (c i)").bitcast(I32))
-        wl_s = reuse.tile([P, PASSES, N], U8, name="wl_s", align_bytes=64, offset=11264)
-        nc.gpsimd.memset(wl_s[:].rearrange("p a c -> p (a c)").bitcast(I32), 0)
-        for q in range(4):
-            nc.sync.dma_start(
-                wl_s[32 * q : 32 * q + 4].bitcast(I32),
-                wl_scales[:, 4 * q : 4 * q + 4, :].rearrange("a r c -> r a c").bitcast(I32),
-            )
+        def v_words(a, lo, hi):
+            h = lo // HALF
+            return v_w[a][h][:, lo - HALF * h : hi - HALF * h].bitcast(FP8X4)
 
-        def v_plane(a, cols):
-            return v_planes[:, a, cols]
-
-        b_ps = [[bank(4 * h + t, "b_ps%d%d" % (h, t)) for t in range(4)] for h in range(2)]
-
-        def pass_order(h):
-            return (0, 1) if h == 0 else (1, 0)
-
-        def b_half(h):
+        for h in range(2):
             cols = slice(HALF * h, HALF * (h + 1))
             for t in range(4):
-                for i, a in enumerate(pass_order(h)):
+                b_ps = bank(4 * h + t, "b_ps%d%d" % (h, t))
+                for a in range(PASSES):
                     nc.tensor.matmul_mx(
-                        out=b_ps[h][t][:],
+                        out=b_ps[:],
                         lhsT=wb_w[:, a, 256 * t : 256 * (t + 1)].bitcast(FP4X4),
                         lhsT_scale=wb_s[:, a, P * t : P * (t + 1)],
-                        rhs=v_w[a][:, cols].bitcast(FP8X4),
-                        rhs_scale=v_plane(a, cols),
-                        start=(i == 0),
-                        stop=(i == PASSES - 1),
+                        rhs=v_words(a, HALF * h, HALF * (h + 1)),
+                        rhs_scale=(v_s, v_s1)[a][:, cols],
+                        start=(a == 0),
+                        stop=(a == PASSES - 1),
                     )
+                nc.scalar.activation(b_sb[:, t, cols], b_ps[:], IDENTITY, bias=bias[:, 4 + t : 5 + t])
 
-        def b_out(h):
-            for t in range(4):
-                nc.scalar.activation(
-                    b_sb[:, t, HALF * h : HALF * (h + 1)], b_ps[h][t][:], IDENTITY, bias=bias[:, 4 + t : 5 + t]
-                )
-
-        b_half(0)
-        b_out(0)
-
-        def round_wa(a, half, pair):
-            slots = slice(2 * pair, 2 * pair + 2)
+        def round_wa(a, t):
             nc.vector.tensor_copy(
-                wa_bf[a][:, slots, 256 * half : 256 * (half + 1)].rearrange("p t (q u j) -> p t q j u", u=8, j=4),
-                wa_raw[a][half].rearrange("p j (q t u) -> p t q j u", t=4, u=8)[:, slots],
+                wa_bf[a][:, t, :].rearrange("p (q g i j) -> p q g j i", g=2, i=4, j=4),
+                wa_raw[a][:].rearrange("p j (q t g i) -> p t q g j i", t=4, g=2, i=4)[:, t],
             )
 
-        for a in range(PASSES):
-            for half in range(2):
-                for pair in range(2):
-                    round_wa(a, half, pair)
-                for t in range(4):
-                    cols = slice(P * t + 64 * half, P * t + 64 * (half + 1))
-                    nc.vector.quantize_mx(
-                        out=wa_w[a][:, cols].bitcast(FP8X4),
-                        scales=wa_s[a][:, cols],
-                        in_=wa_bf[a][:, t, 256 * half : 256 * (half + 1)],
-                    )
+        def quantise_wa(a, t):
+            cols = slice(P * t, P * (t + 1))
+            nc.vector.quantize_mx(out=wa_w[a][:, cols].bitcast(FP8X4), scales=wa_s[a][:, cols], in_=wa_bf[a][:, t, :])
+
+        steps = [(a, t) for a in range(PASSES) for t in range(4)]
+        for i, step in enumerate(steps):
+            round_wa(*step)
+            if i > 0:
+                quantise_wa(*steps[i - 1])
+        quantise_wa(*steps[-1])
         nc.vector.tensor_copy(
             wo_bf[:].rearrange("p (c i) t -> p c t i", i=4), wo_raw[:].rearrange("p t (c i) -> p c t i", i=4)
         )
         nc.vector.quantize_mx(out=wo_w[:].bitcast(FP8X4), scales=wo_s[:], in_=wo_bf[:].rearrange("p n t -> p (n t)"))
+
+        def pass_order(h):
+            return (0, 1) if h == 0 else (1, 0)
+
+        def v_plane(a, cols):
+            return (v_s, v_s1)[a][:, cols]
 
         a_sb = [sb("a_sb%d" % c, [P, 4, hi - lo], F32) for c, (lo, hi) in enumerate(CHUNKS)]
         h_bf = [sb("h_bf%d" % c, [P, hi - lo, 4], BF16) for c, (lo, hi) in enumerate(CHUNKS)]
@@ -238,7 +199,7 @@ def tile_list_ad_feature_cross_kernel(
                         out=a_ps[t][:],
                         lhsT=wa_w[a][:, P * t : P * (t + 1)].bitcast(FP8X4),
                         lhsT_scale=wa_s[a][:, P * t : P * (t + 1)],
-                        rhs=v_w[a][:, cols].bitcast(FP8X4),
+                        rhs=v_words(a, HALF * h, HALF * (h + 1)),
                         rhs_scale=v_plane(a, cols),
                         start=(i == 0),
                         stop=(i == PASSES - 1),
@@ -254,16 +215,14 @@ def tile_list_ad_feature_cross_kernel(
                         )
 
         a_half(0)
-        b_half(1)
-        b_out(1)
         a_half(1)
 
         def cross(c):
             lo, hi = CHUNKS[c]
             nc.vector.tensor_tensor(
-                h_bf[c][:].rearrange("p (c i) t -> p c t i", i=4),
-                a_sb[c][:].rearrange("p t (c i) -> p c t i", i=4),
-                b_sb[:, :, lo:hi].rearrange("p t (c i) -> p c t i", i=4),
+                h_bf[c][:].rearrange("p (c i) t -> p c t i", i=2),
+                a_sb[c][:].rearrange("p t (c i) -> p c t i", i=2),
+                b_sb[:, :, lo:hi].rearrange("p t (c i) -> p c t i", i=2),
                 MULT,
             )
 
@@ -290,7 +249,7 @@ def tile_list_ad_feature_cross_kernel(
                             out=y_ps[n][:, lo - first : hi - first],
                             lhsT=wl_w[:, a, P * n : P * (n + 1)].bitcast(FP8X4),
                             lhsT_scale=wl_s[:, a, P * n : P * (n + 1)],
-                            rhs=v_w[a][:, lo:hi].bitcast(FP8X4),
+                            rhs=v_words(a, lo, hi),
                             rhs_scale=v_plane(a, slice(lo, hi)),
                             start=(a == 0),
                             stop=False,

@@ -22,7 +22,7 @@ P = 128
 PASSES = K // 512
 HALF = 512
 CHUNKS = [(0, 128), (128, 256), (256, 512), (512, 768), (768, 896), (896, 1024)]
-GROUPS = [(0, 1, 2), (3, 4), (5,)]
+GROUPS = [(0, 1, 2), (3,), (4,), (5,)]
 
 
 def tile_list_ad_feature_cross_kernel(
@@ -61,8 +61,7 @@ def tile_list_ad_feature_cross_kernel(
         v_s1 = sb("v_s1", [P, S], U8)
         bias_rows = sb("bias_rows", [P, P], F32)
         ident = sb("ident", [P, P], F32)
-        bias = sb("bias", [P, 8], F32)
-        bo_sb = sb("bo_sb", [P, 2], F32)
+        bias = sb("bias", [P, 10], F32)
         b_sb = sb("b_sb", [P, 4, S], F32)
 
         nc.gpsimd.memset(tab_s[:, 0 : T // 2].bitcast(I32), 0)
@@ -71,7 +70,7 @@ def tile_list_ad_feature_cross_kernel(
         nc.vector.memset(v_s1[96:128, :].bitcast(I32), 0)
         nc.vector.memset(wl_s[:].rearrange("p a c -> p (a c)").bitcast(I32), 0)
         nc.vector.memset(bias_rows[0:96, :], 0.0)
-        nc.vector.memset(bias_rows[96:120, :], 0.0)
+        nc.vector.memset(bias_rows[96:118, :], 0.0)
 
         def load_scale_rows(dst, src):
             for q in range(4):
@@ -96,16 +95,15 @@ def tile_list_ad_feature_cross_kernel(
         load_scale_rows(wb_s_raw, wb_scales)
         load_table_words(1)
         nc.sync.dma_start(
-            bias_rows[124:128, :].rearrange("t (q u) -> t q u", u=8), bb.rearrange("(q t u) -> t q u", t=4, u=8)
+            bias_rows[122:126, :].rearrange("t (q u) -> t q u", u=8), bb.rearrange("(q t u) -> t q u", t=4, u=8)
         )
         load_wa(wa_raw0, 0)
 
         nc.gpsimd.dma_start(
-            bias_rows[120:124, :].rearrange("t (q u) -> t q u", u=8), ba.rearrange("(q t u) -> t q u", t=4, u=8)
+            bias_rows[118:122, :].rearrange("t (q u) -> t q u", u=8), ba.rearrange("(q t u) -> t q u", t=4, u=8)
         )
+        nc.gpsimd.dma_start(bias_rows[126:128, :], bo.rearrange("(h p) -> h p", p=P))
         make_identity(nc, ident[:])
-        with nc.allow_non_contiguous_dma(reason="one bias value a partition and output half"):
-            nc.gpsimd.dma_start(bo_sb[:], bo.rearrange("(h p) -> p h", p=P))
 
         nc.vector.tensor_copy(v_s[:], tab_s[:].indirect(offsets[:]))
         nc.scalar.dma_start(v_s1[0:112, :].bitcast(I32), v_s[4:116, :].bitcast(I32))
@@ -136,7 +134,7 @@ def tile_list_ad_feature_cross_kernel(
 
         bias_ps = bank(7, "bias_ps")
         nc.tensor.transpose(bias_ps[:, 0:P], bias_rows[:], ident[:])
-        nc.scalar.activation(bias[:], bias_ps[:, 120:128], IDENTITY)
+        nc.scalar.activation(bias[:], bias_ps[:, 118:128], IDENTITY)
 
         def v_words(a, lo, hi):
             h = lo // HALF
@@ -207,12 +205,11 @@ def tile_list_ad_feature_cross_kernel(
             for c, (lo, hi) in enumerate(CHUNKS):
                 if lo // HALF == h:
                     for t in range(4):
-                        nc.scalar.activation(
-                            a_sb[c][:, t, :],
-                            a_ps[t][:, lo - HALF * h : hi - HALF * h],
-                            IDENTITY,
-                            bias=bias[:, t : t + 1],
-                        )
+                        sums = a_ps[t][:, lo - HALF * h : hi - HALF * h]
+                        if c == 0:
+                            nc.vector.tensor_scalar(a_sb[c][:, t, :], sums, bias[:, t : t + 1], None, ADD)
+                        else:
+                            nc.scalar.activation(a_sb[c][:, t, :], sums, IDENTITY, bias=bias[:, t : t + 1])
 
         a_half(0)
         a_half(1)
@@ -231,11 +228,13 @@ def tile_list_ad_feature_cross_kernel(
                 out=h_w[c][:].bitcast(FP8X4), scales=h_s[c][:], in_=h_bf[c][:].rearrange("p s t -> p (s t)")
             )
 
-        for c in range(len(CHUNKS)):
-            cross(c)
-            if c > 0:
-                quantise_h(c - 1)
-        quantise_h(len(CHUNKS) - 1)
+        for h in range(2):
+            chunks = [c for c, (lo, hi) in enumerate(CHUNKS) if lo // HALF == h]
+            for c in chunks:
+                cross(c)
+                if c > chunks[0]:
+                    quantise_h(c - 1)
+            quantise_h(chunks[-1])
 
         out_by_half = out.rearrange("(h p) s -> p h s", p=P)
         for g, chunks in enumerate(GROUPS):
@@ -265,9 +264,9 @@ def tile_list_ad_feature_cross_kernel(
                         stop=True,
                     )
             y_sb = sb("y_sb%d" % g, [P, 2, last - first], F32)
-            nc.scalar.activation(y_sb[:, 0, :], y_ps[0][:, 0 : last - first], IDENTITY, bias=bo_sb[:, 0:1])
+            nc.scalar.activation(y_sb[:, 0, :], y_ps[0][:, 0 : last - first], IDENTITY, bias=bias[:, 8:9])
             if g == len(GROUPS) - 1:
-                nc.vector.tensor_scalar(y_sb[:, 1, :], y_ps[1][:, 0 : last - first], bo_sb[:, 1:2], None, ADD)
+                nc.vector.tensor_scalar(y_sb[:, 1, :], y_ps[1][:, 0 : last - first], bias[:, 9:10], None, ADD)
             else:
-                nc.scalar.activation(y_sb[:, 1, :], y_ps[1][:, 0 : last - first], IDENTITY, bias=bo_sb[:, 1:2])
+                nc.scalar.activation(y_sb[:, 1, :], y_ps[1][:, 0 : last - first], IDENTITY, bias=bias[:, 9:10])
             nc.sync.dma_start(out_by_half[:, :, first:last], y_sb[:])

@@ -21,8 +21,8 @@ ADD = mybir.AluOpType.add
 P = 128
 PASSES = K // 512
 HALF = 512
-CHUNKS = [(0, 128), (128, 256), (256, 512), (512, 768), (768, 896), (896, 1024)]
-GROUPS = [(0, 1, 2), (3,), (4,), (5,)]
+CHUNKS = [(0, 256), (256, 512), (512, 768), (768, 896), (896, 1024)]
+EVACS = [(256, 512), (512, 768), (768, 1024)]
 
 
 def tile_list_ad_feature_cross_kernel(
@@ -62,11 +62,10 @@ def tile_list_ad_feature_cross_kernel(
         bias_rows = sb("bias_rows", [P, P], F32)
         ident = sb("ident", [P, P], F32)
         bias = sb("bias", [P, 10], F32)
-        b_sb = sb("b_sb", [P, 4, S], F32)
 
-        nc.gpsimd.memset(tab_s[:, 0 : T // 2].bitcast(I32), 0)
-        nc.vector.memset(tab_s[:, T // 2 : T].bitcast(I32), 0)
-        nc.gpsimd.memset(wb_s_raw[:].rearrange("p a c -> p (a c)").bitcast(I32), 0)
+        nc.vector.memset(tab_s[:].bitcast(I32), 0)
+        nc.vector.memset(ident[:], 0.0)
+        nc.vector.memset(wb_s_raw[:].rearrange("p a c -> p (a c)").bitcast(I32), 0)
         nc.vector.memset(v_s1[96:128, :].bitcast(I32), 0)
         nc.vector.memset(wl_s[:].rearrange("p a c -> p (a c)").bitcast(I32), 0)
         nc.vector.memset(bias_rows[0:96, :], 0.0)
@@ -94,16 +93,16 @@ def tile_list_ad_feature_cross_kernel(
         load_table_words(0)
         load_scale_rows(wb_s_raw, wb_scales)
         load_table_words(1)
-        nc.sync.dma_start(
-            bias_rows[122:126, :].rearrange("t (q u) -> t q u", u=8), bb.rearrange("(q t u) -> t q u", t=4, u=8)
-        )
         load_wa(wa_raw0, 0)
 
+        nc.gpsimd.dma_start(
+            bias_rows[122:126, :].rearrange("t (q u) -> t q u", u=8), bb.rearrange("(q t u) -> t q u", t=4, u=8)
+        )
         nc.gpsimd.dma_start(
             bias_rows[118:122, :].rearrange("t (q u) -> t q u", u=8), ba.rearrange("(q t u) -> t q u", t=4, u=8)
         )
         nc.gpsimd.dma_start(bias_rows[126:128, :], bo.rearrange("(h p) -> h p", p=P))
-        make_identity(nc, ident[:])
+        make_identity(nc, ident[:], nomemset=True)
 
         nc.vector.tensor_copy(v_s[:], tab_s[:].indirect(offsets[:]))
         nc.scalar.dma_start(v_s1[0:112, :].bitcast(I32), v_s[4:116, :].bitcast(I32))
@@ -140,24 +139,32 @@ def tile_list_ad_feature_cross_kernel(
             h = lo // HALF
             return v_w[a][h][:, lo - HALF * h : hi - HALF * h].bitcast(FP8X4)
 
-        for h in range(2):
-            cols = slice(HALF * h, HALF * (h + 1))
-            for t in range(4):
-                b_ps = bank(4 * h + t, "b_ps%d%d" % (h, t))
-                for a in range(PASSES):
+        b_sb = [
+            sb("b_sb0", [P, 4, HALF], F32),
+            reuse.tile([P, 4, HALF], F32, name="b_sb1", align_bytes=64, offset=2048),
+        ]
+        b_ps = [[bank(4 * h + t, "b_ps%d%d" % (h, t)) for t in range(4)] for h in range(2)]
+        for a in range(PASSES):
+            for h in range(2):
+                for t in range(4):
                     nc.tensor.matmul_mx(
-                        out=b_ps[:],
+                        out=b_ps[h][t][:],
                         lhsT=wb_w[:, a, 256 * t : 256 * (t + 1)].bitcast(FP4X4),
                         lhsT_scale=wb_s[:, a, P * t : P * (t + 1)],
                         rhs=v_words(a, HALF * h, HALF * (h + 1)),
-                        rhs_scale=(v_s, v_s1)[a][:, cols],
+                        rhs_scale=(v_s, v_s1)[a][:, HALF * h : HALF * (h + 1)],
                         start=(a == 0),
                         stop=(a == PASSES - 1),
                     )
-                nc.scalar.activation(b_sb[:, t, cols], b_ps[:], IDENTITY, bias=bias[:, 4 + t : 5 + t])
 
-        def round_wa(a, t):
-            nc.vector.tensor_copy(
+        def empty_b(h):
+            for t in range(4):
+                nc.scalar.activation(b_sb[h][:, t, :], b_ps[h][t][:], IDENTITY, bias=bias[:, 4 + t : 5 + t])
+
+        empty_b(0)
+
+        def round_wa(a, t, copy):
+            copy(
                 wa_bf[a][:, t, :].rearrange("p (q g i j) -> p q g j i", g=2, i=4, j=4),
                 wa_raw[a][:].rearrange("p j (q t g i) -> p t q g j i", t=4, g=2, i=4)[:, t],
             )
@@ -166,60 +173,67 @@ def tile_list_ad_feature_cross_kernel(
             cols = slice(P * t, P * (t + 1))
             nc.vector.quantize_mx(out=wa_w[a][:, cols].bitcast(FP8X4), scales=wa_s[a][:, cols], in_=wa_bf[a][:, t, :])
 
-        steps = [(a, t) for a in range(PASSES) for t in range(4)]
-        for i, step in enumerate(steps):
-            round_wa(*step)
-            if i > 0:
-                quantise_wa(*steps[i - 1])
-        quantise_wa(*steps[-1])
-        nc.vector.tensor_copy(
-            wo_bf[:].rearrange("p (c i) t -> p c t i", i=4), wo_raw[:].rearrange("p t (c i) -> p c t i", i=4)
+        for t in range(4):
+            round_wa(0, t, nc.vector.tensor_copy)
+        nc.vector.quantize_mx(
+            out=wa_w[0][:].bitcast(FP8X4), scales=wa_s[0][:], in_=wa_bf[0][:].rearrange("p t c -> p (t c)")
         )
-        nc.vector.quantize_mx(out=wo_w[:].bitcast(FP8X4), scales=wo_s[:], in_=wo_bf[:].rearrange("p n t -> p (n t)"))
-
-        def pass_order(h):
-            return (0, 1) if h == 0 else (1, 0)
+        for t in range(4):
+            round_wa(1, t, nc.scalar.copy if t < 2 else nc.vector.tensor_copy)
+        for t in range(4):
+            quantise_wa(1, t)
+        empty_b(1)
 
         def v_plane(a, cols):
             return (v_s, v_s1)[a][:, cols]
 
-        a_sb = [sb("a_sb%d" % c, [P, 4, hi - lo], F32) for c, (lo, hi) in enumerate(CHUNKS)]
+        a_ps = [[bank(4 * h + t, "a_ps%d%d" % (h, t)) for t in range(4)] for h in range(2)]
+        for h in range(2):
+            for a in range(PASSES):
+                for t in range(4):
+                    nc.tensor.matmul_mx(
+                        out=a_ps[h][t][:],
+                        lhsT=wa_w[a][:, P * t : P * (t + 1)].bitcast(FP8X4),
+                        lhsT_scale=wa_s[a][:, P * t : P * (t + 1)],
+                        rhs=v_words(a, HALF * h, HALF * (h + 1)),
+                        rhs_scale=v_plane(a, slice(HALF * h, HALF * (h + 1))),
+                        start=(a == 0),
+                        stop=(a == PASSES - 1),
+                    )
+
         h_bf = [sb("h_bf%d" % c, [P, hi - lo, 4], BF16) for c, (lo, hi) in enumerate(CHUNKS)]
         h_w = [sb("h_w%d" % c, [P, hi - lo], U32) for c, (lo, hi) in enumerate(CHUNKS)]
         h_s = [sb("h_s%d" % c, [P, hi - lo], U8) for c, (lo, hi) in enumerate(CHUNKS)]
 
-        def a_half(h):
-            cols = slice(HALF * h, HALF * (h + 1))
-            a_ps = [bank(4 * h + t, "a_ps%d%d" % (h, t)) for t in range(4)]
+        first_hi = CHUNKS[0][1]
+        h_planes = sb("h_planes", [P, 4, first_hi], BF16)
+        for t in range(4):
+            nc.vector.scalar_tensor_tensor(
+                h_planes[:, t, :], a_ps[0][t][:, 0:first_hi], bias[:, t : t + 1], b_sb[0][:, t, 0:first_hi], ADD, MULT
+            )
+        a_sb = [sb("a_sb%d" % e, [P, 4, hi - lo], F32) for e, (lo, hi) in enumerate(EVACS)]
+        for e, (lo, hi) in enumerate(EVACS):
+            h = lo // HALF
             for t in range(4):
-                for i, a in enumerate(pass_order(h)):
-                    nc.tensor.matmul_mx(
-                        out=a_ps[t][:],
-                        lhsT=wa_w[a][:, P * t : P * (t + 1)].bitcast(FP8X4),
-                        lhsT_scale=wa_s[a][:, P * t : P * (t + 1)],
-                        rhs=v_words(a, HALF * h, HALF * (h + 1)),
-                        rhs_scale=v_plane(a, cols),
-                        start=(i == 0),
-                        stop=(i == PASSES - 1),
-                    )
-            for c, (lo, hi) in enumerate(CHUNKS):
-                if lo // HALF == h:
-                    for t in range(4):
-                        sums = a_ps[t][:, lo - HALF * h : hi - HALF * h]
-                        if c == 0:
-                            nc.vector.tensor_scalar(a_sb[c][:, t, :], sums, bias[:, t : t + 1], None, ADD)
-                        else:
-                            nc.scalar.activation(a_sb[c][:, t, :], sums, IDENTITY, bias=bias[:, t : t + 1])
-
-        a_half(0)
-        a_half(1)
+                nc.scalar.activation(
+                    a_sb[e][:, t, :], a_ps[h][t][:, lo - HALF * h : hi - HALF * h], IDENTITY, bias=bias[:, t : t + 1]
+                )
 
         def cross(c):
             lo, hi = CHUNKS[c]
+            if c == 0:
+                nc.vector.tensor_copy(
+                    h_bf[0][:].rearrange("p (c i) t -> p c t i", i=4),
+                    h_planes[:].rearrange("p t (c i) -> p c t i", i=4),
+                )
+                return
+            e = [x for x, (elo, ehi) in enumerate(EVACS) if elo <= lo < ehi][0]
+            elo = EVACS[e][0]
+            h = lo // HALF
             nc.vector.tensor_tensor(
                 h_bf[c][:].rearrange("p (c i) t -> p c t i", i=2),
-                a_sb[c][:].rearrange("p t (c i) -> p c t i", i=2),
-                b_sb[:, :, lo:hi].rearrange("p t (c i) -> p c t i", i=2),
+                a_sb[e][:, :, lo - elo : hi - elo].rearrange("p t (c i) -> p c t i", i=2),
+                b_sb[h][:, :, lo - HALF * h : hi - HALF * h].rearrange("p t (c i) -> p c t i", i=2),
                 MULT,
             )
 
@@ -228,45 +242,46 @@ def tile_list_ad_feature_cross_kernel(
                 out=h_w[c][:].bitcast(FP8X4), scales=h_s[c][:], in_=h_bf[c][:].rearrange("p s t -> p (s t)")
             )
 
-        for h in range(2):
-            chunks = [c for c, (lo, hi) in enumerate(CHUNKS) if lo // HALF == h]
-            for c in chunks:
-                cross(c)
-                if c > chunks[0]:
-                    quantise_h(c - 1)
-            quantise_h(chunks[-1])
+        cross(0)
+        nc.vector.tensor_copy(
+            wo_bf[:].rearrange("p (c i) t -> p c t i", i=4), wo_raw[:].rearrange("p t (c i) -> p c t i", i=4)
+        )
+        quantise_h(0)
+        nc.vector.quantize_mx(out=wo_w[:].bitcast(FP8X4), scales=wo_s[:], in_=wo_bf[:].rearrange("p n t -> p (n t)"))
+        for c in range(1, len(CHUNKS)):
+            cross(c)
+            if c > 1:
+                quantise_h(c - 1)
+        quantise_h(len(CHUNKS) - 1)
 
         out_by_half = out.rearrange("(h p) s -> p h s", p=P)
-        for g, chunks in enumerate(GROUPS):
-            first, last = CHUNKS[chunks[0]][0], CHUNKS[chunks[-1]][1]
-            y_ps = [bank(2 * g + n, "y_ps%d%d" % (g, n)) for n in range(2)]
-            for c in chunks:
-                lo, hi = CHUNKS[c]
-                for n in range(2):
-                    for a in range(PASSES):
-                        nc.tensor.matmul_mx(
-                            out=y_ps[n][:, lo - first : hi - first],
-                            lhsT=wl_w[:, a, P * n : P * (n + 1)].bitcast(FP8X4),
-                            lhsT_scale=wl_s[:, a, P * n : P * (n + 1)],
-                            rhs=v_words(a, lo, hi),
-                            rhs_scale=v_plane(a, slice(lo, hi)),
-                            start=(a == 0),
-                            stop=False,
-                        )
-                for n in range(2):
+        for c, (lo, hi) in enumerate(CHUNKS):
+            y_ps = [bank((2 * c + n) % 8, "y_ps%d%d" % (c, n)) for n in range(2)]
+            for n in range(2):
+                for a in range(PASSES):
                     nc.tensor.matmul_mx(
-                        out=y_ps[n][:, lo - first : hi - first],
-                        lhsT=wo_w[:, P * n : P * (n + 1)].bitcast(FP8X4),
-                        lhsT_scale=wo_s[:, P * n : P * (n + 1)],
-                        rhs=h_w[c][:].bitcast(FP8X4),
-                        rhs_scale=h_s[c][:],
-                        start=False,
-                        stop=True,
+                        out=y_ps[n][:, 0 : hi - lo],
+                        lhsT=wl_w[:, a, P * n : P * (n + 1)].bitcast(FP8X4),
+                        lhsT_scale=wl_s[:, a, P * n : P * (n + 1)],
+                        rhs=v_words(a, lo, hi),
+                        rhs_scale=v_plane(a, slice(lo, hi)),
+                        start=(a == 0),
+                        stop=False,
                     )
-            y_sb = sb("y_sb%d" % g, [P, 2, last - first], F32)
-            nc.scalar.activation(y_sb[:, 0, :], y_ps[0][:, 0 : last - first], IDENTITY, bias=bias[:, 8:9])
-            if g == len(GROUPS) - 1:
-                nc.vector.tensor_scalar(y_sb[:, 1, :], y_ps[1][:, 0 : last - first], bias[:, 9:10], None, ADD)
+            for n in range(2):
+                nc.tensor.matmul_mx(
+                    out=y_ps[n][:, 0 : hi - lo],
+                    lhsT=wo_w[:, P * n : P * (n + 1)].bitcast(FP8X4),
+                    lhsT_scale=wo_s[:, P * n : P * (n + 1)],
+                    rhs=h_w[c][:].bitcast(FP8X4),
+                    rhs_scale=h_s[c][:],
+                    start=False,
+                    stop=True,
+                )
+            y_sb = sb("y_sb%d" % c, [P, 2, hi - lo], F32)
+            nc.scalar.activation(y_sb[:, 0, :], y_ps[0][:, 0 : hi - lo], IDENTITY, bias=bias[:, 8:9])
+            if c == len(CHUNKS) - 1:
+                nc.vector.tensor_scalar(y_sb[:, 1, :], y_ps[1][:, 0 : hi - lo], bias[:, 9:10], None, ADD)
             else:
-                nc.scalar.activation(y_sb[:, 1, :], y_ps[1][:, 0 : last - first], IDENTITY, bias=bias[:, 9:10])
-            nc.sync.dma_start(out_by_half[:, :, first:last], y_sb[:])
+                nc.scalar.activation(y_sb[:, 1, :], y_ps[1][:, 0 : hi - lo], IDENTITY, bias=bias[:, 9:10])
+            nc.sync.dma_start(out_by_half[:, :, lo:hi], y_sb[:])

@@ -59,17 +59,20 @@ def tile_list_ad_feature_cross_kernel(
         wo_s = sb("wo_s", [P, N], U8)
         v_s = sb("v_s", [P, S], U8)
         v_s1 = sb("v_s1", [P, S], U8)
+        bb_rows = sb("bb_rows", [P, P], F32)
         bias_rows = sb("bias_rows", [P, P], F32)
+        bias_b = sb("bias_b", [P, 4], F32)
         ident = sb("ident", [P, P], F32)
-        bias = sb("bias", [P, 10], F32)
+        bias = sb("bias", [P, 6], F32)
 
         nc.vector.memset(tab_s[:].bitcast(I32), 0)
         nc.vector.memset(ident[:], 0.0)
         nc.vector.memset(wb_s_raw[:].rearrange("p a c -> p (a c)").bitcast(I32), 0)
         nc.vector.memset(v_s1[96:128, :].bitcast(I32), 0)
         nc.vector.memset(wl_s[:].rearrange("p a c -> p (a c)").bitcast(I32), 0)
-        nc.vector.memset(bias_rows[0:96, :], 0.0)
-        nc.vector.memset(bias_rows[96:118, :], 0.0)
+        nc.vector.memset(bb_rows[0:96, :], 0.0)
+        nc.vector.memset(bb_rows[96:124, :], 0.0)
+        nc.vector.memset(bias_rows[:], 0.0)
 
         def load_scale_rows(dst, src):
             for q in range(4):
@@ -84,28 +87,27 @@ def tile_list_ad_feature_cross_kernel(
         def load_wa(dst, a):
             nc.sync.dma_start(dst[:], wa[512 * a : 512 * (a + 1), :].rearrange("(p j) c -> p j c", j=4))
 
+        def load_bias_rows(dst, src):
+            nc.sync.dma_start(dst.rearrange("t (q u) -> t q u", u=8), src.rearrange("(q t u) -> t q u", t=4, u=8))
+
         nc.sync.dma_start(offsets[:], offs)
         nc.sync.dma_start(wb_raw[:].bitcast(I32), wb_words.rearrange("a p c -> p a c").bitcast(I32))
-        for q in range(4):
+        load_bias_rows(bb_rows[124:128, :], bb)
+        for r in range(4):
             nc.sync.dma_start(
-                tab_s[32 * q : 32 * q + 8, :].bitcast(I32), tab_scales[:, 4 * q : 4 * q + 4, :].bitcast(I32)
+                tab_s[r:P:16, :].bitcast(I32), tab_scales[:, r:16:4, :].rearrange("a q c -> q a c").bitcast(I32)
             )
         load_table_words(0)
         load_scale_rows(wb_s_raw, wb_scales)
         load_table_words(1)
         load_wa(wa_raw0, 0)
+        load_bias_rows(bias_rows[0:4, :], ba)
+        nc.sync.dma_start(bias_rows[4:6, :], bo.rearrange("(h p) -> h p", p=P))
 
-        nc.gpsimd.dma_start(
-            bias_rows[122:126, :].rearrange("t (q u) -> t q u", u=8), bb.rearrange("(q t u) -> t q u", t=4, u=8)
-        )
-        nc.gpsimd.dma_start(
-            bias_rows[118:122, :].rearrange("t (q u) -> t q u", u=8), ba.rearrange("(q t u) -> t q u", t=4, u=8)
-        )
-        nc.gpsimd.dma_start(bias_rows[126:128, :], bo.rearrange("(h p) -> h p", p=P))
         make_identity(nc, ident[:], nomemset=True)
 
         nc.vector.tensor_copy(v_s[:], tab_s[:].indirect(offsets[:]))
-        nc.scalar.dma_start(v_s1[0:112, :].bitcast(I32), v_s[4:116, :].bitcast(I32))
+        nc.scalar.dma_start(v_s1[0:112, :].bitcast(I32), v_s[16:128, :].bitcast(I32))
 
         def gather_words(a, h, dst):
             nc.vector.tensor_copy(dst[:], tab_w[a][:].indirect(offsets[:, 32 * h : 32 * (h + 1)]))
@@ -131,9 +133,9 @@ def tile_list_ad_feature_cross_kernel(
         nc.sync.dma_start(wl_w[:].bitcast(I32), wl_words.rearrange("a p c i -> p a (c i)").bitcast(I32))
         load_scale_rows(wl_s, wl_scales)
 
-        bias_ps = bank(7, "bias_ps")
-        nc.tensor.transpose(bias_ps[:, 0:P], bias_rows[:], ident[:])
-        nc.scalar.activation(bias[:], bias_ps[:, 118:128], IDENTITY)
+        bb_ps = bank(7, "bb_ps")
+        nc.tensor.transpose(bb_ps[:, 0:P], bb_rows[:], ident[:])
+        nc.scalar.activation(bias_b[:], bb_ps[:, 124:128], IDENTITY)
 
         def v_words(a, lo, hi):
             h = lo // HALF
@@ -159,9 +161,12 @@ def tile_list_ad_feature_cross_kernel(
 
         def empty_b(h):
             for t in range(4):
-                nc.scalar.activation(b_sb[h][:, t, :], b_ps[h][t][:], IDENTITY, bias=bias[:, 4 + t : 5 + t])
+                nc.scalar.activation(b_sb[h][:, t, :], b_ps[h][t][:], IDENTITY, bias=bias_b[:, t : t + 1])
 
         empty_b(0)
+        bias_ps = bank(0, "bias_ps")
+        nc.tensor.transpose(bias_ps[:, 0:P], bias_rows[:], ident[:])
+        nc.scalar.activation(bias[:], bias_ps[:, 0:6], IDENTITY)
 
         def round_wa(a, t, copy):
             copy(
@@ -279,9 +284,9 @@ def tile_list_ad_feature_cross_kernel(
                     stop=True,
                 )
             y_sb = sb("y_sb%d" % c, [P, 2, hi - lo], F32)
-            nc.scalar.activation(y_sb[:, 0, :], y_ps[0][:, 0 : hi - lo], IDENTITY, bias=bias[:, 8:9])
+            nc.scalar.activation(y_sb[:, 0, :], y_ps[0][:, 0 : hi - lo], IDENTITY, bias=bias[:, 4:5])
             if c == len(CHUNKS) - 1:
-                nc.vector.tensor_scalar(y_sb[:, 1, :], y_ps[1][:, 0 : hi - lo], bias[:, 9:10], None, ADD)
+                nc.vector.tensor_scalar(y_sb[:, 1, :], y_ps[1][:, 0 : hi - lo], bias[:, 5:6], None, ADD)
             else:
-                nc.scalar.activation(y_sb[:, 1, :], y_ps[1][:, 0 : hi - lo], IDENTITY, bias=bias[:, 9:10])
+                nc.scalar.activation(y_sb[:, 1, :], y_ps[1][:, 0 : hi - lo], IDENTITY, bias=bias[:, 5:6])
             nc.sync.dma_start(out_by_half[:, :, lo:hi], y_sb[:])

@@ -57,9 +57,10 @@ def tile_list_ad_feature_cross_kernel(
         wo_bf = sb("wo_bf", [P, N, 4], BF16)
         wo_w = sb("wo_w", [P, N], U32)
         wo_s = sb("wo_s", [P, N], U8)
-        v_s = sb("v_s", [P, S], U8)
-        v_s1 = sb("v_s1", [P, S], U8)
-        bb_rows = sb("bb_rows", [P, P], F32)
+        v_s = [sb("v_s%d" % h, [P, HALF], U8) for h in range(2)]
+        v_s1 = [sb("v_s1%d" % h, [P, HALF], U8) for h in range(2)]
+        bb_row = sb("bb_row", [P, R], F32)
+        bb_by_t = sb("bb_by_t", [P, 4, P], F32)
         bias_rows = sb("bias_rows", [P, P], F32)
         bias_b = sb("bias_b", [P, 4], F32)
         ident = sb("ident", [P, P], F32)
@@ -68,10 +69,11 @@ def tile_list_ad_feature_cross_kernel(
         nc.vector.memset(tab_s[:].bitcast(I32), 0)
         nc.vector.memset(ident[:], 0.0)
         nc.vector.memset(wb_s_raw[:].rearrange("p a c -> p (a c)").bitcast(I32), 0)
-        nc.vector.memset(v_s1[96:128, :].bitcast(I32), 0)
+        for h in range(2):
+            nc.vector.memset(v_s1[h][96:128, :].bitcast(I32), 0)
         nc.vector.memset(wl_s[:].rearrange("p a c -> p (a c)").bitcast(I32), 0)
-        nc.vector.memset(bb_rows[0:96, :], 0.0)
-        nc.vector.memset(bb_rows[96:124, :], 0.0)
+        nc.vector.memset(bb_row[0:96, :], 0.0)
+        nc.vector.memset(bb_row[96:127, :], 0.0)
         nc.vector.memset(bias_rows[:], 0.0)
 
         def load_scale_rows(dst, src):
@@ -92,7 +94,7 @@ def tile_list_ad_feature_cross_kernel(
 
         nc.sync.dma_start(offsets[:], offs)
         nc.sync.dma_start(wb_raw[:].bitcast(I32), wb_words.rearrange("a p c -> p a c").bitcast(I32))
-        load_bias_rows(bb_rows[124:128, :], bb)
+        nc.sync.dma_start(bb_row[127:128, :], bb.rearrange("(o r) -> o r", o=1))
         for r in range(4):
             nc.sync.dma_start(
                 tab_s[r:P:16, :].bitcast(I32), tab_scales[:, r:16:4, :].rearrange("a q c -> q a c").bitcast(I32)
@@ -100,14 +102,18 @@ def tile_list_ad_feature_cross_kernel(
         load_table_words(0)
         load_scale_rows(wb_s_raw, wb_scales)
         load_table_words(1)
+        for h in range(2):
+            nc.vector.tensor_copy(v_s[h][:], tab_s[:].indirect(offsets[:, 32 * h : 32 * (h + 1)]))
+
+        def shift_plane(h):
+            nc.sync.dma_start(v_s1[h][0:112, :].bitcast(I32), v_s[h][16:128, :].bitcast(I32))
+
+        shift_plane(0)
         load_wa(wa_raw0, 0)
-        load_bias_rows(bias_rows[0:4, :], ba)
-        nc.sync.dma_start(bias_rows[4:6, :], bo.rearrange("(h p) -> h p", p=P))
+        shift_plane(1)
 
         make_identity(nc, ident[:], nomemset=True)
 
-        nc.vector.tensor_copy(v_s[:], tab_s[:].indirect(offsets[:]))
-        nc.scalar.dma_start(v_s1[0:112, :].bitcast(I32), v_s[16:128, :].bitcast(I32))
 
         def gather_words(a, h, dst):
             nc.vector.tensor_copy(dst[:], tab_w[a][:].indirect(offsets[:, 32 * h : 32 * (h + 1)]))
@@ -127,6 +133,8 @@ def tile_list_ad_feature_cross_kernel(
 
         wa_raw = [wa_raw0, reuse.tile([P, 4, R], F32, name="wa_raw1", align_bytes=64, offset=2048)]
         load_wa(wa_raw[1], 1)
+        load_bias_rows(bias_rows[0:4, :], ba)
+        nc.sync.dma_start(bias_rows[4:6, :], bo.rearrange("(h p) -> h p", p=P))
         wo_by_t = wo.rearrange("(q t u) n -> t q u n", t=4, u=8)
         for t in range(4):
             nc.sync.dma_start(wo_raw[:, t, :], wo_by_t[t])
@@ -134,29 +142,37 @@ def tile_list_ad_feature_cross_kernel(
         load_scale_rows(wl_s, wl_scales)
 
         bb_ps = bank(7, "bb_ps")
-        nc.tensor.transpose(bb_ps[:, 0:P], bb_rows[:], ident[:])
-        nc.scalar.activation(bias_b[:], bb_ps[:, 124:128], IDENTITY)
+        nc.scalar.copy(
+            bb_by_t[:].rearrange("k t (z u) -> k t z u", u=8), bb_row[:].rearrange("k (z t u) -> k t z u", t=4, u=8)
+        )
+        for t in range(4):
+            nc.tensor.transpose(bb_ps[:, P * t : P * (t + 1)], bb_by_t[:, t, :], ident[:])
+        nc.scalar.activation(bias_b[:], bb_ps[:, P - 1 : 4 * P : P], IDENTITY)
 
         def v_words(a, lo, hi):
             h = lo // HALF
             return v_w[a][h][:, lo - HALF * h : hi - HALF * h].bitcast(FP8X4)
+
+        def v_plane(a, lo, hi):
+            h = lo // HALF
+            return (v_s, v_s1)[a][h][:, lo - HALF * h : hi - HALF * h]
 
         b_sb = [
             sb("b_sb0", [P, 4, HALF], F32),
             reuse.tile([P, 4, HALF], F32, name="b_sb1", align_bytes=64, offset=2048),
         ]
         b_ps = [[bank(4 * h + t, "b_ps%d%d" % (h, t)) for t in range(4)] for h in range(2)]
-        for a in range(PASSES):
-            for h in range(2):
+        for h in range(2):
+            for i, a in enumerate((0, 1) if h == 0 else (1, 0)):
                 for t in range(4):
                     nc.tensor.matmul_mx(
                         out=b_ps[h][t][:],
                         lhsT=wb_w[:, a, 256 * t : 256 * (t + 1)].bitcast(FP4X4),
                         lhsT_scale=wb_s[:, a, P * t : P * (t + 1)],
                         rhs=v_words(a, HALF * h, HALF * (h + 1)),
-                        rhs_scale=(v_s, v_s1)[a][:, HALF * h : HALF * (h + 1)],
-                        start=(a == 0),
-                        stop=(a == PASSES - 1),
+                        rhs_scale=v_plane(a, HALF * h, HALF * (h + 1)),
+                        start=(i == 0),
+                        stop=(i == PASSES - 1),
                     )
 
         def empty_b(h):
@@ -189,9 +205,6 @@ def tile_list_ad_feature_cross_kernel(
             quantise_wa(1, t)
         empty_b(1)
 
-        def v_plane(a, cols):
-            return (v_s, v_s1)[a][:, cols]
-
         a_ps = [[bank(4 * h + t, "a_ps%d%d" % (h, t)) for t in range(4)] for h in range(2)]
         for h in range(2):
             for a in range(PASSES):
@@ -201,7 +214,7 @@ def tile_list_ad_feature_cross_kernel(
                         lhsT=wa_w[a][:, P * t : P * (t + 1)].bitcast(FP8X4),
                         lhsT_scale=wa_s[a][:, P * t : P * (t + 1)],
                         rhs=v_words(a, HALF * h, HALF * (h + 1)),
-                        rhs_scale=v_plane(a, slice(HALF * h, HALF * (h + 1))),
+                        rhs_scale=v_plane(a, HALF * h, HALF * (h + 1)),
                         start=(a == 0),
                         stop=(a == PASSES - 1),
                     )
@@ -269,7 +282,7 @@ def tile_list_ad_feature_cross_kernel(
                         lhsT=wl_w[:, a, P * n : P * (n + 1)].bitcast(FP8X4),
                         lhsT_scale=wl_s[:, a, P * n : P * (n + 1)],
                         rhs=v_words(a, lo, hi),
-                        rhs_scale=v_plane(a, slice(lo, hi)),
+                        rhs_scale=v_plane(a, lo, hi),
                         start=(a == 0),
                         stop=False,
                     )

@@ -61,10 +61,9 @@ def tile_list_ad_feature_cross_kernel(
         v_s1 = [sb("v_s1%d" % h, [P, HALF], U8) for h in range(2)]
         bb_row = sb("bb_row", [P, R], F32)
         bb_by_t = sb("bb_by_t", [P, 4, P], F32)
-        bias_rows = sb("bias_rows", [P, P], F32)
-        bias_b = sb("bias_b", [P, 4], F32)
         ident = sb("ident", [P, P], F32)
-        bias = sb("bias", [P, 6], F32)
+        bias = sb("bias", [P, 4, 2], F32)
+        bias_o = sb("bias_o", [P, 2], F32)
 
         nc.vector.memset(tab_s[:].bitcast(I32), 0)
         nc.vector.memset(ident[:], 0.0)
@@ -73,8 +72,7 @@ def tile_list_ad_feature_cross_kernel(
             nc.vector.memset(v_s1[h][96:128, :].bitcast(I32), 0)
         nc.vector.memset(wl_s[:].rearrange("p a c -> p (a c)").bitcast(I32), 0)
         nc.vector.memset(bb_row[0:96, :], 0.0)
-        nc.vector.memset(bb_row[96:127, :], 0.0)
-        nc.vector.memset(bias_rows[:], 0.0)
+        nc.vector.memset(bb_row[96:126, :], 0.0)
 
         def load_scale_rows(dst, src):
             for q in range(4):
@@ -89,19 +87,17 @@ def tile_list_ad_feature_cross_kernel(
         def load_wa(dst, a):
             nc.sync.dma_start(dst[:], wa[512 * a : 512 * (a + 1), :].rearrange("(p j) c -> p j c", j=4))
 
-        def load_bias_rows(dst, src):
-            nc.sync.dma_start(dst.rearrange("t (q u) -> t q u", u=8), src.rearrange("(q t u) -> t q u", t=4, u=8))
-
         nc.sync.dma_start(offsets[:], offs)
         nc.sync.dma_start(wb_raw[:].bitcast(I32), wb_words.rearrange("a p c -> p a c").bitcast(I32))
-        nc.sync.dma_start(bb_row[127:128, :], bb.rearrange("(o r) -> o r", o=1))
         for r in range(4):
             nc.sync.dma_start(
                 tab_s[r:P:16, :].bitcast(I32), tab_scales[:, r:16:4, :].rearrange("a q c -> q a c").bitcast(I32)
             )
         load_table_words(0)
-        load_scale_rows(wb_s_raw, wb_scales)
+        nc.sync.dma_start(bb_row[127:128, :], bb.rearrange("(o r) -> o r", o=1))
+        nc.sync.dma_start(bb_row[126:127, :], ba.rearrange("(o r) -> o r", o=1))
         load_table_words(1)
+        load_scale_rows(wb_s_raw, wb_scales)
         for h in range(2):
             nc.vector.tensor_copy(v_s[h][:], tab_s[:].indirect(offsets[:, 32 * h : 32 * (h + 1)]))
 
@@ -113,6 +109,8 @@ def tile_list_ad_feature_cross_kernel(
         shift_plane(1)
 
         make_identity(nc, ident[:], nomemset=True)
+        table_warm = sb("table_warm", [P, 1], F32)
+        nc.scalar.activation(table_warm[:], ident[:, 0:1], IDENTITY)
 
 
         def gather_words(a, h, dst):
@@ -123,23 +121,23 @@ def tile_list_ad_feature_cross_kernel(
             wb_w[:].bitcast(I32).rearrange("p a (t q w) -> p a t q w", t=4, w=4),
             wb_raw[:].bitcast(I32).rearrange("p a (q t w) -> p a t q w", t=4, w=4),
         )
-        v_w00 = gather_words(0, 0, sb("v_w00", [P, HALF], U32))
+        v_w0 = [gather_words(0, h, sb("v_w0%d" % h, [P, HALF], U32)) for h in range(2)]
         nc.vector.tensor_copy(
             wb_s[:].bitcast(I32).rearrange("p a (t q w) -> p a t q w", t=4, w=2),
             wb_s_raw[:].bitcast(I32).rearrange("p a (q t w) -> p a t q w", t=4, w=2),
         )
-        v_w01 = gather_words(0, 1, reuse.tile([P, HALF], U32, name="v_w01", align_bytes=64, offset=0))
-        v_w = [[v_w00, v_w01], [gather_words(1, h, sb("v_w1%d" % h, [P, HALF], U32)) for h in range(2)]]
+        v_w10 = gather_words(1, 0, reuse.tile([P, HALF], U32, name="v_w10", align_bytes=64, offset=0))
+        v_w = [v_w0, [v_w10, gather_words(1, 1, reuse.tile([P, HALF], U32, name="v_w11", align_bytes=64, offset=2048))]]
 
-        wa_raw = [wa_raw0, reuse.tile([P, 4, R], F32, name="wa_raw1", align_bytes=64, offset=2048)]
+        wa_raw = [wa_raw0, reuse.tile([P, 4, R], F32, name="wa_raw1", align_bytes=64, offset=4096)]
         load_wa(wa_raw[1], 1)
-        load_bias_rows(bias_rows[0:4, :], ba)
-        nc.sync.dma_start(bias_rows[4:6, :], bo.rearrange("(h p) -> h p", p=P))
         wo_by_t = wo.rearrange("(q t u) n -> t q u n", t=4, u=8)
         for t in range(4):
             nc.sync.dma_start(wo_raw[:, t, :], wo_by_t[t])
         nc.sync.dma_start(wl_w[:].bitcast(I32), wl_words.rearrange("a p c i -> p a (c i)").bitcast(I32))
         load_scale_rows(wl_s, wl_scales)
+        with nc.allow_non_contiguous_dma(reason="one value of bo a partition and half"):
+            nc.sync.dma_start(bias_o[:], bo.rearrange("(h p) -> p h", p=P))
 
         bb_ps = bank(7, "bb_ps")
         nc.scalar.copy(
@@ -147,7 +145,7 @@ def tile_list_ad_feature_cross_kernel(
         )
         for t in range(4):
             nc.tensor.transpose(bb_ps[:, P * t : P * (t + 1)], bb_by_t[:, t, :], ident[:])
-        nc.scalar.activation(bias_b[:], bb_ps[:, P - 1 : 4 * P : P], IDENTITY)
+        nc.scalar.activation(bias[:], bb_ps[:].rearrange("p (t k) -> p t k", t=4)[:, :, P - 2 : P], IDENTITY)
 
         def v_words(a, lo, hi):
             h = lo // HALF
@@ -159,8 +157,19 @@ def tile_list_ad_feature_cross_kernel(
 
         b_sb = [
             sb("b_sb0", [P, 4, HALF], F32),
-            reuse.tile([P, 4, HALF], F32, name="b_sb1", align_bytes=64, offset=2048),
+            reuse.tile([P, 4, HALF], F32, name="b_sb1", align_bytes=64, offset=4096),
         ]
+        warm_ps = bank(4, "warm_ps")
+        for i in range(3):
+            nc.tensor.matmul_mx(
+                out=warm_ps[:],
+                lhsT=wb_w[:, 0, 0:256].bitcast(FP4X4),
+                lhsT_scale=v_s[0][:, 0:P],
+                rhs=v_w0[0][:].bitcast(FP8X4),
+                rhs_scale=v_s[0][:],
+                start=True,
+                stop=True,
+            )
         b_ps = [[bank(4 * h + t, "b_ps%d%d" % (h, t)) for t in range(4)] for h in range(2)]
         for h in range(2):
             for i, a in enumerate((0, 1) if h == 0 else (1, 0)):
@@ -177,12 +186,9 @@ def tile_list_ad_feature_cross_kernel(
 
         def empty_b(h):
             for t in range(4):
-                nc.scalar.activation(b_sb[h][:, t, :], b_ps[h][t][:], IDENTITY, bias=bias_b[:, t : t + 1])
+                nc.scalar.activation(b_sb[h][:, t, :], b_ps[h][t][:], IDENTITY, bias=bias[:, t, 1:2])
 
         empty_b(0)
-        bias_ps = bank(0, "bias_ps")
-        nc.tensor.transpose(bias_ps[:, 0:P], bias_rows[:], ident[:])
-        nc.scalar.activation(bias[:], bias_ps[:, 0:6], IDENTITY)
 
         def round_wa(a, t, copy):
             copy(
@@ -227,14 +233,14 @@ def tile_list_ad_feature_cross_kernel(
         h_planes = sb("h_planes", [P, 4, first_hi], BF16)
         for t in range(4):
             nc.vector.scalar_tensor_tensor(
-                h_planes[:, t, :], a_ps[0][t][:, 0:first_hi], bias[:, t : t + 1], b_sb[0][:, t, 0:first_hi], ADD, MULT
+                h_planes[:, t, :], a_ps[0][t][:, 0:first_hi], bias[:, t, 0:1], b_sb[0][:, t, 0:first_hi], ADD, MULT
             )
         a_sb = [sb("a_sb%d" % e, [P, 4, hi - lo], F32) for e, (lo, hi) in enumerate(EVACS)]
         for e, (lo, hi) in enumerate(EVACS):
             h = lo // HALF
             for t in range(4):
                 nc.scalar.activation(
-                    a_sb[e][:, t, :], a_ps[h][t][:, lo - HALF * h : hi - HALF * h], IDENTITY, bias=bias[:, t : t + 1]
+                    a_sb[e][:, t, :], a_ps[h][t][:, lo - HALF * h : hi - HALF * h], IDENTITY, bias=bias[:, t, 0:1]
                 )
 
         def cross(c):
@@ -297,9 +303,9 @@ def tile_list_ad_feature_cross_kernel(
                     stop=True,
                 )
             y_sb = sb("y_sb%d" % c, [P, 2, hi - lo], F32)
-            nc.scalar.activation(y_sb[:, 0, :], y_ps[0][:, 0 : hi - lo], IDENTITY, bias=bias[:, 4:5])
+            nc.scalar.activation(y_sb[:, 0, :], y_ps[0][:, 0 : hi - lo], IDENTITY, bias=bias_o[:, 0:1])
             if c == len(CHUNKS) - 1:
-                nc.vector.tensor_scalar(y_sb[:, 1, :], y_ps[1][:, 0 : hi - lo], bias[:, 5:6], None, ADD)
+                nc.vector.tensor_scalar(y_sb[:, 1, :], y_ps[1][:, 0 : hi - lo], bias_o[:, 1:2], None, ADD)
             else:
-                nc.scalar.activation(y_sb[:, 1, :], y_ps[1][:, 0 : hi - lo], IDENTITY, bias=bias[:, 5:6])
+                nc.scalar.activation(y_sb[:, 1, :], y_ps[1][:, 0 : hi - lo], IDENTITY, bias=bias_o[:, 1:2])
             nc.sync.dma_start(out_by_half[:, :, lo:hi], y_sb[:])

@@ -62,7 +62,8 @@ def tile_list_ad_feature_cross_kernel(
         bb_row = sb("bb_row", [P, R], F32)
         bb_by_t = sb("bb_by_t", [P, 4, P], F32)
         ident = sb("ident", [P, P], F32)
-        bias = sb("bias", [P, 4, 2], F32)
+        bias_a = sb("bias_a", [P, 4], F32)
+        bias_b = sb("bias_b", [P, 4], F32)
         bias_o = sb("bias_o", [P, 2], F32)
 
         nc.vector.memset(tab_s[:].bitcast(I32), 0)
@@ -72,7 +73,7 @@ def tile_list_ad_feature_cross_kernel(
             nc.vector.memset(v_s1[h][96:128, :].bitcast(I32), 0)
         nc.vector.memset(wl_s[:].rearrange("p a c -> p (a c)").bitcast(I32), 0)
         nc.vector.memset(bb_row[0:96, :], 0.0)
-        nc.vector.memset(bb_row[96:126, :], 0.0)
+        nc.vector.memset(bb_row[96:127, :], 0.0)
 
         def load_scale_rows(dst, src):
             for q in range(4):
@@ -87,6 +88,21 @@ def tile_list_ad_feature_cross_kernel(
         def load_wa(dst, a):
             nc.sync.dma_start(dst[:], wa[512 * a : 512 * (a + 1), :].rearrange("(p j) c -> p j c", j=4))
 
+        def turn_bias(dst, row, name):
+            nc.scalar.copy(
+                bb_by_t[:].rearrange("k t (z u) -> k t z u", u=8), bb_row[:].rearrange("k (z t u) -> k t z u", t=4, u=8)
+            )
+            turned = bank(7, name)
+            for t in range(4):
+                nc.tensor.transpose(turned[:, P * t : P * (t + 1)], bb_by_t[:, t, :], ident[:])
+            nc.scalar.activation(dst[:], turned[:, row : 4 * P : P], IDENTITY)
+
+        make_identity(nc, ident[:], nomemset=True)
+        table_warm = sb("table_warm", [P, 1], F32)
+        nc.scalar.dma_start(bb_row[127:128, :], bb.rearrange("(o r) -> o r", o=1))
+        nc.scalar.activation(table_warm[:], ident[:, 0:1], IDENTITY)
+        turn_bias(bias_b, 127, "bb_ps")
+
         nc.sync.dma_start(offsets[:], offs)
         nc.sync.dma_start(wb_raw[:].bitcast(I32), wb_words.rearrange("a p c -> p a c").bitcast(I32))
         for r in range(4):
@@ -94,10 +110,10 @@ def tile_list_ad_feature_cross_kernel(
                 tab_s[r:P:16, :].bitcast(I32), tab_scales[:, r:16:4, :].rearrange("a q c -> q a c").bitcast(I32)
             )
         load_table_words(0)
-        nc.sync.dma_start(bb_row[127:128, :], bb.rearrange("(o r) -> o r", o=1))
-        nc.sync.dma_start(bb_row[126:127, :], ba.rearrange("(o r) -> o r", o=1))
-        load_table_words(1)
         load_scale_rows(wb_s_raw, wb_scales)
+        load_table_words(1)
+        nc.sync.dma_start(bb_row[126:127, :], ba.rearrange("(o r) -> o r", o=1))
+        turn_bias(bias_a, 126, "ba_ps")
         for h in range(2):
             nc.vector.tensor_copy(v_s[h][:], tab_s[:].indirect(offsets[:, 32 * h : 32 * (h + 1)]))
 
@@ -108,10 +124,6 @@ def tile_list_ad_feature_cross_kernel(
         load_wa(wa_raw0, 0)
         shift_plane(1)
 
-        make_identity(nc, ident[:], nomemset=True)
-        table_warm = sb("table_warm", [P, 1], F32)
-        nc.scalar.activation(table_warm[:], ident[:, 0:1], IDENTITY)
-
 
         def gather_words(a, h, dst):
             nc.vector.tensor_copy(dst[:], tab_w[a][:].indirect(offsets[:, 32 * h : 32 * (h + 1)]))
@@ -121,13 +133,13 @@ def tile_list_ad_feature_cross_kernel(
             wb_w[:].bitcast(I32).rearrange("p a (t q w) -> p a t q w", t=4, w=4),
             wb_raw[:].bitcast(I32).rearrange("p a (q t w) -> p a t q w", t=4, w=4),
         )
-        v_w0 = [gather_words(0, h, sb("v_w0%d" % h, [P, HALF], U32)) for h in range(2)]
+        v_w00 = gather_words(0, 0, sb("v_w00", [P, HALF], U32))
         nc.vector.tensor_copy(
             wb_s[:].bitcast(I32).rearrange("p a (t q w) -> p a t q w", t=4, w=2),
             wb_s_raw[:].bitcast(I32).rearrange("p a (q t w) -> p a t q w", t=4, w=2),
         )
-        v_w10 = gather_words(1, 0, reuse.tile([P, HALF], U32, name="v_w10", align_bytes=64, offset=0))
-        v_w = [v_w0, [v_w10, gather_words(1, 1, reuse.tile([P, HALF], U32, name="v_w11", align_bytes=64, offset=2048))]]
+        v_w01 = gather_words(0, 1, reuse.tile([P, HALF], U32, name="v_w01", align_bytes=64, offset=0))
+        v_w = [[v_w00, v_w01], [gather_words(1, h, sb("v_w1%d" % h, [P, HALF], U32)) for h in range(2)]]
 
         wa_raw = [wa_raw0, reuse.tile([P, 4, R], F32, name="wa_raw1", align_bytes=64, offset=4096)]
         load_wa(wa_raw[1], 1)
@@ -138,14 +150,6 @@ def tile_list_ad_feature_cross_kernel(
         load_scale_rows(wl_s, wl_scales)
         with nc.allow_non_contiguous_dma(reason="one value of bo a partition and half"):
             nc.sync.dma_start(bias_o[:], bo.rearrange("(h p) -> p h", p=P))
-
-        bb_ps = bank(7, "bb_ps")
-        nc.scalar.copy(
-            bb_by_t[:].rearrange("k t (z u) -> k t z u", u=8), bb_row[:].rearrange("k (z t u) -> k t z u", t=4, u=8)
-        )
-        for t in range(4):
-            nc.tensor.transpose(bb_ps[:, P * t : P * (t + 1)], bb_by_t[:, t, :], ident[:])
-        nc.scalar.activation(bias[:], bb_ps[:].rearrange("p (t k) -> p t k", t=4)[:, :, P - 2 : P], IDENTITY)
 
         def v_words(a, lo, hi):
             h = lo // HALF
@@ -159,17 +163,6 @@ def tile_list_ad_feature_cross_kernel(
             sb("b_sb0", [P, 4, HALF], F32),
             reuse.tile([P, 4, HALF], F32, name="b_sb1", align_bytes=64, offset=4096),
         ]
-        warm_ps = bank(4, "warm_ps")
-        for i in range(3):
-            nc.tensor.matmul_mx(
-                out=warm_ps[:],
-                lhsT=wb_w[:, 0, 0:256].bitcast(FP4X4),
-                lhsT_scale=v_s[0][:, 0:P],
-                rhs=v_w0[0][:].bitcast(FP8X4),
-                rhs_scale=v_s[0][:],
-                start=True,
-                stop=True,
-            )
         b_ps = [[bank(4 * h + t, "b_ps%d%d" % (h, t)) for t in range(4)] for h in range(2)]
         for h in range(2):
             for i, a in enumerate((0, 1) if h == 0 else (1, 0)):
@@ -186,7 +179,7 @@ def tile_list_ad_feature_cross_kernel(
 
         def empty_b(h):
             for t in range(4):
-                nc.scalar.activation(b_sb[h][:, t, :], b_ps[h][t][:], IDENTITY, bias=bias[:, t, 1:2])
+                nc.scalar.activation(b_sb[h][:, t, :], b_ps[h][t][:], IDENTITY, bias=bias_b[:, t : t + 1])
 
         empty_b(0)
 
@@ -233,14 +226,14 @@ def tile_list_ad_feature_cross_kernel(
         h_planes = sb("h_planes", [P, 4, first_hi], BF16)
         for t in range(4):
             nc.vector.scalar_tensor_tensor(
-                h_planes[:, t, :], a_ps[0][t][:, 0:first_hi], bias[:, t, 0:1], b_sb[0][:, t, 0:first_hi], ADD, MULT
+                h_planes[:, t, :], a_ps[0][t][:, 0:first_hi], bias_a[:, t : t + 1], b_sb[0][:, t, 0:first_hi], ADD, MULT
             )
         a_sb = [sb("a_sb%d" % e, [P, 4, hi - lo], F32) for e, (lo, hi) in enumerate(EVACS)]
         for e, (lo, hi) in enumerate(EVACS):
             h = lo // HALF
             for t in range(4):
                 nc.scalar.activation(
-                    a_sb[e][:, t, :], a_ps[h][t][:, lo - HALF * h : hi - HALF * h], IDENTITY, bias=bias[:, t, 0:1]
+                    a_sb[e][:, t, :], a_ps[h][t][:, lo - HALF * h : hi - HALF * h], IDENTITY, bias=bias_a[:, t : t + 1]
                 )
 
         def cross(c):

@@ -35,7 +35,7 @@ def tile_list_ad_feature_cross_kernel(
         psum = ctx.enter_context(tc.psum_pool(name="psum", bufs=1))
 
         def sb(name, shape, dtype):
-            return keep.tile(shape, dtype, name=name, align_bytes=64)
+            return keep.tile(shape, dtype, name=name, align_bytes=256)
 
         def bank(index, name):
             return psum.tile([P, HALF], F32, name=name, tag="bank%d" % index)
@@ -44,7 +44,7 @@ def tile_list_ad_feature_cross_kernel(
         tab_s = sb("tab_s", [P, T], U8)
         tab_w = [sb("tab_w%d" % a, [P, T], U32) for a in range(PASSES)]
         wb_raw = sb("wb_raw", [P, PASSES, 2 * R], U8)
-        wb_s_raw = reuse.tile([P, PASSES, R], U8, name="wb_s_raw", align_bytes=64, offset=1536)
+        wb_s_raw = reuse.tile([P, PASSES, R], U8, name="wb_s_raw", align_bytes=256, offset=1536)
         wb_w = sb("wb_w", [P, PASSES, 2 * R], U8)
         wb_s = sb("wb_s", [P, PASSES, R], U8)
         wl_w = sb("wl_w", [P, PASSES, N], U32)
@@ -98,9 +98,7 @@ def tile_list_ad_feature_cross_kernel(
             nc.scalar.activation(dst[:], turned[:, row : 4 * P : P], IDENTITY)
 
         make_identity(nc, ident[:], nomemset=True)
-        table_warm = sb("table_warm", [P, 1], F32)
         nc.scalar.dma_start(bb_row[127:128, :], bb.rearrange("(o r) -> o r", o=1))
-        nc.scalar.activation(table_warm[:], ident[:, 0:1], IDENTITY)
         turn_bias(bias_b, 127, "bb_ps")
 
         nc.sync.dma_start(offsets[:], offs)
@@ -138,10 +136,10 @@ def tile_list_ad_feature_cross_kernel(
             wb_s[:].bitcast(I32).rearrange("p a (t q w) -> p a t q w", t=4, w=2),
             wb_s_raw[:].bitcast(I32).rearrange("p a (q t w) -> p a t q w", t=4, w=2),
         )
-        v_w01 = gather_words(0, 1, reuse.tile([P, HALF], U32, name="v_w01", align_bytes=64, offset=0))
+        v_w01 = gather_words(0, 1, reuse.tile([P, HALF], U32, name="v_w01", align_bytes=256, offset=0))
         v_w = [[v_w00, v_w01], [gather_words(1, h, sb("v_w1%d" % h, [P, HALF], U32)) for h in range(2)]]
 
-        wa_raw = [wa_raw0, reuse.tile([P, 4, R], F32, name="wa_raw1", align_bytes=64, offset=4096)]
+        wa_raw = [wa_raw0, reuse.tile([P, 4, R], F32, name="wa_raw1", align_bytes=256, offset=4096)]
         load_wa(wa_raw[1], 1)
         wo_by_t = wo.rearrange("(q t u) n -> t q u n", t=4, u=8)
         for t in range(4):
@@ -161,7 +159,7 @@ def tile_list_ad_feature_cross_kernel(
 
         b_sb = [
             sb("b_sb0", [P, 4, HALF], F32),
-            reuse.tile([P, 4, HALF], F32, name="b_sb1", align_bytes=64, offset=4096),
+            reuse.tile([P, 4, HALF], F32, name="b_sb1", align_bytes=256, offset=4096),
         ]
         b_ps = [[bank(4 * h + t, "b_ps%d%d" % (h, t)) for t in range(4)] for h in range(2)]
         for h in range(2):

@@ -159,7 +159,7 @@ def tile_list_ad_feature_cross_kernel(
 
         b_sb = [
             sb("b_sb0", [P, 4, HALF], F32),
-            reuse.tile([P, 4, HALF], F32, name="b_sb1", align_bytes=256, offset=4096),
+            sb("b_sb1", [P, 4, HALF], F32),
         ]
         b_ps = [[bank(4 * h + t, "b_ps%d%d" % (h, t)) for t in range(4)] for h in range(2)]
         for h in range(2):
@@ -180,6 +180,7 @@ def tile_list_ad_feature_cross_kernel(
                 nc.scalar.activation(b_sb[h][:, t, :], b_ps[h][t][:], IDENTITY, bias=bias_b[:, t : t + 1])
 
         empty_b(0)
+        empty_b(1)
 
         def round_wa(a, t, copy):
             copy(
@@ -197,10 +198,10 @@ def tile_list_ad_feature_cross_kernel(
             out=wa_w[0][:].bitcast(FP8X4), scales=wa_s[0][:], in_=wa_bf[0][:].rearrange("p t c -> p (t c)")
         )
         for t in range(4):
-            round_wa(1, t, nc.scalar.copy if t < 2 else nc.vector.tensor_copy)
-        for t in range(4):
-            quantise_wa(1, t)
-        empty_b(1)
+            round_wa(1, t, nc.vector.tensor_copy)
+            if t > 0:
+                quantise_wa(1, t - 1)
+        quantise_wa(1, 3)
 
         a_ps = [[bank(4 * h + t, "a_ps%d%d" % (h, t)) for t in range(4)] for h in range(2)]
         for h in range(2):
@@ -233,6 +234,10 @@ def tile_list_ad_feature_cross_kernel(
                 nc.scalar.activation(
                     a_sb[e][:, t, :], a_ps[h][t][:, lo - HALF * h : hi - HALF * h], IDENTITY, bias=bias_a[:, t : t + 1]
                 )
+            if e == 0:
+                nc.scalar.copy(
+                    wo_bf[:].rearrange("p (c i) t -> p c t i", i=4), wo_raw[:].rearrange("p t (c i) -> p c t i", i=4)
+                )
 
         def cross(c):
             lo, hi = CHUNKS[c]
@@ -258,15 +263,13 @@ def tile_list_ad_feature_cross_kernel(
             )
 
         cross(0)
-        nc.vector.tensor_copy(
-            wo_bf[:].rearrange("p (c i) t -> p c t i", i=4), wo_raw[:].rearrange("p t (c i) -> p c t i", i=4)
-        )
-        quantise_h(0)
-        nc.vector.quantize_mx(out=wo_w[:].bitcast(FP8X4), scales=wo_s[:], in_=wo_bf[:].rearrange("p n t -> p (n t)"))
         for c in range(1, len(CHUNKS)):
             cross(c)
-            if c > 1:
-                quantise_h(c - 1)
+            quantise_h(c - 1)
+            if c == 1:
+                nc.vector.quantize_mx(
+                    out=wo_w[:].bitcast(FP8X4), scales=wo_s[:], in_=wo_bf[:].rearrange("p n t -> p (n t)")
+                )
         quantise_h(len(CHUNKS) - 1)
 
         out_by_half = out.rearrange("(h p) s -> p h s", p=P)

@@ -57,23 +57,20 @@ def tile_list_ad_feature_cross_kernel(
         wo_bf = sb("wo_bf", [P, N, 4], BF16)
         wo_w = sb("wo_w", [P, N], U32)
         wo_s = sb("wo_s", [P, N], U8)
-        v_s = [sb("v_s%d" % h, [P, HALF], U8) for h in range(2)]
-        v_s1 = [sb("v_s1%d" % h, [P, HALF], U8) for h in range(2)]
+        v_s = [sb("v_s%d" % a, [P, S], U8) for a in range(PASSES)]
         bb_row = sb("bb_row", [P, R], F32)
         bb_by_t = sb("bb_by_t", [P, 4, P], F32)
         ident = sb("ident", [P, P], F32)
-        bias_a = sb("bias_a", [P, 4], F32)
-        bias_b = sb("bias_b", [P, 4], F32)
+        bias_ab = sb("bias_ab", [P, 4, 2], F32)
         bias_o = sb("bias_o", [P, 2], F32)
 
         nc.vector.memset(tab_s[:].bitcast(I32), 0)
         nc.vector.memset(ident[:], 0.0)
         nc.vector.memset(wb_s_raw[:].rearrange("p a c -> p (a c)").bitcast(I32), 0)
-        for h in range(2):
-            nc.vector.memset(v_s1[h][96:128, :].bitcast(I32), 0)
+        nc.vector.memset(v_s[1][96:128, :].bitcast(I32), 0)
         nc.vector.memset(wl_s[:].rearrange("p a c -> p (a c)").bitcast(I32), 0)
         nc.vector.memset(bb_row[0:96, :], 0.0)
-        nc.vector.memset(bb_row[96:127, :], 0.0)
+        nc.vector.memset(bb_row[96:126, :], 0.0)
 
         def load_scale_rows(dst, src):
             for q in range(4):
@@ -88,18 +85,16 @@ def tile_list_ad_feature_cross_kernel(
         def load_wa(dst, a):
             nc.sync.dma_start(dst[:], wa[512 * a : 512 * (a + 1), :].rearrange("(p j) c -> p j c", j=4))
 
-        def turn_bias(dst, row, name):
+        def turn_biases():
             nc.scalar.copy(
                 bb_by_t[:].rearrange("k t (z u) -> k t z u", u=8), bb_row[:].rearrange("k (z t u) -> k t z u", t=4, u=8)
             )
-            turned = bank(7, name)
+            turned = bank(7, "bias_ps")
             for t in range(4):
                 nc.tensor.transpose(turned[:, P * t : P * (t + 1)], bb_by_t[:, t, :], ident[:])
-            nc.scalar.activation(dst[:], turned[:, row : 4 * P : P], IDENTITY)
+            nc.scalar.activation(bias_ab[:], turned[:].rearrange("p (t k) -> p t k", t=4)[:, :, 126:128], IDENTITY)
 
         make_identity(nc, ident[:], nomemset=True)
-        nc.scalar.dma_start(bb_row[127:128, :], bb.rearrange("(o r) -> o r", o=1))
-        turn_bias(bias_b, 127, "bb_ps")
 
         nc.sync.dma_start(offsets[:], offs)
         nc.sync.dma_start(wb_raw[:].bitcast(I32), wb_words.rearrange("a p c -> p a c").bitcast(I32))
@@ -108,19 +103,26 @@ def tile_list_ad_feature_cross_kernel(
                 tab_s[r:P:16, :].bitcast(I32), tab_scales[:, r:16:4, :].rearrange("a q c -> q a c").bitcast(I32)
             )
         load_table_words(0)
+        nc.sync.dma_start(bb_row[127:128, :], bb.rearrange("(o r) -> o r", o=1))
+        nc.sync.dma_start(bb_row[126:127, :], ba.rearrange("(o r) -> o r", o=1))
         load_scale_rows(wb_s_raw, wb_scales)
         load_table_words(1)
-        nc.sync.dma_start(bb_row[126:127, :], ba.rearrange("(o r) -> o r", o=1))
-        turn_bias(bias_a, 126, "ba_ps")
-        for h in range(2):
-            nc.vector.tensor_copy(v_s[h][:], tab_s[:].indirect(offsets[:, 32 * h : 32 * (h + 1)]))
-
-        def shift_plane(h):
-            nc.sync.dma_start(v_s1[h][0:112, :].bitcast(I32), v_s[h][16:128, :].bitcast(I32))
-
-        shift_plane(0)
+        nc.vector.tensor_copy(v_s[0][:], tab_s[:].indirect(offsets[:]))
         load_wa(wa_raw0, 0)
-        shift_plane(1)
+        nc.sync.dma_start(v_s[1][0:112, :].bitcast(I32), v_s[0][16:128, :].bitcast(I32))
+
+        warm = bank(4, "warm")
+        for i in range(3):
+            nc.tensor.matmul_mx(
+                out=warm[:],
+                lhsT=tab_w[0][:, HALF : HALF + P].bitcast(FP8X4),
+                lhsT_scale=tab_s[:, HALF : HALF + P],
+                rhs=tab_w[0][:, 0:HALF].bitcast(FP8X4),
+                rhs_scale=v_s[0][:, 0:HALF],
+                start=True,
+                stop=True,
+            )
+        turn_biases()
 
 
         def gather_words(a, h, dst):
@@ -154,8 +156,7 @@ def tile_list_ad_feature_cross_kernel(
             return v_w[a][h][:, lo - HALF * h : hi - HALF * h].bitcast(FP8X4)
 
         def v_plane(a, lo, hi):
-            h = lo // HALF
-            return (v_s, v_s1)[a][h][:, lo - HALF * h : hi - HALF * h]
+            return v_s[a][:, lo:hi]
 
         b_sb = [
             sb("b_sb0", [P, 4, HALF], F32),
@@ -163,7 +164,7 @@ def tile_list_ad_feature_cross_kernel(
         ]
         b_ps = [[bank(4 * h + t, "b_ps%d%d" % (h, t)) for t in range(4)] for h in range(2)]
         for h in range(2):
-            for i, a in enumerate((0, 1) if h == 0 else (1, 0)):
+            for a in range(PASSES):
                 for t in range(4):
                     nc.tensor.matmul_mx(
                         out=b_ps[h][t][:],
@@ -171,16 +172,13 @@ def tile_list_ad_feature_cross_kernel(
                         lhsT_scale=wb_s[:, a, P * t : P * (t + 1)],
                         rhs=v_words(a, HALF * h, HALF * (h + 1)),
                         rhs_scale=v_plane(a, HALF * h, HALF * (h + 1)),
-                        start=(i == 0),
-                        stop=(i == PASSES - 1),
+                        start=(a == 0),
+                        stop=(a == PASSES - 1),
                     )
 
         def empty_b(h):
             for t in range(4):
-                nc.scalar.activation(b_sb[h][:, t, :], b_ps[h][t][:], IDENTITY, bias=bias_b[:, t : t + 1])
-
-        empty_b(0)
-        empty_b(1)
+                nc.scalar.activation(b_sb[h][:, t, :], b_ps[h][t][:], IDENTITY, bias=bias_ab[:, t, 1:2])
 
         def round_wa(a, t, copy):
             copy(
@@ -193,7 +191,9 @@ def tile_list_ad_feature_cross_kernel(
             nc.vector.quantize_mx(out=wa_w[a][:, cols].bitcast(FP8X4), scales=wa_s[a][:, cols], in_=wa_bf[a][:, t, :])
 
         for t in range(4):
-            round_wa(0, t, nc.vector.tensor_copy)
+            round_wa(0, t, nc.scalar.copy if t < 2 else nc.vector.tensor_copy)
+        empty_b(0)
+        empty_b(1)
         nc.vector.quantize_mx(
             out=wa_w[0][:].bitcast(FP8X4), scales=wa_s[0][:], in_=wa_bf[0][:].rearrange("p t c -> p (t c)")
         )
@@ -225,14 +225,14 @@ def tile_list_ad_feature_cross_kernel(
         h_planes = sb("h_planes", [P, 4, first_hi], BF16)
         for t in range(4):
             nc.vector.scalar_tensor_tensor(
-                h_planes[:, t, :], a_ps[0][t][:, 0:first_hi], bias_a[:, t : t + 1], b_sb[0][:, t, 0:first_hi], ADD, MULT
+                h_planes[:, t, :], a_ps[0][t][:, 0:first_hi], bias_ab[:, t, 0:1], b_sb[0][:, t, 0:first_hi], ADD, MULT
             )
         a_sb = [sb("a_sb%d" % e, [P, 4, hi - lo], F32) for e, (lo, hi) in enumerate(EVACS)]
         for e, (lo, hi) in enumerate(EVACS):
             h = lo // HALF
             for t in range(4):
                 nc.scalar.activation(
-                    a_sb[e][:, t, :], a_ps[h][t][:, lo - HALF * h : hi - HALF * h], IDENTITY, bias=bias_a[:, t : t + 1]
+                    a_sb[e][:, t, :], a_ps[h][t][:, lo - HALF * h : hi - HALF * h], IDENTITY, bias=bias_ab[:, t, 0:1]
                 )
             if e == 0:
                 nc.scalar.copy(

@@ -94,6 +94,7 @@ def tile_list_ad_feature_cross_kernel(
                 nc.tensor.transpose(turned[:, P * t : P * (t + 1)], bb_by_t[:, t, :], ident[:])
             nc.scalar.activation(bias_ab[:], turned[:].rearrange("p (t k) -> p t k", t=4)[:, :, 126:128], IDENTITY)
 
+        nc.scalar.activation(bias_ab[0:96, 0, 0:1], bb_row[0:96, 0:1], IDENTITY)
         make_identity(nc, ident[:], nomemset=True)
 
         nc.sync.dma_start(offsets[:], offs)

@@ -252,9 +252,9 @@ def tile_list_ad_feature_cross_kernel(
             elo = EVACS[e][0]
             h = lo // HALF
             nc.vector.tensor_tensor(
-                h_bf[c][:].rearrange("p (c i) t -> p c t i", i=2),
-                a_sb[e][:, :, lo - elo : hi - elo].rearrange("p t (c i) -> p c t i", i=2),
-                b_sb[h][:, :, lo - HALF * h : hi - HALF * h].rearrange("p t (c i) -> p c t i", i=2),
+                h_bf[c][:].rearrange("p (c i) t -> p c t i", i=4),
+                a_sb[e][:, :, lo - elo : hi - elo].rearrange("p t (c i) -> p c t i", i=4),
+                b_sb[h][:, :, lo - HALF * h : hi - HALF * h].rearrange("p t (c i) -> p c t i", i=4),
                 MULT,
             )
 

@@ -22,7 +22,7 @@ P = 128
 PASSES = K // 512
 HALF = 512
 CHUNKS = [(0, 256), (256, 512), (512, 768), (768, 896), (896, 1024)]
-EVACS = [(256, 512), (512, 768), (768, 1024)]
+EVACS = [(512, 768), (768, 1024)]
 
 
 def tile_list_ad_feature_cross_kernel(
@@ -222,30 +222,29 @@ def tile_list_ad_feature_cross_kernel(
         h_w = [sb("h_w%d" % c, [P, hi - lo], U32) for c, (lo, hi) in enumerate(CHUNKS)]
         h_s = [sb("h_s%d" % c, [P, hi - lo], U8) for c, (lo, hi) in enumerate(CHUNKS)]
 
-        first_hi = CHUNKS[0][1]
+        first_hi = HALF
         h_planes = sb("h_planes", [P, 4, first_hi], BF16)
         for t in range(4):
             nc.vector.scalar_tensor_tensor(
                 h_planes[:, t, :], a_ps[0][t][:, 0:first_hi], bias_ab[:, t, 0:1], b_sb[0][:, t, 0:first_hi], ADD, MULT
             )
         a_sb = [sb("a_sb%d" % e, [P, 4, hi - lo], F32) for e, (lo, hi) in enumerate(EVACS)]
+        nc.scalar.copy(
+            wo_bf[:].rearrange("p (c i) t -> p c t i", i=4), wo_raw[:].rearrange("p t (c i) -> p c t i", i=4)
+        )
         for e, (lo, hi) in enumerate(EVACS):
             h = lo // HALF
             for t in range(4):
                 nc.scalar.activation(
                     a_sb[e][:, t, :], a_ps[h][t][:, lo - HALF * h : hi - HALF * h], IDENTITY, bias=bias_ab[:, t, 0:1]
                 )
-            if e == 0:
-                nc.scalar.copy(
-                    wo_bf[:].rearrange("p (c i) t -> p c t i", i=4), wo_raw[:].rearrange("p t (c i) -> p c t i", i=4)
-                )
 
         def cross(c):
             lo, hi = CHUNKS[c]
-            if c == 0:
+            if hi <= first_hi:
                 nc.vector.tensor_copy(
-                    h_bf[0][:].rearrange("p (c i) t -> p c t i", i=4),
-                    h_planes[:].rearrange("p t (c i) -> p c t i", i=4),
+                    h_bf[c][:].rearrange("p (c i) t -> p c t i", i=4),
+                    h_planes[:, :, lo:hi].rearrange("p t (c i) -> p c t i", i=4),
                 )
                 return
             e = [x for x, (elo, ehi) in enumerate(EVACS) if elo <= lo < ehi][0]
@@ -266,11 +265,13 @@ def tile_list_ad_feature_cross_kernel(
         cross(0)
         for c in range(1, len(CHUNKS)):
             cross(c)
-            quantise_h(c - 1)
+            if c != 2:
+                quantise_h(c - 1)
             if c == 1:
                 nc.vector.quantize_mx(
                     out=wo_w[:].bitcast(FP8X4), scales=wo_s[:], in_=wo_bf[:].rearrange("p n t -> p (n t)")
                 )
+                quantise_h(1)
         quantise_h(len(CHUNKS) - 1)
 
         out_by_half = out.rearrange("(h p) s -> p h s", p=P)

@@ -22,6 +22,7 @@ P = 128
 PASSES = K // 512
 HALF = 512
 CHUNKS = [(0, 256), (256, 512), (512, 768), (768, 896), (896, 1024)]
+FUSED = 512
 EVACS = [(512, 768), (768, 1024)]
 
 
@@ -69,8 +70,7 @@ def tile_list_ad_feature_cross_kernel(
         nc.vector.memset(wb_s_raw[:].rearrange("p a c -> p (a c)").bitcast(I32), 0)
         nc.vector.memset(v_s[1][96:128, :].bitcast(I32), 0)
         nc.vector.memset(wl_s[:].rearrange("p a c -> p (a c)").bitcast(I32), 0)
-        nc.vector.memset(bb_row[0:96, :], 0.0)
-        nc.vector.memset(bb_row[96:126, :], 0.0)
+        nc.vector.memset(bb_by_t[:].rearrange("k t c -> k (t c)"), 0.0)
 
         def load_scale_rows(dst, src):
             for q in range(4):
@@ -87,14 +87,15 @@ def tile_list_ad_feature_cross_kernel(
 
         def turn_biases():
             nc.scalar.copy(
-                bb_by_t[:].rearrange("k t (z u) -> k t z u", u=8), bb_row[:].rearrange("k (z t u) -> k t z u", t=4, u=8)
+                bb_by_t[0:2].rearrange("k t (z u) -> k t z u", u=8),
+                bb_row[0:2, :].rearrange("k (z t u) -> k t z u", t=4, u=8),
             )
             turned = bank(7, "bias_ps")
             for t in range(4):
                 nc.tensor.transpose(turned[:, P * t : P * (t + 1)], bb_by_t[:, t, :], ident[:])
-            nc.scalar.activation(bias_ab[:], turned[:].rearrange("p (t k) -> p t k", t=4)[:, :, 126:128], IDENTITY)
+            nc.scalar.activation(bias_ab[:], turned[:].rearrange("p (t k) -> p t k", t=4)[:, :, 0:2], IDENTITY)
 
-        nc.scalar.activation(bias_ab[0:96, 0, 0:1], bb_row[0:96, 0:1], IDENTITY)
+        nc.scalar.activation(bias_ab[:, 0, 0:1], bb_by_t[:, 0, 0:1], IDENTITY)
         make_identity(nc, ident[:], nomemset=True)
 
         nc.sync.dma_start(offsets[:], offs)
@@ -104,8 +105,8 @@ def tile_list_ad_feature_cross_kernel(
                 tab_s[r:P:16, :].bitcast(I32), tab_scales[:, r:16:4, :].rearrange("a q c -> q a c").bitcast(I32)
             )
         load_table_words(0)
-        nc.sync.dma_start(bb_row[127:128, :], bb.rearrange("(o r) -> o r", o=1))
-        nc.sync.dma_start(bb_row[126:127, :], ba.rearrange("(o r) -> o r", o=1))
+        nc.sync.dma_start(bb_row[1:2, :], bb.rearrange("(o r) -> o r", o=1))
+        nc.sync.dma_start(bb_row[0:1, :], ba.rearrange("(o r) -> o r", o=1))
         load_scale_rows(wb_s_raw, wb_scales)
         load_table_words(1)
         nc.vector.tensor_copy(v_s[0][:], tab_s[:].indirect(offsets[:]))
@@ -119,7 +120,7 @@ def tile_list_ad_feature_cross_kernel(
                 lhsT=tab_w[0][:, HALF : HALF + P].bitcast(FP8X4),
                 lhsT_scale=tab_s[:, HALF : HALF + P],
                 rhs=tab_w[0][:, 0:HALF].bitcast(FP8X4),
-                rhs_scale=v_s[0][:, 0:HALF],
+                rhs_scale=tab_s[:, 0:HALF],
                 start=True,
                 stop=True,
             )
@@ -159,27 +160,25 @@ def tile_list_ad_feature_cross_kernel(
         def v_plane(a, lo, hi):
             return v_s[a][:, lo:hi]
 
-        b_sb = [
-            sb("b_sb0", [P, 4, HALF], F32),
-            sb("b_sb1", [P, 4, HALF], F32),
-        ]
+        b_first = sb("b_first", [P, 4, HALF], F32)
+        b_second = sb("b_second", [P, 4, HALF], F32)
         b_ps = [[bank(4 * h + t, "b_ps%d%d" % (h, t)) for t in range(4)] for h in range(2)]
         for h in range(2):
-            for a in range(PASSES):
+            for step in range(PASSES):
                 for t in range(4):
+                    a = step
                     nc.tensor.matmul_mx(
                         out=b_ps[h][t][:],
                         lhsT=wb_w[:, a, 256 * t : 256 * (t + 1)].bitcast(FP4X4),
                         lhsT_scale=wb_s[:, a, P * t : P * (t + 1)],
                         rhs=v_words(a, HALF * h, HALF * (h + 1)),
                         rhs_scale=v_plane(a, HALF * h, HALF * (h + 1)),
-                        start=(a == 0),
-                        stop=(a == PASSES - 1),
+                        start=(step == 0),
+                        stop=(step == PASSES - 1),
                     )
 
-        def empty_b(h):
-            for t in range(4):
-                nc.scalar.activation(b_sb[h][:, t, :], b_ps[h][t][:], IDENTITY, bias=bias_ab[:, t, 1:2])
+        def empty_b(dst, h, t):
+            nc.scalar.activation(dst, b_ps[h][t][:], IDENTITY, bias=bias_ab[:, t, 1:2])
 
         def round_wa(a, t, copy):
             copy(
@@ -192,12 +191,18 @@ def tile_list_ad_feature_cross_kernel(
             nc.vector.quantize_mx(out=wa_w[a][:, cols].bitcast(FP8X4), scales=wa_s[a][:, cols], in_=wa_bf[a][:, t, :])
 
         for t in range(4):
-            round_wa(0, t, nc.scalar.copy if t < 2 else nc.vector.tensor_copy)
-        empty_b(0)
-        empty_b(1)
-        nc.vector.quantize_mx(
-            out=wa_w[0][:].bitcast(FP8X4), scales=wa_s[0][:], in_=wa_bf[0][:].rearrange("p t c -> p (t c)")
-        )
+            round_wa(0, t, nc.scalar.copy if t == 0 else nc.vector.tensor_copy)
+        for t in range(4):
+            empty_b(b_first[:, t, :], 0, t)
+        for t in range(4):
+            empty_b(b_second[:, t, :], 1, t)
+        for lo in (0, 2):
+            cols = slice(P * lo, P * (lo + 2))
+            nc.vector.quantize_mx(
+                out=wa_w[0][:, cols].bitcast(FP8X4),
+                scales=wa_s[0][:, cols],
+                in_=wa_bf[0][:, lo : lo + 2, :].rearrange("p t c -> p (t c)"),
+            )
         for t in range(4):
             round_wa(1, t, nc.vector.tensor_copy)
             if t > 0:
@@ -206,28 +211,30 @@ def tile_list_ad_feature_cross_kernel(
 
         a_ps = [[bank(4 * h + t, "a_ps%d%d" % (h, t)) for t in range(4)] for h in range(2)]
         for h in range(2):
-            for a in range(PASSES):
-                for t in range(4):
+            for t in range(4):
+                for step in range(PASSES):
+                    a = 1 - step if h == 0 and t >= 2 else step
                     nc.tensor.matmul_mx(
                         out=a_ps[h][t][:],
                         lhsT=wa_w[a][:, P * t : P * (t + 1)].bitcast(FP8X4),
                         lhsT_scale=wa_s[a][:, P * t : P * (t + 1)],
                         rhs=v_words(a, HALF * h, HALF * (h + 1)),
                         rhs_scale=v_plane(a, HALF * h, HALF * (h + 1)),
-                        start=(a == 0),
-                        stop=(a == PASSES - 1),
+                        start=(step == 0),
+                        stop=(step == PASSES - 1),
                     )
 
         h_bf = [sb("h_bf%d" % c, [P, hi - lo, 4], BF16) for c, (lo, hi) in enumerate(CHUNKS)]
         h_w = [sb("h_w%d" % c, [P, hi - lo], U32) for c, (lo, hi) in enumerate(CHUNKS)]
         h_s = [sb("h_s%d" % c, [P, hi - lo], U8) for c, (lo, hi) in enumerate(CHUNKS)]
 
-        first_hi = HALF
+        first_hi = FUSED
         h_planes = sb("h_planes", [P, 4, first_hi], BF16)
         for t in range(4):
-            nc.vector.scalar_tensor_tensor(
-                h_planes[:, t, :], a_ps[0][t][:, 0:first_hi], bias_ab[:, t, 0:1], b_sb[0][:, t, 0:first_hi], ADD, MULT
-            )
+            for lo, hi in [CHUNKS[0], (CHUNKS[0][1], first_hi)] if t == 3 else [(0, first_hi)]:
+                nc.vector.scalar_tensor_tensor(
+                    h_planes[:, t, lo:hi], a_ps[0][t][:, lo:hi], bias_ab[:, t, 0:1], b_first[:, t, lo:hi], ADD, MULT
+                )
         a_sb = [sb("a_sb%d" % e, [P, 4, hi - lo], F32) for e, (lo, hi) in enumerate(EVACS)]
         nc.scalar.copy(
             wo_bf[:].rearrange("p (c i) t -> p c t i", i=4), wo_raw[:].rearrange("p t (c i) -> p c t i", i=4)
@@ -239,23 +246,26 @@ def tile_list_ad_feature_cross_kernel(
                     a_sb[e][:, t, :], a_ps[h][t][:, lo - HALF * h : hi - HALF * h], IDENTITY, bias=bias_ab[:, t, 0:1]
                 )
 
+        def by_four(ap):
+            return ap.rearrange("p t (c i) -> p c t i", i=4)
+
         def cross(c):
             lo, hi = CHUNKS[c]
-            if hi <= first_hi:
+            mid = min(max(lo, first_hi), hi)
+            if mid > lo:
                 nc.vector.tensor_copy(
-                    h_bf[c][:].rearrange("p (c i) t -> p c t i", i=4),
-                    h_planes[:, :, lo:hi].rearrange("p t (c i) -> p c t i", i=4),
+                    h_bf[c][:, 0 : mid - lo, :].rearrange("p (c i) t -> p c t i", i=4), by_four(h_planes[:, :, lo:mid])
                 )
-                return
-            e = [x for x, (elo, ehi) in enumerate(EVACS) if elo <= lo < ehi][0]
-            elo = EVACS[e][0]
-            h = lo // HALF
-            nc.vector.tensor_tensor(
-                h_bf[c][:].rearrange("p (c i) t -> p c t i", i=4),
-                a_sb[e][:, :, lo - elo : hi - elo].rearrange("p t (c i) -> p c t i", i=4),
-                b_sb[h][:, :, lo - HALF * h : hi - HALF * h].rearrange("p t (c i) -> p c t i", i=4),
-                MULT,
-            )
+            if hi > mid:
+                e = [x for x, (elo, ehi) in enumerate(EVACS) if elo <= mid < ehi][0]
+                elo = EVACS[e][0]
+                h = lo // HALF
+                nc.vector.tensor_tensor(
+                    h_bf[c][:, mid - lo : hi - lo, :].rearrange("p (c i) t -> p c t i", i=4),
+                    by_four(a_sb[e][:, :, mid - elo : hi - elo]),
+                    by_four((b_first, b_second)[h][:, :, mid - HALF * h : hi - HALF * h]),
+                    MULT,
+                )
 
         def quantise_h(c):
             nc.vector.quantize_mx(

@@ -44,7 +44,7 @@ def tile_list_ad_feature_cross_kernel(
         offsets = keep.tile([P, S // 16], U16, name="offsets")
         tab_s = sb("tab_s", [P, T], U8)
         tab_w = [sb("tab_w%d" % a, [P, T], U32) for a in range(PASSES)]
-        wb_raw = sb("wb_raw", [P, PASSES, 2 * R], U8)
+        wb_raw = reuse.tile([P, PASSES, 2 * R], U8, name="wb_raw", align_bytes=256, offset=24576)
         wb_s_raw = reuse.tile([P, PASSES, R], U8, name="wb_s_raw", align_bytes=256, offset=1536)
         wb_w = sb("wb_w", [P, PASSES, 2 * R], U8)
         wb_s = sb("wb_s", [P, PASSES, R], U8)
@@ -58,7 +58,7 @@ def tile_list_ad_feature_cross_kernel(
         wo_bf = sb("wo_bf", [P, N, 4], BF16)
         wo_w = sb("wo_w", [P, N], U32)
         wo_s = sb("wo_s", [P, N], U8)
-        v_s = [sb("v_s%d" % a, [P, S], U8) for a in range(PASSES)]
+        v_s = [reuse.tile([P, S], U8, name="v_s0", align_bytes=256, offset=24576), sb("v_s1", [P, S], U8)]
         bb_row = sb("bb_row", [P, R], F32)
         bb_by_t = sb("bb_by_t", [P, 4, P], F32)
         ident = sb("ident", [P, P], F32)
@@ -73,10 +73,10 @@ def tile_list_ad_feature_cross_kernel(
         nc.vector.memset(bb_by_t[:].rearrange("k t c -> k (t c)"), 0.0)
 
         def load_scale_rows(dst, src):
-            for q in range(4):
+            for r in range(4):
                 nc.sync.dma_start(
-                    dst[32 * q : 32 * q + 4].bitcast(I32),
-                    src[:, 4 * q : 4 * q + 4, :].rearrange("a r c -> r a c").bitcast(I32),
+                    dst[r:P:32].bitcast(I32),
+                    src[:, r:16:4, :].rearrange("a q c -> q a c").bitcast(I32),
                 )
 
         def load_table_words(a):
@@ -109,6 +109,10 @@ def tile_list_ad_feature_cross_kernel(
         nc.sync.dma_start(bb_row[0:1, :], ba.rearrange("(o r) -> o r", o=1))
         load_scale_rows(wb_s_raw, wb_scales)
         load_table_words(1)
+        nc.vector.tensor_copy(
+            wb_w[:].bitcast(I32).rearrange("p a (t q w) -> p a t q w", t=4, w=4),
+            wb_raw[:].bitcast(I32).rearrange("p a (q t w) -> p a t q w", t=4, w=4),
+        )
         nc.vector.tensor_copy(v_s[0][:], tab_s[:].indirect(offsets[:]))
         load_wa(wa_raw0, 0)
         nc.sync.dma_start(v_s[1][0:112, :].bitcast(I32), v_s[0][16:128, :].bitcast(I32))
@@ -131,10 +135,6 @@ def tile_list_ad_feature_cross_kernel(
             nc.vector.tensor_copy(dst[:], tab_w[a][:].indirect(offsets[:, 32 * h : 32 * (h + 1)]))
             return dst
 
-        nc.vector.tensor_copy(
-            wb_w[:].bitcast(I32).rearrange("p a (t q w) -> p a t q w", t=4, w=4),
-            wb_raw[:].bitcast(I32).rearrange("p a (q t w) -> p a t q w", t=4, w=4),
-        )
         v_w00 = gather_words(0, 0, sb("v_w00", [P, HALF], U32))
         nc.vector.tensor_copy(
             wb_s[:].bitcast(I32).rearrange("p a (t q w) -> p a t q w", t=4, w=2),
@@ -143,8 +143,13 @@ def tile_list_ad_feature_cross_kernel(
         v_w01 = gather_words(0, 1, reuse.tile([P, HALF], U32, name="v_w01", align_bytes=256, offset=0))
         v_w = [[v_w00, v_w01], [gather_words(1, h, sb("v_w1%d" % h, [P, HALF], U32)) for h in range(2)]]
 
-        wa_raw = [wa_raw0, reuse.tile([P, 4, R], F32, name="wa_raw1", align_bytes=256, offset=4096)]
-        load_wa(wa_raw[1], 1)
+        wa_raw1 = [
+            reuse.tile([P, 4, R // 2], F32, name="wa_raw1%d" % g, align_bytes=256, offset=4096 * (g + 1))
+            for g in range(2)
+        ]
+        wa_rows1 = wa[512:1024, :].rearrange("(p j) c -> p j c", j=4)
+        for g in range(2):
+            nc.sync.dma_start(wa_raw1[g][:], wa_rows1[:, :, 256 * g : 256 * (g + 1)])
         wo_by_t = wo.rearrange("(q t u) n -> t q u n", t=4, u=8)
         for t in range(4):
             nc.sync.dma_start(wo_raw[:, t, :], wo_by_t[t])
@@ -183,7 +188,13 @@ def tile_list_ad_feature_cross_kernel(
         def round_wa(a, t, copy):
             copy(
                 wa_bf[a][:, t, :].rearrange("p (q g i j) -> p q g j i", g=2, i=4, j=4),
-                wa_raw[a][:].rearrange("p j (q t g i) -> p t q g j i", t=4, g=2, i=4)[:, t],
+                wa_raw0[:].rearrange("p j (q t g i) -> p t q g j i", t=4, g=2, i=4)[:, t],
+            )
+
+        def round_wa1(half, t):
+            nc.vector.tensor_copy(
+                wa_bf[1][:, t, 256 * half : 256 * (half + 1)].rearrange("p (q g i j) -> p q g j i", g=2, i=4, j=4),
+                wa_raw1[half][:].rearrange("p j (q t g i) -> p t q g j i", t=4, g=2, i=4)[:, t],
             )
 
         def quantise_wa(a, t):
@@ -204,7 +215,9 @@ def tile_list_ad_feature_cross_kernel(
                 in_=wa_bf[0][:, lo : lo + 2, :].rearrange("p t c -> p (t c)"),
             )
         for t in range(4):
-            round_wa(1, t, nc.vector.tensor_copy)
+            round_wa1(0, t)
+        for t in range(4):
+            round_wa1(1, t)
             if t > 0:
                 quantise_wa(1, t - 1)
         quantise_wa(1, 3)

@@ -22,8 +22,8 @@ P = 128
 PASSES = K // 512
 HALF = 512
 CHUNKS = [(0, 256), (256, 512), (512, 768), (768, 896), (896, 1024)]
-FUSED = 512
 EVACS = [(512, 768), (768, 1024)]
+WARM_UPS = 3
 
 
 def tile_list_ad_feature_cross_kernel(
@@ -38,19 +38,23 @@ def tile_list_ad_feature_cross_kernel(
         def sb(name, shape, dtype):
             return keep.tile(shape, dtype, name=name, align_bytes=256)
 
+        def placed(name, shape, dtype, offset):
+            return reuse.tile(shape, dtype, name=name, align_bytes=256, offset=offset)
+
         def bank(index, name):
             return psum.tile([P, HALF], F32, name=name, tag="bank%d" % index)
 
         offsets = keep.tile([P, S // 16], U16, name="offsets")
         tab_s = sb("tab_s", [P, T], U8)
         tab_w = [sb("tab_w%d" % a, [P, T], U32) for a in range(PASSES)]
-        wb_raw = reuse.tile([P, PASSES, 2 * R], U8, name="wb_raw", align_bytes=256, offset=24576)
-        wb_s_raw = reuse.tile([P, PASSES, R], U8, name="wb_s_raw", align_bytes=256, offset=1536)
+        wb_raw = placed("wb_raw", [P, PASSES, 2 * R], U8, 4096)
+        wb_s_raw = placed("wb_s_raw", [P, PASSES, R], U8, 1536)
         wb_w = sb("wb_w", [P, PASSES, 2 * R], U8)
         wb_s = sb("wb_s", [P, PASSES, R], U8)
         wl_w = sb("wl_w", [P, PASSES, N], U32)
         wl_s = sb("wl_s", [P, PASSES, N], U8)
         wa_raw0 = sb("wa_raw0", [P, 4, R], F32)
+        wa_raw1 = [sb("wa_raw1%d" % g, [P, 4, R // 2], F32) for g in range(2)]
         wa_bf = [sb("wa_bf%d" % a, [P, 4, 4 * P], BF16) for a in range(PASSES)]
         wa_w = [sb("wa_w%d" % a, [P, R], U32) for a in range(PASSES)]
         wa_s = [sb("wa_s%d" % a, [P, R], U8) for a in range(PASSES)]
@@ -58,7 +62,7 @@ def tile_list_ad_feature_cross_kernel(
         wo_bf = sb("wo_bf", [P, N, 4], BF16)
         wo_w = sb("wo_w", [P, N], U32)
         wo_s = sb("wo_s", [P, N], U8)
-        v_s = [reuse.tile([P, S], U8, name="v_s0", align_bytes=256, offset=24576), sb("v_s1", [P, S], U8)]
+        v_s = [placed("v_s0", [P, S], U8, 4096), sb("v_s1", [P, S], U8)]
         bb_row = sb("bb_row", [P, R], F32)
         bb_by_t = sb("bb_by_t", [P, 4, P], F32)
         ident = sb("ident", [P, P], F32)
@@ -75,25 +79,13 @@ def tile_list_ad_feature_cross_kernel(
         def load_scale_rows(dst, src):
             for r in range(4):
                 nc.sync.dma_start(
-                    dst[r:P:32].bitcast(I32),
-                    src[:, r:16:4, :].rearrange("a q c -> q a c").bitcast(I32),
+                    dst[r:P:32].bitcast(I32), src[:, r:16:4, :].rearrange("a q c -> q a c").bitcast(I32)
                 )
 
         def load_table_words(a):
             nc.sync.dma_start(tab_w[a][:].bitcast(I32), tab_words[a].rearrange("p t i -> p (t i)").bitcast(I32))
 
-        def load_wa(dst, a):
-            nc.sync.dma_start(dst[:], wa[512 * a : 512 * (a + 1), :].rearrange("(p j) c -> p j c", j=4))
-
-        def turn_biases():
-            nc.scalar.copy(
-                bb_by_t[0:2].rearrange("k t (z u) -> k t z u", u=8),
-                bb_row[0:2, :].rearrange("k (z t u) -> k t z u", t=4, u=8),
-            )
-            turned = bank(7, "bias_ps")
-            for t in range(4):
-                nc.tensor.transpose(turned[:, P * t : P * (t + 1)], bb_by_t[:, t, :], ident[:])
-            nc.scalar.activation(bias_ab[:], turned[:].rearrange("p (t k) -> p t k", t=4)[:, :, 0:2], IDENTITY)
+        wa_rows = [wa[512 * a : 512 * (a + 1), :].rearrange("(p j) c -> p j c", j=4) for a in range(PASSES)]
 
         nc.scalar.activation(bias_ab[:, 0, 0:1], bb_by_t[:, 0, 0:1], IDENTITY)
         make_identity(nc, ident[:], nomemset=True)
@@ -110,15 +102,16 @@ def tile_list_ad_feature_cross_kernel(
         load_scale_rows(wb_s_raw, wb_scales)
         load_table_words(1)
         nc.vector.tensor_copy(
-            wb_w[:].bitcast(I32).rearrange("p a (t q w) -> p a t q w", t=4, w=4),
-            wb_raw[:].bitcast(I32).rearrange("p a (q t w) -> p a t q w", t=4, w=4),
+            wb_w[:].bitcast(I32).rearrange("p a (t m w) -> p a t m w", t=4, w=2),
+            wb_raw[:].bitcast(I32).rearrange("p a (m t w) -> p a t m w", t=4, w=2),
         )
         nc.vector.tensor_copy(v_s[0][:], tab_s[:].indirect(offsets[:]))
-        load_wa(wa_raw0, 0)
+        nc.sync.dma_start(wa_raw0[:, 0:2, :], wa_rows[0][:, 0:2, :])
         nc.sync.dma_start(v_s[1][0:112, :].bitcast(I32), v_s[0][16:128, :].bitcast(I32))
+        nc.sync.dma_start(wa_raw0[:, 2:4, :], wa_rows[0][:, 2:4, :])
 
         warm = bank(4, "warm")
-        for i in range(3):
+        for i in range(WARM_UPS):
             nc.tensor.matmul_mx(
                 out=warm[:],
                 lhsT=tab_w[0][:, HALF : HALF + P].bitcast(FP8X4),
@@ -128,8 +121,14 @@ def tile_list_ad_feature_cross_kernel(
                 start=True,
                 stop=True,
             )
-        turn_biases()
-
+        nc.scalar.copy(
+            bb_by_t[0:2].rearrange("k t (m i) -> k t m i", i=4),
+            bb_row[0:2, :].rearrange("k (m t i) -> k t m i", t=4, i=4),
+        )
+        turned = bank(7, "bias_ps")
+        for t in range(4):
+            nc.tensor.transpose(turned[:, P * t : P * (t + 1)], bb_by_t[:, t, :], ident[:])
+        nc.scalar.activation(bias_ab[:], turned[:].rearrange("p (t k) -> p t k", t=4)[:, :, 0:2], IDENTITY)
 
         def gather_words(a, h, dst):
             nc.vector.tensor_copy(dst[:], tab_w[a][:].indirect(offsets[:, 32 * h : 32 * (h + 1)]))
@@ -137,20 +136,15 @@ def tile_list_ad_feature_cross_kernel(
 
         v_w00 = gather_words(0, 0, sb("v_w00", [P, HALF], U32))
         nc.vector.tensor_copy(
-            wb_s[:].bitcast(I32).rearrange("p a (t q w) -> p a t q w", t=4, w=2),
-            wb_s_raw[:].bitcast(I32).rearrange("p a (q t w) -> p a t q w", t=4, w=2),
+            wb_s[:].bitcast(I32).rearrange("p a (t m) -> p a m t", t=4),
+            wb_s_raw[:].bitcast(I32).rearrange("p a (m t) -> p a m t", t=4),
         )
-        v_w01 = gather_words(0, 1, reuse.tile([P, HALF], U32, name="v_w01", align_bytes=256, offset=0))
+        v_w01 = gather_words(0, 1, placed("v_w01", [P, HALF], U32, 0))
         v_w = [[v_w00, v_w01], [gather_words(1, h, sb("v_w1%d" % h, [P, HALF], U32)) for h in range(2)]]
 
-        wa_raw1 = [
-            reuse.tile([P, 4, R // 2], F32, name="wa_raw1%d" % g, align_bytes=256, offset=4096 * (g + 1))
-            for g in range(2)
-        ]
-        wa_rows1 = wa[512:1024, :].rearrange("(p j) c -> p j c", j=4)
         for g in range(2):
-            nc.sync.dma_start(wa_raw1[g][:], wa_rows1[:, :, 256 * g : 256 * (g + 1)])
-        wo_by_t = wo.rearrange("(q t u) n -> t q u n", t=4, u=8)
+            nc.sync.dma_start(wa_raw1[g][:], wa_rows[1][:, :, 256 * g : 256 * (g + 1)])
+        wo_by_t = wo.rearrange("(m t i) n -> t m i n", t=4, i=4)
         for t in range(4):
             nc.sync.dma_start(wo_raw[:, t, :], wo_by_t[t])
         nc.sync.dma_start(wl_w[:].bitcast(I32), wl_words.rearrange("a p c i -> p a (c i)").bitcast(I32))
@@ -165,118 +159,121 @@ def tile_list_ad_feature_cross_kernel(
         def v_plane(a, lo, hi):
             return v_s[a][:, lo:hi]
 
-        b_first = sb("b_first", [P, 4, HALF], F32)
-        b_second = sb("b_second", [P, 4, HALF], F32)
+        b_sb = [sb("b_sb%d" % h, [P, 4, HALF], F32) for h in range(2)]
         b_ps = [[bank(4 * h + t, "b_ps%d%d" % (h, t)) for t in range(4)] for h in range(2)]
-        for h in range(2):
-            for step in range(PASSES):
-                for t in range(4):
-                    a = step
-                    nc.tensor.matmul_mx(
-                        out=b_ps[h][t][:],
-                        lhsT=wb_w[:, a, 256 * t : 256 * (t + 1)].bitcast(FP4X4),
-                        lhsT_scale=wb_s[:, a, P * t : P * (t + 1)],
-                        rhs=v_words(a, HALF * h, HALF * (h + 1)),
-                        rhs_scale=v_plane(a, HALF * h, HALF * (h + 1)),
-                        start=(step == 0),
-                        stop=(step == PASSES - 1),
-                    )
 
-        def empty_b(dst, h, t):
-            nc.scalar.activation(dst, b_ps[h][t][:], IDENTITY, bias=bias_ab[:, t, 1:2])
-
-        def round_wa(a, t, copy):
-            copy(
-                wa_bf[a][:, t, :].rearrange("p (q g i j) -> p q g j i", g=2, i=4, j=4),
-                wa_raw0[:].rearrange("p j (q t g i) -> p t q g j i", t=4, g=2, i=4)[:, t],
+        def b_pass(h, t, a, first):
+            nc.tensor.matmul_mx(
+                out=b_ps[h][t][:],
+                lhsT=wb_w[:, a, 256 * t : 256 * (t + 1)].bitcast(FP4X4),
+                lhsT_scale=wb_s[:, a, P * t : P * (t + 1)],
+                rhs=v_words(a, HALF * h, HALF * (h + 1)),
+                rhs_scale=v_plane(a, HALF * h, HALF * (h + 1)),
+                start=first,
+                stop=not first,
             )
 
-        def round_wa1(half, t):
+        for a in range(PASSES):
+            for t in range(4):
+                b_pass(0, t, a, a == 0)
+        for t in range(4):
+            order = (0, 1) if t < 2 else (1, 0)
+            for a in order:
+                b_pass(1, t, a, a == order[0])
+
+        def round_wa(dst, src):
             nc.vector.tensor_copy(
-                wa_bf[1][:, t, 256 * half : 256 * (half + 1)].rearrange("p (q g i j) -> p q g j i", g=2, i=4, j=4),
-                wa_raw1[half][:].rearrange("p j (q t g i) -> p t q g j i", t=4, g=2, i=4)[:, t],
+                dst.rearrange("p t (m i j) -> p t m j i", i=4, j=4),
+                src,
             )
 
-        def quantise_wa(a, t):
-            cols = slice(P * t, P * (t + 1))
-            nc.vector.quantize_mx(out=wa_w[a][:, cols].bitcast(FP8X4), scales=wa_s[a][:, cols], in_=wa_bf[a][:, t, :])
+        def by_slice(raw):
+            return raw[:].rearrange("p j (m t i) -> p t m j i", t=4, i=4)
 
-        for t in range(4):
-            round_wa(0, t, nc.scalar.copy if t == 0 else nc.vector.tensor_copy)
-        for t in range(4):
-            empty_b(b_first[:, t, :], 0, t)
-        for t in range(4):
-            empty_b(b_second[:, t, :], 1, t)
-        for lo in (0, 2):
-            cols = slice(P * lo, P * (lo + 2))
+        def quantise_wa(a, lo, hi):
+            cols = slice(P * lo, P * hi)
             nc.vector.quantize_mx(
-                out=wa_w[0][:, cols].bitcast(FP8X4),
-                scales=wa_s[0][:, cols],
-                in_=wa_bf[0][:, lo : lo + 2, :].rearrange("p t c -> p (t c)"),
+                out=wa_w[a][:, cols].bitcast(FP8X4),
+                scales=wa_s[a][:, cols],
+                in_=wa_bf[a][:, lo:hi, :].rearrange("p t c -> p (t c)"),
             )
-        for t in range(4):
-            round_wa1(0, t)
-        for t in range(4):
-            round_wa1(1, t)
-            if t > 0:
-                quantise_wa(1, t - 1)
-        quantise_wa(1, 3)
 
-        a_ps = [[bank(4 * h + t, "a_ps%d%d" % (h, t)) for t in range(4)] for h in range(2)]
+        for lo in (0, 2):
+            round_wa(wa_bf[0][:, lo : lo + 2, :], by_slice(wa_raw0)[:, lo : lo + 2])
         for h in range(2):
             for t in range(4):
-                for step in range(PASSES):
-                    a = 1 - step if h == 0 and t >= 2 else step
-                    nc.tensor.matmul_mx(
-                        out=a_ps[h][t][:],
-                        lhsT=wa_w[a][:, P * t : P * (t + 1)].bitcast(FP8X4),
-                        lhsT_scale=wa_s[a][:, P * t : P * (t + 1)],
-                        rhs=v_words(a, HALF * h, HALF * (h + 1)),
-                        rhs_scale=v_plane(a, HALF * h, HALF * (h + 1)),
-                        start=(step == 0),
-                        stop=(step == PASSES - 1),
-                    )
+                nc.scalar.activation(b_sb[h][:, t, :], b_ps[h][t][:], IDENTITY, bias=bias_ab[:, t, 1:2])
+        for lo in (0, 2):
+            quantise_wa(0, lo, lo + 2)
+        round_wa(wa_bf[1][:, :, 0:256], by_slice(wa_raw1[0]))
+        round_wa(wa_bf[1][:, 0:1, 256:512], by_slice(wa_raw1[1])[:, 0:1])
+        nc.vector.tensor_copy(
+            wa_bf[1][:, 1:4, 256:512].rearrange("p t (m i j) -> p m t j i", i=4, j=4),
+            wa_raw1[1][:].rearrange("p j (m t i) -> p m t j i", t=4, i=4)[:, :, 1:4],
+        )
+        for lo, hi in ((0, 1), (1, 2), (2, 4)):
+            quantise_wa(1, lo, hi)
+
+        def a_pass(dst, t, a, lo, hi, first):
+            nc.tensor.matmul_mx(
+                out=dst,
+                lhsT=wa_w[a][:, P * t : P * (t + 1)].bitcast(FP8X4),
+                lhsT_scale=wa_s[a][:, P * t : P * (t + 1)],
+                rhs=v_words(a, lo, hi),
+                rhs_scale=v_plane(a, lo, hi),
+                start=first,
+                stop=not first,
+            )
+
+        a_first = [bank(t, "a_first%d" % t) for t in range(4)]
+        for t in range(4):
+            order = (0, 1) if t < 2 else (1, 0)
+            for a in order:
+                a_pass(a_first[t][:], t, a, 0, HALF, a == order[0])
+        a_late = [[bank(4 + 2 * e + i, "a_late%d%d" % (e, i)) for i in range(2)] for e in range(len(EVACS))]
+
+        def a_late_slice(e, t):
+            return a_late[e][t % 2][:, 256 * (t // 2) : 256 * (t // 2 + 1)]
+
+        late_order = (2, 0, 3, 1)
+        for e, (lo, hi) in enumerate(EVACS):
+            for t in late_order:
+                for a in (1, 0):
+                    a_pass(a_late_slice(e, t), t, a, lo, hi, a == 1)
 
         h_bf = [sb("h_bf%d" % c, [P, hi - lo, 4], BF16) for c, (lo, hi) in enumerate(CHUNKS)]
         h_w = [sb("h_w%d" % c, [P, hi - lo], U32) for c, (lo, hi) in enumerate(CHUNKS)]
         h_s = [sb("h_s%d" % c, [P, hi - lo], U8) for c, (lo, hi) in enumerate(CHUNKS)]
 
-        first_hi = FUSED
-        h_planes = sb("h_planes", [P, 4, first_hi], BF16)
+        h_planes = sb("h_planes", [P, 4, HALF], BF16)
         for t in range(4):
-            for lo, hi in [CHUNKS[0], (CHUNKS[0][1], first_hi)] if t == 3 else [(0, first_hi)]:
+            for lo, hi in CHUNKS[0:2] if t == 3 else [(0, HALF)]:
                 nc.vector.scalar_tensor_tensor(
-                    h_planes[:, t, lo:hi], a_ps[0][t][:, lo:hi], bias_ab[:, t, 0:1], b_first[:, t, lo:hi], ADD, MULT
+                    h_planes[:, t, lo:hi], a_first[t][:, lo:hi], bias_ab[:, t, 0:1], b_sb[0][:, t, lo:hi], ADD, MULT
                 )
         a_sb = [sb("a_sb%d" % e, [P, 4, hi - lo], F32) for e, (lo, hi) in enumerate(EVACS)]
         nc.scalar.copy(
             wo_bf[:].rearrange("p (c i) t -> p c t i", i=4), wo_raw[:].rearrange("p t (c i) -> p c t i", i=4)
         )
-        for e, (lo, hi) in enumerate(EVACS):
-            h = lo // HALF
-            for t in range(4):
-                nc.scalar.activation(
-                    a_sb[e][:, t, :], a_ps[h][t][:, lo - HALF * h : hi - HALF * h], IDENTITY, bias=bias_ab[:, t, 0:1]
-                )
+        for e in range(len(EVACS)):
+            for t in late_order:
+                nc.scalar.activation(a_sb[e][:, t, :], a_late_slice(e, t), IDENTITY, bias=bias_ab[:, t, 0:1])
 
         def by_four(ap):
             return ap.rearrange("p t (c i) -> p c t i", i=4)
 
         def cross(c):
             lo, hi = CHUNKS[c]
-            mid = min(max(lo, first_hi), hi)
-            if mid > lo:
-                nc.vector.tensor_copy(
-                    h_bf[c][:, 0 : mid - lo, :].rearrange("p (c i) t -> p c t i", i=4), by_four(h_planes[:, :, lo:mid])
-                )
-            if hi > mid:
-                e = [x for x, (elo, ehi) in enumerate(EVACS) if elo <= mid < ehi][0]
+            woven = h_bf[c][:].rearrange("p (c i) t -> p c t i", i=4)
+            if hi <= HALF:
+                nc.vector.tensor_copy(woven, by_four(h_planes[:, :, lo:hi]))
+            else:
+                e = (lo - HALF) // 256
                 elo = EVACS[e][0]
-                h = lo // HALF
                 nc.vector.tensor_tensor(
-                    h_bf[c][:, mid - lo : hi - lo, :].rearrange("p (c i) t -> p c t i", i=4),
-                    by_four(a_sb[e][:, :, mid - elo : hi - elo]),
-                    by_four((b_first, b_second)[h][:, :, mid - HALF * h : hi - HALF * h]),
+                    woven,
+                    by_four(a_sb[e][:, :, lo - elo : hi - elo]),
+                    by_four(b_sb[1][:, :, lo - HALF : hi - HALF]),
                     MULT,
                 )
 
@@ -286,16 +283,16 @@ def tile_list_ad_feature_cross_kernel(
             )
 
         cross(0)
-        for c in range(1, len(CHUNKS)):
-            cross(c)
-            if c != 2:
-                quantise_h(c - 1)
-            if c == 1:
-                nc.vector.quantize_mx(
-                    out=wo_w[:].bitcast(FP8X4), scales=wo_s[:], in_=wo_bf[:].rearrange("p n t -> p (n t)")
-                )
-                quantise_h(1)
-        quantise_h(len(CHUNKS) - 1)
+        cross(1)
+        quantise_h(0)
+        nc.vector.quantize_mx(out=wo_w[:].bitcast(FP8X4), scales=wo_s[:], in_=wo_bf[:].rearrange("p n t -> p (n t)"))
+        quantise_h(1)
+        cross(2)
+        cross(3)
+        quantise_h(2)
+        cross(4)
+        quantise_h(3)
+        quantise_h(4)
 
         out_by_half = out.rearrange("(h p) s -> p h s", p=P)
         for c, (lo, hi) in enumerate(CHUNKS):

@@ -53,7 +53,7 @@ def tile_list_ad_feature_cross_kernel(
         wb_s = sb("wb_s", [P, PASSES, R], U8)
         wl_w = sb("wl_w", [P, PASSES, N], U32)
         wl_s = sb("wl_s", [P, PASSES, N], U8)
-        wa_raw0 = sb("wa_raw0", [P, 4, R], F32)
+        wa_raw0 = [sb("wa_raw0%d" % g, [P, 4, R // 2], F32) for g in range(2)]
         wa_raw1 = [sb("wa_raw1%d" % g, [P, 4, R // 2], F32) for g in range(2)]
         wa_bf = [sb("wa_bf%d" % a, [P, 4, 4 * P], BF16) for a in range(PASSES)]
         wa_w = [sb("wa_w%d" % a, [P, R], U32) for a in range(PASSES)]
@@ -72,7 +72,7 @@ def tile_list_ad_feature_cross_kernel(
         nc.vector.memset(tab_s[:].bitcast(I32), 0)
         nc.vector.memset(ident[:], 0.0)
         nc.vector.memset(wb_s_raw[:].rearrange("p a c -> p (a c)").bitcast(I32), 0)
-        nc.vector.memset(v_s[1][96:128, :].bitcast(I32), 0)
+        nc.vector.memset(v_s[1][:].bitcast(I32), 0)
         nc.vector.memset(wl_s[:].rearrange("p a c -> p (a c)").bitcast(I32), 0)
         nc.vector.memset(bb_by_t[:].rearrange("k t c -> k (t c)"), 0.0)
 
@@ -106,9 +106,10 @@ def tile_list_ad_feature_cross_kernel(
             wb_raw[:].bitcast(I32).rearrange("p a (m t w) -> p a t m w", t=4, w=2),
         )
         nc.vector.tensor_copy(v_s[0][:], tab_s[:].indirect(offsets[:]))
-        nc.sync.dma_start(wa_raw0[:, 0:2, :], wa_rows[0][:, 0:2, :])
-        nc.sync.dma_start(v_s[1][0:112, :].bitcast(I32), v_s[0][16:128, :].bitcast(I32))
-        nc.sync.dma_start(wa_raw0[:, 2:4, :], wa_rows[0][:, 2:4, :])
+        nc.sync.dma_start(wa_raw0[0][:], wa_rows[0][:, :, 0:256])
+        for r in range(4):
+            nc.sync.dma_start(v_s[1][r:P:32, :].bitcast(I32), v_s[0][16 + r : P : 32, :].bitcast(I32))
+        nc.sync.dma_start(wa_raw0[1][:], wa_rows[0][:, :, 256:512])
 
         warm = bank(4, "warm")
         for i in range(WARM_UPS):
@@ -198,8 +199,11 @@ def tile_list_ad_feature_cross_kernel(
                 in_=wa_bf[a][:, lo:hi, :].rearrange("p t c -> p (t c)"),
             )
 
+        nc.scalar.copy(
+            wa_bf[0][:, :, 0:256].rearrange("p t (m i j) -> p t m j i", i=4, j=4), by_slice(wa_raw0[0])
+        )
         for lo in (0, 2):
-            round_wa(wa_bf[0][:, lo : lo + 2, :], by_slice(wa_raw0)[:, lo : lo + 2])
+            round_wa(wa_bf[0][:, lo : lo + 2, 256:512], by_slice(wa_raw0[1])[:, lo : lo + 2])
         for h in range(2):
             for t in range(4):
                 nc.scalar.activation(b_sb[h][:, t, :], b_ps[h][t][:], IDENTITY, bias=bias_ab[:, t, 1:2])

@@ -23,7 +23,7 @@ PASSES = K // 512
 HALF = 512
 CHUNKS = [(0, 256), (256, 512), (512, 768), (768, 896), (896, 1024)]
 EVACS = [(512, 768), (768, 1024)]
-WARM_UPS = 3
+WARM_UPS = 2
 
 
 def tile_list_ad_feature_cross_kernel(
@@ -54,7 +54,7 @@ def tile_list_ad_feature_cross_kernel(
         wl_w = sb("wl_w", [P, PASSES, N], U32)
         wl_s = sb("wl_s", [P, PASSES, N], U8)
         wa_raw0 = [sb("wa_raw0%d" % g, [P, 4, R // 2], F32) for g in range(2)]
-        wa_raw1 = [sb("wa_raw1%d" % g, [P, 4, R // 2], F32) for g in range(2)]
+        wa_raw1 = [placed("wa_raw10", [P, 4, R // 2], F32, 12288), sb("wa_raw11", [P, 4, R // 2], F32)]
         wa_bf = [sb("wa_bf%d" % a, [P, 4, 4 * P], BF16) for a in range(PASSES)]
         wa_w = [sb("wa_w%d" % a, [P, R], U32) for a in range(PASSES)]
         wa_s = [sb("wa_s%d" % a, [P, R], U8) for a in range(PASSES)]
@@ -63,7 +63,7 @@ def tile_list_ad_feature_cross_kernel(
         wo_w = sb("wo_w", [P, N], U32)
         wo_s = sb("wo_s", [P, N], U8)
         v_s = [placed("v_s0", [P, S], U8, 4096), sb("v_s1", [P, S], U8)]
-        bb_row = sb("bb_row", [P, R], F32)
+        bb_row = placed("bb_row", [P, R], F32, 8192)
         bb_by_t = sb("bb_by_t", [P, 4, P], F32)
         ident = sb("ident", [P, P], F32)
         bias_ab = sb("bias_ab", [P, 4, 2], F32)
@@ -97,9 +97,9 @@ def tile_list_ad_feature_cross_kernel(
                 tab_s[r:P:16, :].bitcast(I32), tab_scales[:, r:16:4, :].rearrange("a q c -> q a c").bitcast(I32)
             )
         load_table_words(0)
+        load_scale_rows(wb_s_raw, wb_scales)
         nc.sync.dma_start(bb_row[1:2, :], bb.rearrange("(o r) -> o r", o=1))
         nc.sync.dma_start(bb_row[0:1, :], ba.rearrange("(o r) -> o r", o=1))
-        load_scale_rows(wb_s_raw, wb_scales)
         load_table_words(1)
         nc.vector.tensor_copy(
             wb_w[:].bitcast(I32).rearrange("p a (t m w) -> p a t m w", t=4, w=2),
@@ -140,7 +140,7 @@ def tile_list_ad_feature_cross_kernel(
             wb_s[:].bitcast(I32).rearrange("p a (t m) -> p a m t", t=4),
             wb_s_raw[:].bitcast(I32).rearrange("p a (m t) -> p a m t", t=4),
         )
-        v_w01 = gather_words(0, 1, placed("v_w01", [P, HALF], U32, 0))
+        v_w01 = gather_words(0, 1, placed("v_w01", [P, HALF], U32, 8192))
         v_w = [[v_w00, v_w01], [gather_words(1, h, sb("v_w1%d" % h, [P, HALF], U32)) for h in range(2)]]
 
         for g in range(2):
@@ -160,7 +160,7 @@ def tile_list_ad_feature_cross_kernel(
         def v_plane(a, lo, hi):
             return v_s[a][:, lo:hi]
 
-        b_sb = [sb("b_sb%d" % h, [P, 4, HALF], F32) for h in range(2)]
+        b_sb = [sb("b_sb0", [P, 4, HALF], F32), placed("b_sb1", [P, 4, HALF], F32, 12288)]
         b_ps = [[bank(4 * h + t, "b_ps%d%d" % (h, t)) for t in range(4)] for h in range(2)]
 
         def b_pass(h, t, a, first):
@@ -204,18 +204,24 @@ def tile_list_ad_feature_cross_kernel(
         )
         for lo in (0, 2):
             round_wa(wa_bf[0][:, lo : lo + 2, 256:512], by_slice(wa_raw0[1])[:, lo : lo + 2])
-        for h in range(2):
-            for t in range(4):
-                nc.scalar.activation(b_sb[h][:, t, :], b_ps[h][t][:], IDENTITY, bias=bias_ab[:, t, 1:2])
+        for t in range(4):
+            nc.scalar.activation(b_sb[0][:, t, :], b_ps[0][t][:], IDENTITY, bias=bias_ab[:, t, 1:2])
         for lo in (0, 2):
             quantise_wa(0, lo, lo + 2)
-        round_wa(wa_bf[1][:, :, 0:256], by_slice(wa_raw1[0]))
-        round_wa(wa_bf[1][:, 0:1, 256:512], by_slice(wa_raw1[1])[:, 0:1])
         nc.vector.tensor_copy(
-            wa_bf[1][:, 1:4, 256:512].rearrange("p t (m i j) -> p m t j i", i=4, j=4),
-            wa_raw1[1][:].rearrange("p j (m t i) -> p m t j i", t=4, i=4)[:, :, 1:4],
+            wa_bf[1][:, 0:3, 0:256].rearrange("p t (m i j) -> p m t j i", i=4, j=4),
+            wa_raw1[0][:].rearrange("p j (m t i) -> p m t j i", t=4, i=4)[:, :, 0:3],
         )
-        for lo, hi in ((0, 1), (1, 2), (2, 4)):
+        nc.scalar.copy(
+            wa_bf[1][:, 3:4, 0:256].rearrange("p t (m i j) -> p t m j i", i=4, j=4), by_slice(wa_raw1[0])[:, 3:4]
+        )
+        for t in range(4):
+            nc.scalar.activation(b_sb[1][:, t, :], b_ps[1][t][:], IDENTITY, bias=bias_ab[:, t, 1:2])
+        for t in range(2):
+            round_wa(wa_bf[1][:, t : t + 1, 256:512], by_slice(wa_raw1[1])[:, t : t + 1])
+        quantise_wa(1, 0, 1)
+        round_wa(wa_bf[1][:, 2:4, 256:512], by_slice(wa_raw1[1])[:, 2:4])
+        for lo, hi in ((1, 2), (2, 4)):
             quantise_wa(1, lo, hi)
 
         def a_pass(dst, t, a, lo, hi, first):
@@ -231,7 +237,7 @@ def tile_list_ad_feature_cross_kernel(
 
         a_first = [bank(t, "a_first%d" % t) for t in range(4)]
         for t in range(4):
-            order = (0, 1) if t < 2 else (1, 0)
+            order = (0, 1) if t < 1 else (1, 0)
             for a in order:
                 a_pass(a_first[t][:], t, a, 0, HALF, a == order[0])
         a_late = [[bank(4 + 2 * e + i, "a_late%d%d" % (e, i)) for i in range(2)] for e in range(len(EVACS))]

@@ -23,7 +23,8 @@ PASSES = K // 512
 HALF = 512
 CHUNKS = [(0, 256), (256, 512), (512, 768), (768, 896), (896, 1024)]
 EVACS = [(512, 768), (768, 1024)]
-WARM_UPS = 2
+WARM_UPS = 3
+LIVE = 96
 
 
 def tile_list_ad_feature_cross_kernel(
@@ -45,36 +46,30 @@ def tile_list_ad_feature_cross_kernel(
             return psum.tile([P, HALF], F32, name=name, tag="bank%d" % index)
 
         offsets = keep.tile([P, S // 16], U16, name="offsets")
-        tab_s = sb("tab_s", [P, T], U8)
-        tab_w = [sb("tab_w%d" % a, [P, T], U32) for a in range(PASSES)]
-        wb_raw = placed("wb_raw", [P, PASSES, 2 * R], U8, 4096)
-        wb_s_raw = placed("wb_s_raw", [P, PASSES, R], U8, 1536)
-        wb_w = sb("wb_w", [P, PASSES, 2 * R], U8)
-        wb_s = sb("wb_s", [P, PASSES, R], U8)
-        wl_w = sb("wl_w", [P, PASSES, N], U32)
-        wl_s = sb("wl_s", [P, PASSES, N], U8)
-        wa_raw0 = [sb("wa_raw0%d" % g, [P, 4, R // 2], F32) for g in range(2)]
-        wa_raw1 = [placed("wa_raw10", [P, 4, R // 2], F32, 12288), sb("wa_raw11", [P, 4, R // 2], F32)]
+        tab_s = placed("tab_s", [P, T], U8, 3072)
+        tab_w = [placed("tab_w0", [P, T], U32, 16384), sb("tab_w1", [P, T], U32)]
+        wb_raw = sb("wb_raw", [P, PASSES, 2 * R], U8)
+        rows_s = sb("rows_s", [P, PASSES, R], U8)
+        wb_w = [sb("wb_w%d" % a, [P, 2 * R], U8) for a in range(PASSES)]
+        wb_s = [sb("wb_s%d" % a, [P, R], U8) for a in range(PASSES)]
         wa_bf = [sb("wa_bf%d" % a, [P, 4, 4 * P], BF16) for a in range(PASSES)]
         wa_w = [sb("wa_w%d" % a, [P, R], U32) for a in range(PASSES)]
         wa_s = [sb("wa_s%d" % a, [P, R], U8) for a in range(PASSES)]
-        wo_raw = sb("wo_raw", [P, 4, N], F32)
         wo_bf = sb("wo_bf", [P, N, 4], BF16)
         wo_w = sb("wo_w", [P, N], U32)
         wo_s = sb("wo_s", [P, N], U8)
-        v_s = [placed("v_s0", [P, S], U8, 4096), sb("v_s1", [P, S], U8)]
-        bb_row = placed("bb_row", [P, R], F32, 8192)
+        picked_s = placed("picked_s", [P, S], U8, 27648)
+        v_s = sb("v_s", [P, PASSES, S], U8)
+        bb_row = sb("bb_row", [P, R], F32)
         bb_by_t = sb("bb_by_t", [P, 4, P], F32)
         ident = sb("ident", [P, P], F32)
         bias_ab = sb("bias_ab", [P, 4, 2], F32)
-        bias_o = sb("bias_o", [P, 2], F32)
 
-        nc.vector.memset(tab_s[:].bitcast(I32), 0)
+        nc.vector.memset(tab_s[0:LIVE, :].bitcast(I32), 0)
+        nc.vector.memset(bb_by_t[:, 0, :], 0.0)
         nc.vector.memset(ident[:], 0.0)
-        nc.vector.memset(wb_s_raw[:].rearrange("p a c -> p (a c)").bitcast(I32), 0)
-        nc.vector.memset(v_s[1][:].bitcast(I32), 0)
-        nc.vector.memset(wl_s[:].rearrange("p a c -> p (a c)").bitcast(I32), 0)
-        nc.vector.memset(bb_by_t[:].rearrange("k t c -> k (t c)"), 0.0)
+        nc.vector.memset(rows_s[:].rearrange("p a c -> p (a c)").bitcast(I32), 0)
+        nc.vector.memset(v_s[:].rearrange("p a c -> p (a c)").bitcast(I32), 0)
 
         def load_scale_rows(dst, src):
             for r in range(4):
@@ -87,41 +82,19 @@ def tile_list_ad_feature_cross_kernel(
 
         wa_rows = [wa[512 * a : 512 * (a + 1), :].rearrange("(p j) c -> p j c", j=4) for a in range(PASSES)]
 
-        nc.scalar.activation(bias_ab[:, 0, 0:1], bb_by_t[:, 0, 0:1], IDENTITY)
         make_identity(nc, ident[:], nomemset=True)
+        nc.scalar.copy(bb_by_t[:, 1:4, :], bb_by_t[:, 0:1, :].to_broadcast([P, 3, P]))
 
         nc.sync.dma_start(offsets[:], offs)
-        nc.sync.dma_start(wb_raw[:].bitcast(I32), wb_words.rearrange("a p c -> p a c").bitcast(I32))
-        for r in range(4):
-            nc.sync.dma_start(
-                tab_s[r:P:16, :].bitcast(I32), tab_scales[:, r:16:4, :].rearrange("a q c -> q a c").bitcast(I32)
-            )
+        nc.scalar.dma_start(bb_row[0:1, :], ba.rearrange("(o r) -> o r", o=1))
+        nc.scalar.dma_start(bb_row[1:2, :], bb.rearrange("(o r) -> o r", o=1))
+        nc.sync.dma_start(tab_s[LIVE:P, :].bitcast(I32), tab_scales.rearrange("a q c -> q a c").bitcast(I32))
         load_table_words(0)
-        load_scale_rows(wb_s_raw, wb_scales)
-        nc.sync.dma_start(bb_row[1:2, :], bb.rearrange("(o r) -> o r", o=1))
-        nc.sync.dma_start(bb_row[0:1, :], ba.rearrange("(o r) -> o r", o=1))
+        load_scale_rows(rows_s, wb_scales)
         load_table_words(1)
-        nc.vector.tensor_copy(
-            wb_w[:].bitcast(I32).rearrange("p a (t m w) -> p a t m w", t=4, w=2),
-            wb_raw[:].bitcast(I32).rearrange("p a (m t w) -> p a t m w", t=4, w=2),
-        )
-        nc.vector.tensor_copy(v_s[0][:], tab_s[:].indirect(offsets[:]))
-        nc.sync.dma_start(wa_raw0[0][:], wa_rows[0][:, :, 0:256])
-        for r in range(4):
-            nc.sync.dma_start(v_s[1][r:P:32, :].bitcast(I32), v_s[0][16 + r : P : 32, :].bitcast(I32))
-        nc.sync.dma_start(wa_raw0[1][:], wa_rows[0][:, :, 256:512])
+        for a in range(PASSES):
+            nc.sync.dma_start(wb_raw[:, a, :].bitcast(I32), wb_words[a].bitcast(I32))
 
-        warm = bank(4, "warm")
-        for i in range(WARM_UPS):
-            nc.tensor.matmul_mx(
-                out=warm[:],
-                lhsT=tab_w[0][:, HALF : HALF + P].bitcast(FP8X4),
-                lhsT_scale=tab_s[:, HALF : HALF + P],
-                rhs=tab_w[0][:, 0:HALF].bitcast(FP8X4),
-                rhs_scale=tab_s[:, 0:HALF],
-                start=True,
-                stop=True,
-            )
         nc.scalar.copy(
             bb_by_t[0:2].rearrange("k t (m i) -> k t m i", i=4),
             bb_row[0:2, :].rearrange("k (m t i) -> k t m i", t=4, i=4),
@@ -130,44 +103,76 @@ def tile_list_ad_feature_cross_kernel(
         for t in range(4):
             nc.tensor.transpose(turned[:, P * t : P * (t + 1)], bb_by_t[:, t, :], ident[:])
         nc.scalar.activation(bias_ab[:], turned[:].rearrange("p (t k) -> p t k", t=4)[:, :, 0:2], IDENTITY)
+        for a in range(PASSES):
+            nc.scalar.copy(
+                wb_s[a][:].bitcast(U32).rearrange("p (t m) -> p t m", t=4),
+                rows_s[:, a, :].bitcast(U32).rearrange("p (m t) -> p t m", t=4),
+            )
+        for a in range(PASSES):
+            nc.scalar.copy(
+                wb_w[a][:].bitcast(U32).rearrange("p (t m w) -> p t m w", t=4, w=2),
+                wb_raw[:, a, :].bitcast(U32).rearrange("p (m t w) -> p t m w", t=4, w=2),
+            )
 
-        def gather_words(a, h, dst):
+        nc.vector.tensor_copy(picked_s[:], tab_s[:].indirect(offsets[:]))
+        for q in range(4):
+            rows = picked_s[LIVE + 8 * q : LIVE + 8 * q + 8, :]
+            nc.sync.dma_start(v_s[32 * q : 32 * q + 4].bitcast(I32), rows.bitcast(I32))
+        wa_raw0 = [placed("wa_raw0%d" % g, [P, 4, R // 2], F32, 4096 * g) for g in range(2)]
+        for g in range(2):
+            nc.sync.dma_start(wa_raw0[g][:], wa_rows[0][:, :, 256 * g : 256 * (g + 1)])
+
+        warm = bank(4, "warm")
+        for i in range(WARM_UPS):
+            nc.tensor.matmul_mx(
+                out=warm[:],
+                lhsT=tab_w[0][:, HALF : HALF + P].bitcast(FP8X4),
+                lhsT_scale=wb_s[0][:, 0:P],
+                rhs=tab_w[0][:, 0:HALF].bitcast(FP8X4),
+                rhs_scale=wb_s[1][:],
+                start=True,
+                stop=True,
+            )
+
+        def gather_words(a, h):
+            dst = sb("v_w%d%d" % (a, h), [P, HALF], U32)
             nc.vector.tensor_copy(dst[:], tab_w[a][:].indirect(offsets[:, 32 * h : 32 * (h + 1)]))
             return dst
 
-        v_w00 = gather_words(0, 0, sb("v_w00", [P, HALF], U32))
-        nc.vector.tensor_copy(
-            wb_s[:].bitcast(I32).rearrange("p a (t m) -> p a m t", t=4),
-            wb_s_raw[:].bitcast(I32).rearrange("p a (m t) -> p a m t", t=4),
-        )
-        v_w01 = gather_words(0, 1, placed("v_w01", [P, HALF], U32, 8192))
-        v_w = [[v_w00, v_w01], [gather_words(1, h, sb("v_w1%d" % h, [P, HALF], U32)) for h in range(2)]]
+        v_w = [[gather_words(a, h) for h in range(2)] for a in range(PASSES)]
 
+        wa_raw1 = [placed("wa_raw10", [P, 4, R // 2], F32, 13312), placed("wa_raw11", [P, 4, R // 2], F32, 23552)]
         for g in range(2):
             nc.sync.dma_start(wa_raw1[g][:], wa_rows[1][:, :, 256 * g : 256 * (g + 1)])
+        wo_raw = placed("wo_raw", [P, 4, N], F32, 17408)
+        wl_w = placed("wl_w", [P, PASSES, N], U32, 21504)
+        bias_o = [placed("bias_o%d" % n, [P, 1], F32, 27648 + 256 * n) for n in range(2)]
+        wl_s = rows_s[:, :, 0:N]
         wo_by_t = wo.rearrange("(m t i) n -> t m i n", t=4, i=4)
         for t in range(4):
             nc.sync.dma_start(wo_raw[:, t, :], wo_by_t[t])
-        nc.sync.dma_start(wl_w[:].bitcast(I32), wl_words.rearrange("a p c i -> p a (c i)").bitcast(I32))
+        for a in range(PASSES):
+            nc.sync.dma_start(wl_w[:, a, :].bitcast(I32), wl_words[a].rearrange("p c i -> p (c i)").bitcast(I32))
         load_scale_rows(wl_s, wl_scales)
         with nc.allow_non_contiguous_dma(reason="one value of bo a partition and half"):
-            nc.sync.dma_start(bias_o[:], bo.rearrange("(h p) -> p h", p=P))
+            for n in range(2):
+                nc.sync.dma_start(bias_o[n][:], bo[P * n : P * (n + 1)].rearrange("(p o) -> p o", o=1))
 
         def v_words(a, lo, hi):
             h = lo // HALF
             return v_w[a][h][:, lo - HALF * h : hi - HALF * h].bitcast(FP8X4)
 
         def v_plane(a, lo, hi):
-            return v_s[a][:, lo:hi]
+            return v_s[:, a, lo:hi]
 
-        b_sb = [sb("b_sb0", [P, 4, HALF], F32), placed("b_sb1", [P, 4, HALF], F32, 12288)]
+        b_sb = [sb("b_sb0", [P, 4, HALF], F32), placed("b_sb1", [P, 4, HALF], F32, 8192)]
         b_ps = [[bank(4 * h + t, "b_ps%d%d" % (h, t)) for t in range(4)] for h in range(2)]
 
         def b_pass(h, t, a, first):
             nc.tensor.matmul_mx(
                 out=b_ps[h][t][:],
-                lhsT=wb_w[:, a, 256 * t : 256 * (t + 1)].bitcast(FP4X4),
-                lhsT_scale=wb_s[:, a, P * t : P * (t + 1)],
+                lhsT=wb_w[a][:, 256 * t : 256 * (t + 1)].bitcast(FP4X4),
+                lhsT_scale=wb_s[a][:, P * t : P * (t + 1)],
                 rhs=v_words(a, HALF * h, HALF * (h + 1)),
                 rhs_scale=v_plane(a, HALF * h, HALF * (h + 1)),
                 start=first,
@@ -329,9 +334,9 @@ def tile_list_ad_feature_cross_kernel(
                     stop=True,
                 )
             y_sb = sb("y_sb%d" % c, [P, 2, hi - lo], F32)
-            nc.scalar.activation(y_sb[:, 0, :], y_ps[0][:, 0 : hi - lo], IDENTITY, bias=bias_o[:, 0:1])
+            nc.scalar.activation(y_sb[:, 0, :], y_ps[0][:, 0 : hi - lo], IDENTITY, bias=bias_o[0][:])
             if c == len(CHUNKS) - 1:
-                nc.vector.tensor_scalar(y_sb[:, 1, :], y_ps[1][:, 0 : hi - lo], bias_o[:, 1:2], None, ADD)
+                nc.vector.tensor_scalar(y_sb[:, 1, :], y_ps[1][:, 0 : hi - lo], bias_o[1][:], None, ADD)
             else:
-                nc.scalar.activation(y_sb[:, 1, :], y_ps[1][:, 0 : hi - lo], IDENTITY, bias=bias_o[:, 1:2])
+                nc.scalar.activation(y_sb[:, 1, :], y_ps[1][:, 0 : hi - lo], IDENTITY, bias=bias_o[1][:])
             nc.sync.dma_start(out_by_half[:, :, lo:hi], y_sb[:])

@@ -310,33 +310,61 @@ def tile_list_ad_feature_cross_kernel(
         quantise_h(4)
 
         out_by_half = out.rearrange("(h p) s -> p h s", p=P)
-        for c, (lo, hi) in enumerate(CHUNKS):
-            y_ps = [bank((2 * c + n) % 8, "y_ps%d%d" % (c, n)) for n in range(2)]
+        y_banks = [(0, 0), (1, 1), (2, 2), (3, 4), (5, 6)]
+        y_ps = {}
+
+        def open_y(c):
+            lo, hi = CHUNKS[c]
+            width = hi - lo
+            first, second = y_banks[c]
+            tile = bank(first, "y_ps%d0" % c)
+            if first == second:
+                y_ps[c] = [tile[:, 0:width], tile[:, width : 2 * width]]
+            else:
+                y_ps[c] = [tile[:, 0:width], bank(second, "y_ps%d1" % c)[:, 0:width]]
             for n in range(2):
                 for a in range(PASSES):
                     nc.tensor.matmul_mx(
-                        out=y_ps[n][:, 0 : hi - lo],
+                        out=y_ps[c][n],
                         lhsT=wl_w[:, a, P * n : P * (n + 1)].bitcast(FP8X4),
                         lhsT_scale=wl_s[:, a, P * n : P * (n + 1)],
                         rhs=v_words(a, lo, hi),
                         rhs_scale=v_plane(a, lo, hi),
-                        start=(a == 0),
+                        start=(a == 0 and (n == 0 or first != second)),
                         stop=False,
                     )
+
+        def close_y(c):
+            lo, hi = CHUNKS[c]
+            shared = y_banks[c][0] == y_banks[c][1]
             for n in range(2):
                 nc.tensor.matmul_mx(
-                    out=y_ps[n][:, 0 : hi - lo],
+                    out=y_ps[c][n],
                     lhsT=wo_w[:, P * n : P * (n + 1)].bitcast(FP8X4),
                     lhsT_scale=wo_s[:, P * n : P * (n + 1)],
                     rhs=h_w[c][:].bitcast(FP8X4),
                     rhs_scale=h_s[c][:],
                     start=False,
-                    stop=True,
+                    stop=(n == 1 or not shared),
                 )
             y_sb = sb("y_sb%d" % c, [P, 2, hi - lo], F32)
-            nc.scalar.activation(y_sb[:, 0, :], y_ps[0][:, 0 : hi - lo], IDENTITY, bias=bias_o[0][:])
-            if c == len(CHUNKS) - 1:
-                nc.vector.tensor_scalar(y_sb[:, 1, :], y_ps[1][:, 0 : hi - lo], bias_o[1][:], None, ADD)
+            nc.scalar.activation(y_sb[:, 0, :], y_ps[c][0], IDENTITY, bias=bias_o[0][:])
+            if shared:
+                nc.scalar.activation(y_sb[:, 1, :], y_ps[c][1], IDENTITY, bias=bias_o[1][:])
             else:
-                nc.scalar.activation(y_sb[:, 1, :], y_ps[1][:, 0 : hi - lo], IDENTITY, bias=bias_o[1][:])
-            nc.sync.dma_start(out_by_half[:, :, lo:hi], y_sb[:])
+                nc.vector.tensor_scalar(y_sb[:, 1, :], y_ps[c][1], bias_o[1][:], None, ADD)
+            if c == 2:
+                for n in range(2):
+                    nc.sync.dma_start(out_by_half[:, n, lo:hi], y_sb[:, n, :])
+            else:
+                nc.sync.dma_start(out_by_half[:, :, lo:hi], y_sb[:])
+
+        open_y(0)
+        close_y(0)
+        open_y(1)
+        open_y(2)
+        close_y(1)
+        open_y(3)
+        open_y(4)
+        for c in (2, 3, 4):
+            close_y(c)

@@ -165,7 +165,7 @@ def tile_list_ad_feature_cross_kernel(
         def v_plane(a, lo, hi):
             return v_s[:, a, lo:hi]
 
-        b_sb = [sb("b_sb0", [P, 4, HALF], F32), placed("b_sb1", [P, 4, HALF], F32, 8192)]
+        b_sb = [sb("b_sb0", [P, 4, HALF], F32), sb("b_sb1", [P, 4, HALF], F32)]
         b_ps = [[bank(4 * h + t, "b_ps%d%d" % (h, t)) for t in range(4)] for h in range(2)]
 
         def b_pass(h, t, a, first):
@@ -213,13 +213,7 @@ def tile_list_ad_feature_cross_kernel(
             nc.scalar.activation(b_sb[0][:, t, :], b_ps[0][t][:], IDENTITY, bias=bias_ab[:, t, 1:2])
         for lo in (0, 2):
             quantise_wa(0, lo, lo + 2)
-        nc.vector.tensor_copy(
-            wa_bf[1][:, 0:3, 0:256].rearrange("p t (m i j) -> p m t j i", i=4, j=4),
-            wa_raw1[0][:].rearrange("p j (m t i) -> p m t j i", t=4, i=4)[:, :, 0:3],
-        )
-        nc.scalar.copy(
-            wa_bf[1][:, 3:4, 0:256].rearrange("p t (m i j) -> p t m j i", i=4, j=4), by_slice(wa_raw1[0])[:, 3:4]
-        )
+        round_wa(wa_bf[1][:, :, 0:256], by_slice(wa_raw1[0]))
         for t in range(4):
             nc.scalar.activation(b_sb[1][:, t, :], b_ps[1][t][:], IDENTITY, bias=bias_ab[:, t, 1:2])
         for t in range(2):

@@ -25,6 +25,7 @@ CHUNKS = [(0, 256), (256, 512), (512, 768), (768, 896), (896, 1024)]
 EVACS = [(512, 768), (768, 1024)]
 WARM_UPS = 3
 LIVE = 96
+WO_SPLIT = 192
 
 
 def tile_list_ad_feature_cross_kernel(
@@ -52,10 +53,9 @@ def tile_list_ad_feature_cross_kernel(
         rows_s = sb("rows_s", [P, PASSES, R], U8)
         wb_w = [sb("wb_w%d" % a, [P, 2 * R], U8) for a in range(PASSES)]
         wb_s = [sb("wb_s%d" % a, [P, R], U8) for a in range(PASSES)]
-        wa_bf = [sb("wa_bf%d" % a, [P, 4, 4 * P], BF16) for a in range(PASSES)]
+        wa_bf = [sb("wa_bf0", [P, 4, 4 * P], BF16), placed("wa_bf1", [P, 4, 4 * P], BF16, 28672)]
         wa_w = [sb("wa_w%d" % a, [P, R], U32) for a in range(PASSES)]
         wa_s = [sb("wa_s%d" % a, [P, R], U8) for a in range(PASSES)]
-        wo_bf = sb("wo_bf", [P, N, 4], BF16)
         wo_w = sb("wo_w", [P, N], U32)
         wo_s = sb("wo_s", [P, N], U8)
         picked_s = placed("picked_s", [P, S], U8, 27648)
@@ -139,7 +139,9 @@ def tile_list_ad_feature_cross_kernel(
             nc.vector.tensor_copy(dst[:], tab_w[a][:].indirect(offsets[:, 32 * h : 32 * (h + 1)]))
             return dst
 
-        v_w = [[gather_words(a, h) for h in range(2)] for a in range(PASSES)]
+        first_pass = sb("v_w0", [P, S], U32)
+        nc.vector.tensor_copy(first_pass[:], tab_w[0][:].indirect(offsets[:]))
+        v_w = [[first_pass[:, 0:HALF], first_pass[:, HALF:S]], [gather_words(1, h) for h in range(2)]]
 
         wa_raw1 = [placed("wa_raw10", [P, 4, R // 2], F32, 13312), placed("wa_raw11", [P, 4, R // 2], F32, 23552)]
         for g in range(2):
@@ -216,11 +218,9 @@ def tile_list_ad_feature_cross_kernel(
         round_wa(wa_bf[1][:, :, 0:256], by_slice(wa_raw1[0]))
         for t in range(4):
             nc.scalar.activation(b_sb[1][:, t, :], b_ps[1][t][:], IDENTITY, bias=bias_ab[:, t, 1:2])
-        for t in range(2):
-            round_wa(wa_bf[1][:, t : t + 1, 256:512], by_slice(wa_raw1[1])[:, t : t + 1])
-        quantise_wa(1, 0, 1)
-        round_wa(wa_bf[1][:, 2:4, 256:512], by_slice(wa_raw1[1])[:, 2:4])
-        for lo, hi in ((1, 2), (2, 4)):
+        for lo in (0, 2):
+            round_wa(wa_bf[1][:, lo : lo + 2, 256:512], by_slice(wa_raw1[1])[:, lo : lo + 2])
+        for lo, hi in ((0, 1), (1, 2), (2, 4)):
             quantise_wa(1, lo, hi)
 
         def a_pass(dst, t, a, lo, hi, first):
@@ -261,12 +261,22 @@ def tile_list_ad_feature_cross_kernel(
                     h_planes[:, t, lo:hi], a_first[t][:, lo:hi], bias_ab[:, t, 0:1], b_sb[0][:, t, lo:hi], ADD, MULT
                 )
         a_sb = [sb("a_sb%d" % e, [P, 4, hi - lo], F32) for e, (lo, hi) in enumerate(EVACS)]
+        wo_bf = placed("wo_bf", [P, N, 4], BF16, 28672)
+        nc.gpsimd.tensor_scalar(
+            wo_bf[:, 0:WO_SPLIT, :], wo_raw[:, :, 0:WO_SPLIT].rearrange("p t n -> p n t"), 1.0, 0.0, MULT, ADD
+        )
         nc.scalar.copy(
-            wo_bf[:].rearrange("p (c i) t -> p c t i", i=4), wo_raw[:].rearrange("p t (c i) -> p c t i", i=4)
+            wo_bf[:, WO_SPLIT:N, :].rearrange("p (c i) t -> p c t i", i=4),
+            wo_raw[:, :, WO_SPLIT:N].rearrange("p t (c i) -> p c t i", i=4),
         )
         for e in range(len(EVACS)):
             for t in late_order:
                 nc.scalar.activation(a_sb[e][:, t, :], a_late_slice(e, t), IDENTITY, bias=bias_ab[:, t, 0:1])
+            if e == 0:
+                nc.scalar.copy(
+                    h_bf[1][:, P : 2 * P, :].rearrange("p (c i) t -> p c t i", i=4),
+                    h_planes[:, :, HALF - P : HALF].rearrange("p t (c i) -> p c t i", i=4),
+                )
 
         def by_four(ap):
             return ap.rearrange("p t (c i) -> p c t i", i=4)
@@ -274,8 +284,10 @@ def tile_list_ad_feature_cross_kernel(
         def cross(c):
             lo, hi = CHUNKS[c]
             woven = h_bf[c][:].rearrange("p (c i) t -> p c t i", i=4)
-            if hi <= HALF:
+            if hi < HALF:
                 nc.vector.tensor_copy(woven, by_four(h_planes[:, :, lo:hi]))
+            elif hi == HALF:
+                nc.vector.tensor_copy(woven[:, 0 : P // 4], by_four(h_planes[:, :, lo : hi - P]))
             else:
                 e = (lo - HALF) // 256
                 elo = EVACS[e][0]
@@ -295,10 +307,10 @@ def tile_list_ad_feature_cross_kernel(
         cross(1)
         quantise_h(0)
         nc.vector.quantize_mx(out=wo_w[:].bitcast(FP8X4), scales=wo_s[:], in_=wo_bf[:].rearrange("p n t -> p (n t)"))
-        quantise_h(1)
         cross(2)
-        cross(3)
+        quantise_h(1)
         quantise_h(2)
+        cross(3)
         cross(4)
         quantise_h(3)
         quantise_h(4)
@@ -353,12 +365,10 @@ def tile_list_ad_feature_cross_kernel(
             else:
                 nc.sync.dma_start(out_by_half[:, :, lo:hi], y_sb[:])
 
-        open_y(0)
-        close_y(0)
-        open_y(1)
-        open_y(2)
-        close_y(1)
+        for c in range(3):
+            open_y(c)
+            close_y(c)
         open_y(3)
         open_y(4)
-        for c in (2, 3, 4):
-            close_y(c)
+        close_y(3)
+        close_y(4)

from contextlib import ExitStack

import concourse.mybir as mybir
from concourse.masks import make_identity

K, T, S, R, N = 1024, 2048, 1024, 512, 256
FLOPS = 2 * S * (2 * K * R + R * N + K * N)

F32 = mybir.dt.float32
BF16 = mybir.dt.bfloat16
I32 = mybir.dt.int32
U32 = mybir.dt.uint32
U16 = mybir.dt.uint16
U8 = mybir.dt.uint8
FP8X4 = mybir.dt.float8_e4m3fn_x4
FP4X4 = mybir.dt.float4_e2m1fn_x4
IDENTITY = mybir.ActivationFunctionType.Identity
MULT = mybir.AluOpType.mult
ADD = mybir.AluOpType.add

P = 128
PASSES = K // 512
HALF = 512
CHUNKS = [(0, 256), (256, 512), (512, 768), (768, 896), (896, 1024)]
EVACS = [(512, 768), (768, 1024)]
WARM_UPS = 3
LIVE = 96
WO_SPLIT = 192


def tile_list_ad_feature_cross_kernel(
    tc, tab_words, tab_scales, offs, wa, ba, wb_words, wb_scales, bb, wl_words, wl_scales, wo, bo, out
):
    nc = tc.nc
    with ExitStack() as ctx:
        keep = ctx.enter_context(tc.tile_pool(name="keep", bufs=1))
        reuse = ctx.enter_context(tc.tile_pool(name="reuse", bufs=1))
        psum = ctx.enter_context(tc.psum_pool(name="psum", bufs=1))

        def sb(name, shape, dtype):
            return keep.tile(shape, dtype, name=name, align_bytes=256)

        def placed(name, shape, dtype, offset):
            return reuse.tile(shape, dtype, name=name, align_bytes=256, offset=offset)

        def bank(index, name):
            return psum.tile([P, HALF], F32, name=name, tag="bank%d" % index)

        offsets = keep.tile([P, S // 16], U16, name="offsets")
        tab_s = placed("tab_s", [P, T], U8, 3072)
        tab_w = [placed("tab_w0", [P, T], U32, 16384), sb("tab_w1", [P, T], U32)]
        wb_raw = sb("wb_raw", [P, PASSES, 2 * R], U8)
        rows_s = sb("rows_s", [P, PASSES, R], U8)
        wb_w = [sb("wb_w%d" % a, [P, 2 * R], U8) for a in range(PASSES)]
        wb_s = [sb("wb_s%d" % a, [P, R], U8) for a in range(PASSES)]
        wa_bf = [sb("wa_bf0", [P, 4, 4 * P], BF16), placed("wa_bf1", [P, 4, 4 * P], BF16, 28672)]
        wa_w = [sb("wa_w%d" % a, [P, R], U32) for a in range(PASSES)]
        wa_s = [sb("wa_s%d" % a, [P, R], U8) for a in range(PASSES)]
        wo_w = sb("wo_w", [P, N], U32)
        wo_s = sb("wo_s", [P, N], U8)
        picked_s = placed("picked_s", [P, S], U8, 27648)
        v_s = sb("v_s", [P, PASSES, S], U8)
        bb_row = sb("bb_row", [P, R], F32)
        bb_by_t = sb("bb_by_t", [P, 4, P], F32)
        ident = sb("ident", [P, P], F32)
        bias_ab = sb("bias_ab", [P, 4, 2], F32)

        nc.vector.memset(tab_s[0:LIVE, :].bitcast(I32), 0)
        nc.vector.memset(bb_by_t[:, 0, :], 0.0)
        nc.vector.memset(ident[:], 0.0)
        nc.vector.memset(rows_s[:].rearrange("p a c -> p (a c)").bitcast(I32), 0)
        nc.vector.memset(v_s[:].rearrange("p a c -> p (a c)").bitcast(I32), 0)

        def load_scale_rows(dst, src):
            for r in range(4):
                nc.sync.dma_start(
                    dst[r:P:32].bitcast(I32), src[:, r:16:4, :].rearrange("a q c -> q a c").bitcast(I32)
                )

        def load_table_words(a):
            nc.sync.dma_start(tab_w[a][:].bitcast(I32), tab_words[a].rearrange("p t i -> p (t i)").bitcast(I32))

        wa_rows = [wa[512 * a : 512 * (a + 1), :].rearrange("(p j) c -> p j c", j=4) for a in range(PASSES)]

        make_identity(nc, ident[:], nomemset=True)
        nc.scalar.copy(bb_by_t[:, 1:4, :], bb_by_t[:, 0:1, :].to_broadcast([P, 3, P]))

        nc.sync.dma_start(offsets[:], offs)
        nc.scalar.dma_start(bb_row[0:1, :], ba.rearrange("(o r) -> o r", o=1))
        nc.scalar.dma_start(bb_row[1:2, :], bb.rearrange("(o r) -> o r", o=1))
        nc.sync.dma_start(tab_s[LIVE:P, :].bitcast(I32), tab_scales.rearrange("a q c -> q a c").bitcast(I32))
        load_table_words(0)
        load_scale_rows(rows_s, wb_scales)
        load_table_words(1)
        for a in range(PASSES):
            nc.sync.dma_start(wb_raw[:, a, :].bitcast(I32), wb_words[a].bitcast(I32))

        nc.scalar.copy(
            bb_by_t[0:2].rearrange("k t (m i) -> k t m i", i=4),
            bb_row[0:2, :].rearrange("k (m t i) -> k t m i", t=4, i=4),
        )
        turned = bank(7, "bias_ps")
        for t in range(4):
            nc.tensor.transpose(turned[:, P * t : P * (t + 1)], bb_by_t[:, t, :], ident[:])
        nc.scalar.activation(bias_ab[:], turned[:].rearrange("p (t k) -> p t k", t=4)[:, :, 0:2], IDENTITY)
        for a in range(PASSES):
            nc.scalar.copy(
                wb_s[a][:].bitcast(U32).rearrange("p (t m) -> p t m", t=4),
                rows_s[:, a, :].bitcast(U32).rearrange("p (m t) -> p t m", t=4),
            )
        for a in range(PASSES):
            nc.scalar.copy(
                wb_w[a][:].bitcast(U32).rearrange("p (t m w) -> p t m w", t=4, w=2),
                wb_raw[:, a, :].bitcast(U32).rearrange("p (m t w) -> p t m w", t=4, w=2),
            )

        nc.vector.tensor_copy(picked_s[:], tab_s[:].indirect(offsets[:]))
        for q in range(4):
            rows = picked_s[LIVE + 8 * q : LIVE + 8 * q + 8, :]
            nc.sync.dma_start(v_s[32 * q : 32 * q + 4].bitcast(I32), rows.bitcast(I32))
        wa_raw0 = [placed("wa_raw0%d" % g, [P, 4, R // 2], F32, 4096 * g) for g in range(2)]
        for g in range(2):
            nc.sync.dma_start(wa_raw0[g][:], wa_rows[0][:, :, 256 * g : 256 * (g + 1)])

        warm = bank(4, "warm")
        for i in range(WARM_UPS):
            nc.tensor.matmul_mx(
                out=warm[:],
                lhsT=tab_w[0][:, HALF : HALF + P].bitcast(FP8X4),
                lhsT_scale=wb_s[0][:, 0:P],
                rhs=tab_w[0][:, 0:HALF].bitcast(FP8X4),
                rhs_scale=wb_s[1][:],
                start=True,
                stop=True,
            )

        def gather_words(a, h):
            dst = sb("v_w%d%d" % (a, h), [P, HALF], U32)
            nc.vector.tensor_copy(dst[:], tab_w[a][:].indirect(offsets[:, 32 * h : 32 * (h + 1)]))
            return dst

        first_pass = sb("v_w0", [P, S], U32)
        nc.vector.tensor_copy(first_pass[:], tab_w[0][:].indirect(offsets[:]))
        v_w = [[first_pass[:, 0:HALF], first_pass[:, HALF:S]], [gather_words(1, h) for h in range(2)]]

        wa_raw1 = [placed("wa_raw10", [P, 4, R // 2], F32, 13312), placed("wa_raw11", [P, 4, R // 2], F32, 23552)]
        for g in range(2):
            nc.sync.dma_start(wa_raw1[g][:], wa_rows[1][:, :, 256 * g : 256 * (g + 1)])
        wo_raw = placed("wo_raw", [P, 4, N], F32, 17408)
        wl_w = placed("wl_w", [P, PASSES, N], U32, 21504)
        bias_o = [placed("bias_o%d" % n, [P, 1], F32, 27648 + 256 * n) for n in range(2)]
        wl_s = rows_s[:, :, 0:N]
        wo_by_t = wo.rearrange("(m t i) n -> t m i n", t=4, i=4)
        for t in range(4):
            nc.sync.dma_start(wo_raw[:, t, :], wo_by_t[t])
        for a in range(PASSES):
            nc.sync.dma_start(wl_w[:, a, :].bitcast(I32), wl_words[a].rearrange("p c i -> p (c i)").bitcast(I32))
        load_scale_rows(wl_s, wl_scales)
        with nc.allow_non_contiguous_dma(reason="one value of bo a partition and half"):
            for n in range(2):
                nc.sync.dma_start(bias_o[n][:], bo[P * n : P * (n + 1)].rearrange("(p o) -> p o", o=1))

        def v_words(a, lo, hi):
            h = lo // HALF
            return v_w[a][h][:, lo - HALF * h : hi - HALF * h].bitcast(FP8X4)

        def v_plane(a, lo, hi):
            return v_s[:, a, lo:hi]

        b_sb = [sb("b_sb0", [P, 4, HALF], F32), sb("b_sb1", [P, 4, HALF], F32)]
        b_ps = [[bank(4 * h + t, "b_ps%d%d" % (h, t)) for t in range(4)] for h in range(2)]

        def b_pass(h, t, a, first):
            nc.tensor.matmul_mx(
                out=b_ps[h][t][:],
                lhsT=wb_w[a][:, 256 * t : 256 * (t + 1)].bitcast(FP4X4),
                lhsT_scale=wb_s[a][:, P * t : P * (t + 1)],
                rhs=v_words(a, HALF * h, HALF * (h + 1)),
                rhs_scale=v_plane(a, HALF * h, HALF * (h + 1)),
                start=first,
                stop=not first,
            )

        for a in range(PASSES):
            for t in range(4):
                b_pass(0, t, a, a == 0)
        for t in range(4):
            order = (0, 1) if t < 2 else (1, 0)
            for a in order:
                b_pass(1, t, a, a == order[0])

        def round_wa(dst, src):
            nc.vector.tensor_copy(
                dst.rearrange("p t (m i j) -> p t m j i", i=4, j=4),
                src,
            )

        def by_slice(raw):
            return raw[:].rearrange("p j (m t i) -> p t m j i", t=4, i=4)

        def quantise_wa(a, lo, hi):
            cols = slice(P * lo, P * hi)
            nc.vector.quantize_mx(
                out=wa_w[a][:, cols].bitcast(FP8X4),
                scales=wa_s[a][:, cols],
                in_=wa_bf[a][:, lo:hi, :].rearrange("p t c -> p (t c)"),
            )

        nc.scalar.copy(
            wa_bf[0][:, :, 0:256].rearrange("p t (m i j) -> p t m j i", i=4, j=4), by_slice(wa_raw0[0])
        )
        for lo in (0, 2):
            round_wa(wa_bf[0][:, lo : lo + 2, 256:512], by_slice(wa_raw0[1])[:, lo : lo + 2])
        for t in range(4):
            nc.scalar.activation(b_sb[0][:, t, :], b_ps[0][t][:], IDENTITY, bias=bias_ab[:, t, 1:2])
        for lo in (0, 2):
            quantise_wa(0, lo, lo + 2)
        round_wa(wa_bf[1][:, :, 0:256], by_slice(wa_raw1[0]))
        for t in range(4):
            nc.scalar.activation(b_sb[1][:, t, :], b_ps[1][t][:], IDENTITY, bias=bias_ab[:, t, 1:2])
        for lo in (0, 2):
            round_wa(wa_bf[1][:, lo : lo + 2, 256:512], by_slice(wa_raw1[1])[:, lo : lo + 2])
        for lo, hi in ((0, 1), (1, 2), (2, 4)):
            quantise_wa(1, lo, hi)

        def a_pass(dst, t, a, lo, hi, first):
            nc.tensor.matmul_mx(
                out=dst,
                lhsT=wa_w[a][:, P * t : P * (t + 1)].bitcast(FP8X4),
                lhsT_scale=wa_s[a][:, P * t : P * (t + 1)],
                rhs=v_words(a, lo, hi),
                rhs_scale=v_plane(a, lo, hi),
                start=first,
                stop=not first,
            )

        a_first = [bank(t, "a_first%d" % t) for t in range(4)]
        for t in range(4):
            order = (0, 1) if t < 1 else (1, 0)
            for a in order:
                a_pass(a_first[t][:], t, a, 0, HALF, a == order[0])
        a_late = [[bank(4 + 2 * e + i, "a_late%d%d" % (e, i)) for i in range(2)] for e in range(len(EVACS))]

        def a_late_slice(e, t):
            return a_late[e][t % 2][:, 256 * (t // 2) : 256 * (t // 2 + 1)]

        late_order = (2, 0, 3, 1)
        for e, (lo, hi) in enumerate(EVACS):
            for t in late_order:
                for a in (1, 0):
                    a_pass(a_late_slice(e, t), t, a, lo, hi, a == 1)

        h_bf = [sb("h_bf%d" % c, [P, hi - lo, 4], BF16) for c, (lo, hi) in enumerate(CHUNKS)]
        h_w = [sb("h_w%d" % c, [P, hi - lo], U32) for c, (lo, hi) in enumerate(CHUNKS)]
        h_s = [sb("h_s%d" % c, [P, hi - lo], U8) for c, (lo, hi) in enumerate(CHUNKS)]

        h_planes = sb("h_planes", [P, 4, HALF], BF16)
        for t in range(4):
            for lo, hi in CHUNKS[0:2] if t == 3 else [(0, HALF)]:
                nc.vector.scalar_tensor_tensor(
                    h_planes[:, t, lo:hi], a_first[t][:, lo:hi], bias_ab[:, t, 0:1], b_sb[0][:, t, lo:hi], ADD, MULT
                )
        a_sb = [sb("a_sb%d" % e, [P, 4, hi - lo], F32) for e, (lo, hi) in enumerate(EVACS)]
        wo_bf = placed("wo_bf", [P, N, 4], BF16, 28672)
        nc.gpsimd.tensor_scalar(
            wo_bf[:, 0:WO_SPLIT, :], wo_raw[:, :, 0:WO_SPLIT].rearrange("p t n -> p n t"), 1.0, 0.0, MULT, ADD
        )
        nc.scalar.copy(
            wo_bf[:, WO_SPLIT:N, :].rearrange("p (c i) t -> p c t i", i=4),
            wo_raw[:, :, WO_SPLIT:N].rearrange("p t (c i) -> p c t i", i=4),
        )
        for e in range(len(EVACS)):
            for t in late_order:
                nc.scalar.activation(a_sb[e][:, t, :], a_late_slice(e, t), IDENTITY, bias=bias_ab[:, t, 0:1])
            if e == 0:
                nc.scalar.copy(
                    h_bf[1][:, P : 2 * P, :].rearrange("p (c i) t -> p c t i", i=4),
                    h_planes[:, :, HALF - P : HALF].rearrange("p t (c i) -> p c t i", i=4),
                )

        def by_four(ap):
            return ap.rearrange("p t (c i) -> p c t i", i=4)

        def cross(c):
            lo, hi = CHUNKS[c]
            woven = h_bf[c][:].rearrange("p (c i) t -> p c t i", i=4)
            if hi < HALF:
                nc.vector.tensor_copy(woven, by_four(h_planes[:, :, lo:hi]))
            elif hi == HALF:
                nc.vector.tensor_copy(woven[:, 0 : P // 4], by_four(h_planes[:, :, lo : hi - P]))
            else:
                e = (lo - HALF) // 256
                elo = EVACS[e][0]
                nc.vector.tensor_tensor(
                    woven,
                    by_four(a_sb[e][:, :, lo - elo : hi - elo]),
                    by_four(b_sb[1][:, :, lo - HALF : hi - HALF]),
                    MULT,
                )

        def quantise_h(c):
            nc.vector.quantize_mx(
                out=h_w[c][:].bitcast(FP8X4), scales=h_s[c][:], in_=h_bf[c][:].rearrange("p s t -> p (s t)")
            )

        cross(0)
        cross(1)
        quantise_h(0)
        nc.vector.quantize_mx(out=wo_w[:].bitcast(FP8X4), scales=wo_s[:], in_=wo_bf[:].rearrange("p n t -> p (n t)"))
        cross(2)
        quantise_h(1)
        quantise_h(2)
        cross(3)
        cross(4)
        quantise_h(3)
        quantise_h(4)

        out_by_half = out.rearrange("(h p) s -> p h s", p=P)
        y_banks = [(0, 0), (1, 1), (2, 2), (3, 4), (5, 6)]
        y_ps = {}

        def open_y(c):
            lo, hi = CHUNKS[c]
            width = hi - lo
            first, second = y_banks[c]
            tile = bank(first, "y_ps%d0" % c)
            if first == second:
                y_ps[c] = [tile[:, 0:width], tile[:, width : 2 * width]]
            else:
                y_ps[c] = [tile[:, 0:width], bank(second, "y_ps%d1" % c)[:, 0:width]]
            for n in range(2):
                for a in range(PASSES):
                    nc.tensor.matmul_mx(
                        out=y_ps[c][n],
                        lhsT=wl_w[:, a, P * n : P * (n + 1)].bitcast(FP8X4),
                        lhsT_scale=wl_s[:, a, P * n : P * (n + 1)],
                        rhs=v_words(a, lo, hi),
                        rhs_scale=v_plane(a, lo, hi),
                        start=(a == 0 and (n == 0 or first != second)),
                        stop=False,
                    )

        def close_y(c):
            lo, hi = CHUNKS[c]
            shared = y_banks[c][0] == y_banks[c][1]
            for n in range(2):
                nc.tensor.matmul_mx(
                    out=y_ps[c][n],
                    lhsT=wo_w[:, P * n : P * (n + 1)].bitcast(FP8X4),
                    lhsT_scale=wo_s[:, P * n : P * (n + 1)],
                    rhs=h_w[c][:].bitcast(FP8X4),
                    rhs_scale=h_s[c][:],
                    start=False,
                    stop=(n == 1 or not shared),
                )
            y_sb = sb("y_sb%d" % c, [P, 2, hi - lo], F32)
            nc.scalar.activation(y_sb[:, 0, :], y_ps[c][0], IDENTITY, bias=bias_o[0][:])
            if shared:
                nc.scalar.activation(y_sb[:, 1, :], y_ps[c][1], IDENTITY, bias=bias_o[1][:])
            else:
                nc.vector.tensor_scalar(y_sb[:, 1, :], y_ps[c][1], bias_o[1][:], None, ADD)
            if c == 2:
                for n in range(2):
                    nc.sync.dma_start(out_by_half[:, n, lo:hi], y_sb[:, n, :])
            else:
                nc.sync.dma_start(out_by_half[:, :, lo:hi], y_sb[:])

        for c in range(3):
            open_y(c)
            close_y(c)
        open_y(3)
        open_y(4)
        close_y(3)
        close_y(4)
